import numpy as np, ml_dtypes
CORES = [1,5,17,21,33,37,49,53]
N = 8
BF = ml_dtypes.bfloat16
P, M, C, I, D, S, SH = 384, 320, 128, 32, 2, 3, 6
J = I // D; U = 1 << SH; FILL = (P - M) // S + 2
def at(rng, t, e):
    b = e >> 4
    a = b + (((np.arange(16)[:, None] + rng.integers(0, 16, e.shape)) & 15) < (e & 15))
    sh = e.shape[:-2] + (8, e.shape[-1])
    z = np.floor((np.minimum(b, 127 - b) + 1) * rng.random(sh)).astype(np.int64) * (2 * rng.integers(0, 2, sh) - 1)
    a[..., 0::2, :] += z; a[..., 1::2, :] -= z
    return t + np.where(t < 128, 1, -1) * a
def lean(rng, t, e, m):
    a = (e >> 4) + (((np.arange(16)[:, None] + rng.integers(0, 16, e.shape)) & 15) < (e & 15))
    z = rng.integers(0, m + 1, e.shape[:-2] + (8, e.shape[-1]))
    a[..., 0::2, :] -= z; a[..., 1::2, :] += z
    return t + a
def far(rng, t, k):
    u = rng.integers(0, 16, t.shape[:-1] + (k,))
    return np.where(t < 128, 255 - u, u)
def parts(rng, dev):
    t = np.clip(rng.integers(0, 256, (1, 8, 16, 1)) + rng.integers(-dev, dev + 1, (N, 8, 16, 1)), 0, 255)
    e = U * np.repeat(np.arange(16), M) + rng.integers(0, U, (N, 8, 1, 16 * M))
    return {"t": t, "n": rng.integers(M >> 1, M + 1, (N, 8, 16)), "hs": at(rng, t, e), "x": at(rng, t, rng.integers(0, 16 * U, (N, 8, 1, C))),
            "dv": rng.integers(0, 256, (N, 8, 16, S * C)) >> rng.integers(0, 8, (N, 8, 1, S * C)), "te": rng.integers(0, 5, (N, 8))}
def pack(p):
    def b(v):
        return np.ascontiguousarray(v.reshape(N, 128, -1)).astype(np.float32).astype(BF)
    return {"hs": b(p["hs"]), "cn": p["n"].reshape(N, 128, 1).astype(np.int32), "x0": b(p["x"]), "tg": b(p["t"]), "dv": b(p["dv"]),
            "te": np.repeat(p["te"], 16, axis=1).reshape(N, 128, 1).astype(np.int32)}
def setup_inputs(rng):
    p = parts(rng, 4); t = p["t"]
    lo = rng.integers(0, 12, (N, 8, 1, 1)); wd = rng.choice(np.array([1, 4, 16]), (N, 8, 1, 1))
    e = np.minimum((lo * U + wd * U * rng.random((N, 8, 1, C))).astype(np.int64), 16 * U - 1)
    low = np.zeros((N, 8, 1, 1), bool); low[np.arange(N), rng.integers(0, 8, N)] = True
    e = np.where(low, rng.integers(0, U, e.shape), e); p["te"] = np.where(low[..., 0, 0], 0, p["te"])
    away = (rng.random(e.shape) < 0.125) & ~low
    p["x"] = np.where(away, far(rng, t, C), at(rng, t, e))
    p["hs"][..., 15 * M:] = np.where(rng.random((N, 8, 1, M)) < 0.25, far(rng, t, M), p["hs"][..., 15 * M:])
    return pack(p)
def setup_inputs_caps(rng):
    p = parts(rng, 0); p["te"] = 0 * p["te"]; p["dv"] = 0 * p["dv"]; kr = np.zeros((N, 8, 1, C), np.int64); ov = rng.integers(0, 15, 8)
    F = min(C, P >> 1); fk = rng.integers(3, 8, 8)
    for g in (2, 3):
        k = int(fk[g])
        goal = 2655 - ((97 * (I - 1) + 5 * (C - 1) + U) >> 1) - U * k
        p["t"][:, g] = at(rng, np.zeros((16, 1), np.int64), np.array([[goal]]))
        p["hs"][:, g] = at(rng, p["t"][:, g], U * np.repeat(np.arange(16), M) + rng.integers(0, U, (N, 1, 16 * M)))
        p["hs"][:, g, :, k * M:(k + 1) * M] = lean(rng, p["t"][:, g], U * k + rng.integers(1, U, (N, 1, M)), U * k >> 5)
    for r in range(N):
        for g in range(8):
            if g < 2:
                o = rng.permutation(16)
                kr[r, g, 0] = rng.permutation(np.concatenate([np.repeat(o[:3], FILL), rng.choice(o[3:9], C - 3 * FILL)]))
                p["n"][r, g, o[:3]] = P + np.array([0, -1, 1]) - S * FILL
            elif g < 4:
                k = int(fk[g])
                kr[r, g, 0] = rng.choice(np.delete(np.arange(16), k), C)
                kr[r, g, 0, rng.permutation(C)[:F]] = k
                p["n"][r, g, k] = P - F
            else:
                k = int(ov[g])
                kr[r, g, 0] = rng.permutation(np.concatenate([np.repeat(k, C - 4), np.repeat(k + 1, 4)]))
                p["n"][r, g, k] = M; p["n"][r, g, k + 1] = 1
    p["x"] = at(rng, p["t"], U * kr + rng.integers(0, U, kr.shape))
    for r in range(N):
        for g in (2, 3):
            k = int(fk[g]); c = np.flatnonzero(kr[r, g, 0] == k)
            p["x"][r, g][:, c] = lean(rng, p["t"][r, g], U * k + rng.integers(1, U, (1, len(c))), U * k >> 5)
            p["x"][r, g, :, int(c[-1])] = p["t"][r, g, :, 0] + (U * k >> 3) * (1 - (np.arange(16) & 1))
    return pack(p)
def setup_inputs_crowd(rng):
    p = parts(rng, 4); kr = rng.integers(0, 16, (N, 8, 1, 1)); kr[:, 0] = 0; kr[:, 1] = 15; kr[:, 2] = 15
    p["x"] = at(rng, p["t"], U * kr + rng.integers(0, U, (N, 8, 1, C)))
    p["n"] = np.where(np.arange(16) == kr[..., 0], M, p["n"])
    p["te"] = rng.choice(np.array([0, 0, 3, 1024]), (N, 8))
    t = 255 * rng.integers(0, 2, (N, 16, 1)); p["t"][:, 2] = t
    p["hs"][:, 2] = at(rng, t, U * np.repeat(np.arange(16), M) + rng.integers(0, U, (N, 1, 16 * M)))
    p["hs"][:, 2, :, 15 * M:] = far(rng, t, M)
    p["x"][:, 2] = np.where(np.arange(C) & 1, far(rng, t, C), 255 - t)
    return pack(p)
def setup_inputs_ties(rng):
    p = parts(rng, 0); t = p["t"]; lv = np.array([0, U >> 2, U >> 1, U - 1])
    p["hs"] = at(rng, t, U * np.repeat(np.arange(16), M) + rng.choice(lv, (N, 8, 1, 16 * M)))
    x = at(rng, t, U * rng.integers(0, 16, (N, 8, 1, C)) + rng.choice(lv, (N, 8, 1, C)))
    on = (rng.random((N, 8, 1, C)) < 0.5) & (np.arange(8)[:, None, None] >= 4)
    p["x"] = np.where(on, t, x); p["te"] = rng.integers(0, 9, (N, 8)); p["te"][:, :2] = 0
    p["dv"] = p["dv"] * rng.integers(0, 2, (N, 8, 1, S * C))
    back = np.where(t < 128, np.clip(2 * (p["x"] - t), 0, 255), 0)
    p["dv"][..., :C] = np.where(rng.random((N, 8, 1, C)) < 0.7, back, p["dv"][..., :C])
    y = rng.integers(240, 256, (16, 1)); y[0, 0] ^= int(np.add.reduce(y[:, 0])) & 1
    u = rng.integers(32, 41, (16, 1)); ty = int(np.add.reduce(y[:, 0])); tu = int(np.add.reduce(u[:, 0]))
    p["t"][:, 3] = u; p["hs"][:, 3] = y; p["dv"][:, 3] = 0
    for r in range(N):
        T, m = ((257, 8), (513, 4), (1021, 3), (1024, 2))[r & 3]
        e = ty - tu - T * m; v = ((tu + e - m) & 63) >> 1
        b = (e - v) // 15
        a = b + (((np.arange(15)[:, None] + rng.integers(0, 15, (1, C))) % 15) < e - v - 15 * b)
        z = rng.integers(0, b + 1, (7, C)) * (2 * rng.integers(0, 2, (7, C)) - 1)
        a[0:14:2] += z; a[1:14:2] -= z
        p["x"][r, 3] = np.concatenate([u[:15] + a, np.full((1, C), int(u[15, 0]) - v)], axis=0); p["te"][r, 3] = T
    return pack(p)
def setup_inputs_alike(rng):
    p = parts(rng, 4)
    p["x"] = np.repeat(at(rng, p["t"], rng.integers(0, 16 * U, (N, 8, 1, 1))), C, axis=3)
    p["n"] = rng.choice(np.array([1, 2, 3, M]), (N, 8, 16))
    p["hs"] = p["hs"][..., np.arange(16 * M) >> 2 << 2]
    return pack(p)
def setup_inputs_spread(rng):
    def un(*sh):
        return np.floor(np.exp2(8 * rng.random(sh[:-2] + (1, sh[-1]))) * rng.random(sh)).astype(np.int64)
    p = {"t": rng.integers(0, 256, (N, 8, 16, 1)), "hs": un(N, 8, 16, 16 * M), "x": un(N, 8, 16, C), "dv": un(N, 8, 16, S * C)}
    p["n"] = 1 + np.floor(M * rng.random((N, 8, 16)) ** 3).astype(np.int64)
    p["te"] = np.floor(np.exp2(10 * rng.random((N, 8)))).astype(np.int64) * (rng.random((N, 8)) < 0.75)
    return pack(p)
def check_inputs(d):
    bad = []
    for k, lo, hi in (("hs", 0, 255), ("cn", 1, M), ("x0", 0, 255), ("tg", 0, 255), ("dv", 0, 255), ("te", 0, 1024)):
        v = np.asarray(d[k]).astype(np.float64)
        if not (np.all(v >= lo) and np.all(v <= hi) and np.all(v == np.floor(v))): bad.append("whole numbers and range of " + k)
    v = np.asarray(d["te"]).reshape(N, 8, 16)
    if not np.all(v == v[:, :, :1]): bad.append("te alike in a group")
    return bad
def num(a, k):
    return a.astype(np.float32).astype(np.int64).reshape(N, 8, 16, k)
def energy(z, t):
    return np.add.reduce(np.abs(z - t), axis=-2)
def reference(hs, cn, x0, tg, dv, te):
    x = num(x0, C); goal = num(tg, 1); mv = num(dv, S * C); n = cn.astype(np.int64).reshape(N, 8, 16); T = te.astype(np.int64).reshape(N, 8, 16)[:, :, :1]
    H = np.zeros((N, 8, 16, 16, P), np.int64); H[..., :M] = num(hs, 16 * M).reshape(N, 8, 16, 16, M); H = H.reshape(N, 8, 16, 16 * P)
    cs = np.arange(C)
    for t in range(S):
        E = energy(x, goal); k = np.minimum(15, E >> SH); s = np.add.reduce(x, axis=2)
        bound = E + T * (s & 63); new = []
        for r in range(N):
            ys = []
            for d in range(D):
                q = (r + 1 + d) % N; i = d * J + np.arange(J)
                w = (s[r][:, None, :] + 97 * i[None, :, None] + 31 * t + 5 * cs) & 4095
                h = ((w * w >> 7) + w) & 4095
                nk = np.take_along_axis(n[q], k[r], 1)
                col = P * k[r][:, None, :] + (h * nk[:, None, :] >> 12)
                ys.append(np.take_along_axis(H[q], col.reshape(8, 1, J * C), 2).reshape(8, 16, J, C))
            ys = np.concatenate(ys, axis=2)
            dist = np.add.reduce(np.abs(ys - x[r][:, :, None, :]), axis=1)
            best = np.argmax(dist, axis=1)
            y = np.take_along_axis(ys, best[:, None, None, :], 2)[:, :, 0, :]
            z = np.abs(x[r] - mv[r][..., t * C:(t + 1) * C])
            oky = energy(y, goal[r]) <= bound[r]; okz = energy(z, goal[r]) <= bound[r]
            new.append(np.where(oky[:, None, :], y, np.where(okz[:, None, :], z, x[r])))
        x = np.stack(new)
        k = np.minimum(15, energy(x, goal) >> SH)
        eq = (k[:, :, None, :] == np.arange(16)[:, None]).astype(np.int64)
        place = np.take_along_axis(n[..., None] + np.add.accumulate(eq, axis=3) - eq, k[:, :, None, :], 2)[:, :, 0, :]
        for r in range(N):
            for g in range(8):
                m = place[r, g] < P
                H[r, g][:, (P * k[r, g] + place[r, g])[m]] = x[r, g][:, m]
        n = np.minimum(P, n + np.add.reduce(eq, axis=3))
    return {"yx": x.reshape(N, 128, C).astype(np.float32).astype(BF), "yn": n.reshape(N, 128, 1).astype(np.float32)}

@@ -1,0 +1,565 @@
+from concourse.bass import DstId, RemoteDMATransfer
+from concourse.mybir import AluOpType as ALU, ActivationFunctionType as ACT
+
+NR = 8
+STEPS = 3
+RING = 320
+WIDE = 512
+BLOCKS = [[512, 512, 512, 512], [512, 512, 512, 256, 256]]
+ONV = []
+MAGIC = 128.5078125
+HEAD = 2048
+BYDMA = 9
+BYS = 4
+CY, OVH, WAKE, GAT, SCA, PEC, HOP, ROW, RATE, CALL = 0.00104, 0.04, 0.06, 1.56, 3.8, 0.0006, 1.8, 0.05, 20e3, 0.5
+AT = {"ld0": 2.4, "ldt": 2.8, "ldc": 3.2, "go": 4.0, "h1a": 5.0, "h1b": 9.5, "ldv": 10.2, "h2": 18.5}
+LOOK, TOL, BETA, PEN = 0.6, 0.03, 0.3, 1.0
+
+SCRATCH = {}
+for _dt, _bufs in (
+    ("bfloat16", dict(H1=16 * RING, H2=16 * WIDE, IN0=144, X=416, DVS=392, DVL=784, ID=128, IDN=128, IDN64=128, IDBIG=128,
+                      BB=128, BN=128, B1024=128, BN512=128, BK=128, MA=128, C16=128, C256=128, ONE=128, RB=128, BS=24,
+                      RN=16 * STEPS, AX=384, KQ=384, EQ=384, VV=128, T2N=512, TQ=256, ZZ=256, AZ=256, OKZ=256, MZ=256,
+                      Y0=2048, Y1=2048, M0=2048, M1=2048, YB=256, AY=256, MB=256, OKY=256)),
+    ("int32", dict(CNI=4, TEI=4, TE2=4, PI=4, KI=128, RI=128, CI=256, TI1=128, TI2=128, TI3=128, TI4=128, MI=384, XI=384,
+                   UI=256, WI=256, PP=256, HI=256, AI=256, PL=256, CL=256, BI=32)),
+    ("float32", dict(COL=16, CC=256 * STEPS, IDF=128, RS=128, D0=128, CT=128, RF=128, SC2=128, T2S=256, TS=256, S1=256,
+                     TT=256, MY=256, KA=384 * STEPS, KB=384 * STEPS, YN=4)),
+    ("uint16", dict(SOFF=8, OFF=256, BOFF=16)),
+):
+    for _n, _c in _bufs.items():
+        SCRATCH[_n] = ("sbuf", [128, _c], _dt)
+for _b in range(8):
+    SCRATCH["PB%d" % _b] = ("psum", [128, 512], "float32")
+
+SEMAPHORES = ["qv", "qs", "qp", "qg", "ld0", "ldv", "ldt", "ldc", "h1a", "h1b", "h2", "go", "sent", "xa0", "xa1", "da0",
+              "da1", "db0", "db1", "out0", "out1"]
+for _t in range(STEPS):
+    SEMAPHORES += ["ka1_%d" % _t, "ka2_%d" % _t, "kb0_%d" % _t, "kb2_%d" % _t]
+
+
+def banks(o):
+    return set(n[1] for n in o["r"] + o["w"] if n[0] == "#")
+
+
+def hazards(o, k, writer, readers):
+    deps = set(writer[r] for r in o["r"] if r in writer)
+    for w in o["w"]:
+        if w in writer:
+            deps.add(writer[w])
+        deps.update(readers.get(w, []))
+    for r in o["r"]:
+        if o["inc"]:
+            readers.setdefault(r, []).append(k)
+    for w in o["w"]:
+        writer[w] = k
+        readers[w] = []
+    deps.discard(k)
+    return deps
+
+
+def schedule(progs):
+    ops, pred, sender = [], [], {}
+    for role, prog in enumerate(progs):
+        writer, readers, fixed = {}, {}, {}
+        for o in prog:
+            k = len(ops)
+            ops.append((role, o))
+            p = {d: WAKE for d in hazards(o, k, writer, readers)}
+            line = o["e"] if o["e"] in "gy" or not o["inc"] else o["line"]
+            if line:
+                if line in fixed:
+                    p.setdefault(fixed[line], 0.0)
+                fixed[line] = k
+            pred.append(p)
+            for s, lat in o["out"]:
+                sender[role, s] = (k, lat)
+    base = [0.0] * len(ops)
+    for k, (role, o) in enumerate(ops):
+        for s, v, frm in o["x"]:
+            if s in AT:
+                base[k] = max(base[k], AT[s])
+            else:
+                d, lat = sender[frm, s]
+                pred[k][d] = lat
+    prio = [o["c"] + o["tail"] for role, o in ops]
+    moved = True
+    while moved:
+        moved = False
+        for k in range(len(ops) - 1, -1, -1):
+            for d, lat in pred[k].items():
+                v = prio[k] + lat + ops[d][1]["c"]
+                if v > prio[d] + 1e-9:
+                    prio[d], moved = v, True
+    prio = [p - o["pen"] for p, (role, o) in zip(prio, ops)]
+    succ = [[] for _ in ops]
+    for k, p in enumerate(pred):
+        for d in p:
+            succ[d].append(k)
+    left = [len(p) for p in pred]
+    ready, free, bank, end, late, order = {}, {}, {}, {}, {}, [[] for _ in progs]
+    for k, (role, o) in enumerate(ops):
+        if not left[k]:
+            ready.setdefault((role, o["e"]), []).append(k)
+
+    def start(k):
+        role, o = ops[k]
+        t = max([base[k], free.get((role, o["e"]), 0.0)]
+                + [end[d] + lat + late.get(d, 0.0) * (lat > 1) for d, lat in pred[k].items()])
+        for b in banks(o):
+            for e2, t2 in bank.get((role, b), {}).items():
+                if e2 != o["e"]:
+                    t = max(t, t2 + WAKE)
+        return t
+
+    while True:
+        pick = None
+        for q, cand in ready.items():
+            if cand:
+                st = {k: start(k) for k in cand}
+                t0 = min(st.values())
+                if pick is None or t0 < pick[0]:
+                    pick = (t0, q, st)
+        if pick is None:
+            return order
+        t0, q, st = pick
+        top = max((k for k in st if st[k] <= t0 + LOOK), key=lambda k: (prio[k], -k))
+        if st[top] > t0 + 0.02:
+            fit = [k for k in st if st[k] + ops[k][1]["c"] <= st[top] + TOL]
+            now = max((k for k in st if st[k] <= t0 + 0.02), key=lambda k: (prio[k], -k))
+            if fit:
+                top = max(fit, key=lambda k: (prio[k], -k))
+            elif st[top] - t0 >= BETA * ops[now][1]["c"]:
+                top = now
+        role, o = ops[top]
+        end[top] = free[q] = st[top] + o["c"]
+        if o["out"]:
+            late[top] = max(0.0, free.get((role, "d"), 0.0) - end[top])
+            free[role, "d"] = end[top] + late[top] + max(lat for s, lat in o["out"]) - HOP
+        for b in banks(o):
+            bank.setdefault((role, b), {})[o["e"]] = end[top]
+        ready[q].remove(top)
+        order[role].append(o)
+        for k in succ[top]:
+            left[k] -= 1
+            if not left[k]:
+                ready.setdefault((ops[k][0], ops[k][1]["e"]), []).append(k)
+
+
+def emit(g, T, ops):
+    queue = {"v": g.vector, "s": g.scalar, "p": g.tensor, "g": g, "y": g.sync}
+    semof = {"v": T.sem.qv, "s": T.sem.qs, "p": T.sem.qp, "g": T.sem.qg}
+    writer, readers, bank = {}, {}, {}
+    known = {e: {} for e in queue}
+    clock, waits, needed = [], [], set()
+    for k, o in enumerate(ops):
+        e = o["e"]
+        deps = hazards(o, k, writer, readers)
+        for b in banks(o):
+            deps.update(k2 for e2, k2 in bank.get(b, {}).items() if e2 != e)
+            bank.setdefault(b, {})[e] = k
+        kn = known[e]
+        mine = []
+        for d in sorted(deps, reverse=True):
+            e2 = ops[d]["e"]
+            if (e2 == "p" and e == "p") or kn.get("@" + e2, -1) >= d:
+                continue
+            mine.append(("@", d))
+            needed.add(d)
+            for key, val in clock[d].items():
+                if kn.get(key, -1) < val:
+                    kn[key] = val
+        for s, v, frm in o["x"]:
+            if kn.get(s, 0) < v:
+                mine.append((s, v))
+                kn[s] = v
+        c = dict(kn)
+        if o["inc"]:
+            c["@" + e] = k
+        clock.append(c)
+        waits.append(mine)
+    count, n = {}, {e: 0 for e in queue}
+    for k, o in enumerate(ops):
+        if k in needed:
+            n[o["e"]] += 1
+            count[k] = n[o["e"]]
+    for k, o in enumerate(ops):
+        q = queue[o["e"]]
+        for s, v in waits[k]:
+            if s == "@":
+                q.wait_ge(semof[ops[v]["e"]], count[v])
+            else:
+                q.wait_ge(T.sem[s], v)
+        ins = o["f"](q)
+        if k in needed:
+            ins.then_inc(semof[o["e"]], 1)
+
+
+def engine_sets(topo, src, dsts):
+    open_to = [topo.engines(src, d) for d in dsts]
+    order = sorted(range(len(dsts)), key=lambda i: len(open_to[i]))
+    res, used = [None] * len(dsts), []
+    for pos, i in enumerate(order):
+        free = [e for e in open_to[i] if e not in used]
+        rivals = len([j for j in order[pos:] if len(open_to[j]) == len(open_to[i])])
+        share = len(free) // rivals
+        n = 1
+        while 2 * n <= share:
+            n *= 2
+        res[i] = free[:n]
+        used += res[i]
+    return res
+
+
+def role_of(T, topo, rank):
+    return 0 if topo.chip(T.cores[rank % NR]) == topo.chip(T.cores[(rank + 1) % NR]) else 1
+
+
+def program(T, topo, rank):
+    ops = []
+    sent = [0]
+
+    def peer(k, of=rank):
+        return T.cores[(of + k) % NR]
+
+    def op(e, f, r=(), w=(), x=(), c=0.0, inc=True, out=(), tail=0.0):
+        x = [(s[0], s[1], role_of(T, topo, rank + s[2]) if len(s) > 2 else 0) for s in x]
+        ops.append({"e": e, "f": f, "r": list(r), "w": list(w), "x": x, "c": c, "inc": inc, "out": out, "tail": tail,
+                    "line": None, "pen": 0.0})
+
+    def cost(n):
+        return OVH + max(64, n) * CY
+
+    def ts(out, in0, s1, s2, o0, o1, r, w, x=(), n=128):
+        op("v", lambda q: q.tensor_scalar(out, in0, s1, s2, o0, o1), r, w, x, cost(n))
+
+    def t1(out, in0, s1, o0, r, w, x=(), n=128):
+        op("v", lambda q: q.tensor_scalar(out, in0, s1, None, o0), r, w, x, cost(n))
+
+    def tt(out, a, c, o, r, w, x=(), n=128):
+        op("v", lambda q: q.tensor_tensor(out, a, c, o), r, w, x, cost(n))
+
+    def cp(out, a, r, w, x=(), n=128):
+        op("v", lambda q: q.tensor_copy(out, a), r, w, x, cost(n))
+
+    def fill(out, v, w):
+        op("v", lambda q: q.memset(out, v), (), w, (), cost(64))
+
+    def scan(out, d0, d1, init, o0, o1, r, w):
+        op("v", lambda q: q.tensor_tensor_scan(out, d0, d1, init, o0, o1), r, w, (), cost(128))
+
+    def act(out, a, fn, r, w, x=(), bias=None, scale=None, n=128):
+        kw = {}
+        if bias is not None:
+            kw["bias"] = bias
+        if scale is not None:
+            kw["scale"] = scale
+        op("s", lambda q: q.activation(out, a, fn, **kw), r, w, x, cost(n))
+
+    def mms(groups, r, w, n, x=()):
+        def f(q):
+            for out, terms in groups:
+                for i, (l, rh) in enumerate(terms):
+                    ins = q.matmul(out, l, rh, i == 0, i == len(terms) - 1)
+            return ins
+        op("p", f, r, w, x, n * PEC + 0.004 * sum(len(t) for o, t in groups))
+
+    def mm(out, terms, r, w, x=()):
+        mms([(out, terms)], r, w, 128 * len(terms), x)
+
+    def dma(e, out, a, sem, r=(), x=(), tail=0.0):
+        op(e, lambda q: q.dma_start(out, a).then_inc(T.sem[sem], 16), r, (), x, 0.06, False, (), tail)
+
+    def plan(src_rank, offs):
+        return engine_sets(topo, peer(0, src_rank), [peer(k, src_rank) for k in offs])
+
+    def send(items, nbytes, r, x=(), first=0.0):
+        sets = plan(rank, [it[0] for it in items])
+        trs, out = [], []
+        for (k, src, dst, sem), es in zip(items, sets):
+            rid, pid, _ = topo.addr(peer(k))
+            m = 0
+            for e in es:
+                m |= 1 << e
+            trs.append(RemoteDMATransfer(dst_ids=[DstId(rid=rid, pnc=pid)], dma_engine_mask=m, remote_sem=T.sem[sem],
+                                         src=src, dst=dst))
+            sent[0] += len(es)
+            out.append((sem, HOP + 128 / len(es) * (ROW + nbytes / RATE)))
+        op("g", lambda q: q.remote_dma_fused(trs, local_sem=T.sem.sent), r, (), x, CALL + first, False, out)
+
+    def arrival(sem, k, offs):
+        return (sem, len(plan(rank + k, offs)[offs.index(-k)]), k)
+
+    PB = [T["PB%d" % b] for b in range(8)]
+    X, COL = T.X, T.COL
+    YY, MM, KK = [T.Y0, T.Y1], [T.M0, T.M1], [T.KA, T.KB]
+    xcol = [8, 144, 272]
+    xs = [X[:, c:c + 128] for c in xcol]
+    tgc = [X[:, 7:8], X[:, 143:144], T.IN0[:, 7:8]]
+    E, Z = (1, 0) if role_of(T, topo, rank) == 0 else (0, 1)
+
+    def sl(buf, d, n=128):
+        return buf[:, d * n:(d + 1) * n]
+
+    def ps(b, s):
+        return "#%d%d" % (b, s)
+
+    def key_offs(d, t):
+        if t == STEPS - 1:
+            return [-1 - d]
+        return [1, -1] if d == 0 else [-1, -2]
+
+    dma("y", T.IN0[:, 8:136], T.x0[:], "ld0")
+    dma("s", T.IN0[:, 7:8], T.tg[:], "ld0", tail=999.0)
+    dma("s", T.TEI[:, 0:1], T.te[:], "ldt", tail=999.0)
+    dma("s", T.CNI[:, 0:1], T.cn[:], "ldc", tail=999.0)
+    dma("y", T.H1[:, 0:HEAD], T.hs[:, 0:HEAD], "h1a")
+    op("g", lambda q: q.iota(T.PI[:, 0:1], [[0, 1]], 0, 1), (), ["PI0"], c=0.14)
+    op("g", lambda q: q.iota(T.KI[:], [[1, 128]], 0, 0), (), ["KI"], c=0.4)
+    op("g", lambda q: q.iota(T.RI[:], [[0, 16], [1, 8]], 0, -1), (), ["RI"], c=0.4)
+    op("g", lambda q: q.iota(T.CI[:], [[97 * 16, 2], [-97, 16], [80, 8]], 97 * 15, 0), (), ["CI"], c=0.66)
+    send([(1, T.IN0[:, 7:136], X[:, 7:136], "xa0"), (2, T.IN0[:, 7:136], X[:, 143:272], "xa1")], 258, (), [("ld0", 32)], 1.0)
+    op("g", lambda q: q.sem_inc(T.sem.go, 1), inc=False)
+    dma("y", T.H1[:, HEAD:5120], T.hs[:, HEAD:5120], "h1b", x=[("go", 1)])
+    dma("y", T.DVS[:, 8:392], T.dv[:], "ldv")
+    t1(T.TE2[:, 0:1], T.TEI[:, 0:1], 3, ALU.arith_shift_right, [], ["TE20"], [("ldt", 16)], 1)
+    t1(T.TE2[:, 1:2], T.TEI[:, 0:1], 7, ALU.bitwise_and, [], ["TE21"], [("ldt", 16)], 1)
+    cp(T.DVS[:, 6:8], T.TE2[:, 0:2], ["TE20", "TE21"], ["DVS"], n=2)
+    send([(1, T.DVS[:, 6:136], T.DVL[:, 6:136], "da0"), (2, T.DVS[:, 6:136], T.DVL[:, 398:528], "da1")], 260, ["DVS"],
+         [("ldv", 16)])
+    send([(1, T.DVS[:, 136:392], T.DVL[:, 136:392], "db0"), (2, T.DVS[:, 136:392], T.DVL[:, 528:784], "db1")], 512, [])
+    for k in range(BYDMA):
+        dma("y", T.H2[:, WIDE * k:WIDE * k + RING], T.hs[:, RING * k:RING * (k + 1)], "h2", x=[("ldv", 16)])
+
+    cp(COL[:, 0:1], T.PI[:, 0:1], ["PI0"], ["c0"], n=1)
+    t1(T.PI[:, 1:2], T.PI[:, 0:1], 4, ALU.arith_shift_right, ["PI0"], ["PI1"], n=1)
+    t1(T.PI[:, 2:3], T.PI[:, 0:1], 15, ALU.bitwise_and, ["PI0"], ["PI2"], n=1)
+    t1(COL[:, 5:6], T.PI[:, 0:1], 16.0, ALU.mult, ["PI0"], ["c5"], n=1)
+    cp(COL[:, 1:2], T.PI[:, 1:2], ["PI1"], ["c1"], n=1)
+    t1(T.TI1[:], T.KI[:], COL[:, 0:1], ALU.subtract, ["KI", "c0"], ["TI1"])
+    t1(T.TI2[:], T.KI[:], 4, ALU.arith_shift_right, ["KI"], ["TI2"])
+    t1(T.TI3[:], T.KI[:], 15, ALU.bitwise_and, ["KI"], ["TI3"])
+    t1(T.ID[:], T.TI1[:], 0.0, ALU.is_equal, ["TI1"], ["ID"])
+    t1(T.BB[:], T.TI2[:], COL[:, 1:2], ALU.is_equal, ["TI2", "c1"], ["BB"])
+    for col, fac, o in ((3, 129.0, ALU.add), (4, 5.0, ALU.mult), (6, float(WIDE), ALU.mult), (7, float(RING), ALU.mult)):
+        t1(COL[:, col:col + 1], T.PI[:, 2:3], fac, o, ["PI2"], ["c%d" % col], n=1)
+    t1(T.RF[:], T.RI[:], 0.0, ALU.is_equal, ["RI"], ["RF"])
+    t1(T.RB[:], T.RI[:], 0.0, ALU.is_equal, ["RI"], ["RB"])
+    cp(T.BS[:, 0:8], T.BB[:, 0:128:16], ["BB"], ["BS0"], n=8)
+    for buf, v in (("C256", 256.0), ("C16", 16.0), ("ONE", 1.0)):
+        fill(T[buf][:], v, [buf])
+    t1(T.BS[:, 8:16], T.BS[:, 0:8], 4096.0, ALU.mult, ["BS0"], ["BSP"], n=8)
+    t1(T.BS[:, 16:24], T.BS[:, 0:8], -2048.0, ALU.mult, ["BS0"], ["BSN"], n=8)
+    for buf, src, v in (("IDN", "ID", -1.0), ("IDN64", "ID", -64.0), ("IDBIG", "ID", 16384.0), ("BN", "BB", -1.0),
+                        ("B1024", "BB", 1024.0), ("BN512", "BB", -512.0)):
+        t1(T[buf][:], T[src][:], v, ALU.mult, [src], [buf], n=64)
+    cp(T.IDF[:], T.ID[:], ["ID"], ["IDF"])
+    t1(T.RS[:], T.TI3[:], 0.0, ALU.is_gt, ["TI3"], ["RS"])
+    t1(T.CT[:], T.TI3[:], COL[:, 5:6], ALU.add, ["TI3", "c5"], ["CT"])
+    ts(T.D0[:], T.RS[:], float(2 ** 25 + 128), -float(2 ** 25), ALU.mult, ALU.add, ["RS"], ["D0"])
+    t1(COL[:, 12:13], T.CNI[:, 0:1], -256.0, ALU.add, [], ["nm0"], [("ldc", 16)], 1)
+    t1(T.TI4[:], T.TI1[:], 15, ALU.bitwise_and, ["TI1"], ["TI4"])
+    t1(T.RN[:, 0:8], T.BS[:, 0:8], COL[:, 12:13], ALU.mult, ["BS0", "nm0"], ["RNn0"], n=8)
+    t1(T.BK[:], T.BB[:], COL[:, 6:7], ALU.mult, ["BB", "c6"], ["BK"], n=64)
+    t1(T.MA[:], T.TI4[:], 0.0, ALU.is_equal, ["TI4"], ["MA"])
+    for t in range(STEPS):
+        col = 6 if t else 7
+        ts(T.CC[:, 256 * t:256 * t + 256], T.CI[:], COL[:, 4:5], 31.0 * t, ALU.add, ALU.add, ["CI", "c4"], ["CC%d" % t], n=256)
+        t1(T.RN[:, 16 * t + 8:16 * t + 16], T.BS[:, 0:8], COL[:, col:col + 1], ALU.mult, ["BS0", "c%d" % col], ["RNb%d" % t], n=8)
+    for k in range(BYDMA, 16):
+        dst, src = T.H2[:, WIDE * k:WIDE * k + RING], T.H1[:, RING * k:RING * (k + 1)]
+        if k < BYDMA + BYS:
+            act(dst, src, ACT.Copy, [], ["H2r%d" % k], [("h1a", 16), ("h1b", 16)], n=RING)
+        else:
+            cp(dst, src, [], ["H2r%d" % k], [("h1a", 16), ("h1b", 16)], RING // 2)
+    hall = ["H2r%d" % k for k in range(BYDMA, 16)] + ["H2"]
+
+    def kext(d, t, j):
+        s = [[None, ("kb0", 1)], [("ka1", -1), None], [("ka2", 1), ("kb2", 2)]][d][j]
+        return [] if s is None else [arrival("%s_%d" % (s[0], t), s[1], key_offs(j, t))]
+
+    def finish(d, t, park):
+        o = 384 * t + 128 * d
+        a, r = [T.KA[:, o:o + 128], T.KB[:, o:o + 128]], ["key%d_%d" % (d, t)]
+        j, b, slot = park
+        act(sl(PB[b], slot), a[j], ACT.Copy, r, [ps(b, slot)], kext(d, t, j))
+        a[j], r = sl(PB[b], slot), r + [ps(b, slot)]
+        tt(sl(T.MI, d), a[0], a[1], ALU.max, r, ["MI%d" % d], kext(d, t, 0) + kext(d, t, 1))
+        t1(sl(T.XI, d), sl(T.MI, d), 255, ALU.bitwise_and, ["MI%d" % d], ["XI%d" % d])
+        cp(xs[d], sl(T.XI, d), ["XI%d" % d], ["X%d" % d])
+
+    def xext(d):
+        return [("ld0", 32)] if d == 2 else [arrival("xa%d" % d, -1 - d, [1, 2])]
+
+    def ring(d):
+        act(sl(T.AX, d), xs[d], ACT.Abs, ["X%d" % d], ["AX%d" % d], xext(d), tgc[d], -1.0)
+        mm(sl(PB[6], d), [(T.BB[:], sl(T.AX, d))], ["BB", "AX%d" % d], [ps(6, d)])
+        act(sl(T.KQ, d), sl(PB[6], d), ACT.Identity, [ps(6, d)], ["KQ%d" % d], bias=MAGIC, scale=1.0 / 64)
+        ts(sl(T.EQ, d), sl(T.KQ, d), 144.0, COL[:, 3:4], ALU.min, ALU.is_equal, ["KQ%d" % d, "c3"], ["EQ%d" % d], n=64)
+
+    def hashes(d, t):
+        o, b = 256 * t + 128 * d, 4 + d
+        mms([(PB[b][0:8, 128 + a:256:16], [(X[:, xcol[d] + a:xcol[d] + 128:16], T.BS[:, 0:8])]) for a in range(16)],
+            ["X%d" % d, "BS0"], [ps(b, 1)], 128, xext(d))
+        act(T.T2S[0:8, 128 * d:128 * d + 128], PB[b][0:8, 128:256], ACT.Copy, [ps(b, 1)], ["T2S%d" % d])
+        mms([(sl(PB[b], 0), [(T.T2S[0:8, 128 * d:128 * d + 128], T.RF[0:8, :])])], ["T2S%d" % d, "RF"], [ps(b, 0)], 512)
+        tt(sl(T.UI, d), sl(PB[b], 0), T.CC[:, o:o + 128], ALU.add, [ps(b, 0), "CC%d" % t], ["UI%d" % d])
+        t1(sl(T.WI, d), sl(T.UI, d), 4095, ALU.bitwise_and, ["UI%d" % d], ["WI%d" % d])
+        t1(sl(PB[b], 1), sl(T.WI, d), 128.0, ALU.add, ["WI%d" % d], [ps(b, 1)])
+        tt(sl(T.PP, d), sl(T.WI, d), sl(PB[b], 1), ALU.mult, ["WI%d" % d, ps(b, 1)], ["PP%d" % d])
+        ts(sl(T.HI, d), sl(T.PP, d), 7, 4095, ALU.arith_shift_right, ALU.bitwise_and, ["PP%d" % d], ["HI%d" % d])
+
+    def xrep(d):
+        mms([(sl(PB[d], k), [(T.ID[:], xs[d])]) for k in range(4)], ["ID", "X%d" % d], [ps(d, k) for k in range(4)], 512,
+            xext(d))
+
+    def counts(d, t, lo, hi):
+        o, b = 256 * d, 4 + d
+        slots = [ps(b, 2 + k) for k in range(lo, hi)]
+        mms([(PB[b][0:8, 256 + 128 * lo + a:256 + 128 * hi:16],
+              [(T.EQ[:, 128 * d + a:128 * d + 128:16], T.RN[:, 16 * t + 8 * lo:16 * t + 8 * hi])]) for a in range(16)],
+            ["EQ%d" % d] + ["RNn%d" % t, "RNb%d" % t][lo:hi], slots, 128 * (hi - lo))
+        names = ["T2N%d%d" % (d, k) for k in range(lo, hi)]
+        act(T.T2N[0:8, o + 128 * lo:o + 128 * hi], PB[b][0:8, 256 + 128 * lo:256 + 128 * hi], ACT.Copy, slots, names,
+            n=128 * (hi - lo))
+        if lo == 0:
+            mm(sl(PB[b], 2), [(T.C256[0:8, :], T.RB[0:8, :]), (T.T2N[0:8, o:o + 128], T.RB[0:8, :])],
+               ["C256", "RB", names[0]], [ps(b, 2)])
+        if hi == 2:
+            mm(sl(PB[b], 3), [(T.T2N[0:8, o + 128:o + 256], T.RB[0:8, :])], ["RB", names[-1]], [ps(b, 3)])
+
+    def places(d):
+        b = 4 + d
+        tt(sl(T.AI, d), sl(T.HI, d), sl(PB[b], 2), ALU.mult, ["HI%d" % d, ps(b, 2)], ["AI%d" % d])
+        t1(sl(T.PL, d), sl(T.AI, d), 12, ALU.arith_shift_right, ["AI%d" % d], ["PL%d" % d])
+        tt(sl(T.CL, d), sl(T.PL, d), sl(PB[b], 3), ALU.add, ["PL%d" % d, ps(b, 3)], ["CL%d" % d])
+        cp(sl(T.OFF, d), sl(T.CL, d), ["CL%d" % d], ["OFF%d" % d])
+
+    def fallback(d, t):
+        o = 392 * d
+        if t == 0:
+            ts(COL[:, 8 + d:9 + d], T.DVL[:, o + 6:o + 7], 8.0, T.DVL[:, o + 7:o + 8], ALU.mult, ALU.add, [], ["T%d" % d],
+               [arrival("da%d" % d, -1 - d, [1, 2])], 1)
+            t1(COL[:, 10 + d:11 + d], COL[:, 8 + d:9 + d], 129.0 * 64, ALU.mult, ["T%d" % d], ["TB%d" % d], n=1)
+        o += 8 + 128 * t
+        a, b, c = (sl(PB[7], d), ps(7, d)), (sl(PB[7], 2 + d), ps(7, 2 + d)), (sl(PB[6], d), ps(6, d))
+        mm(a[0], [(T.BB[:], xs[d])], ["BB", "X%d" % d], [a[1]], xext(d))
+        act(sl(T.TQ, d), a[0], ACT.Identity, [a[1]], ["TQ%d" % d], bias=MAGIC, scale=1.0 / 64)
+        mm(b[0], [(T.BB[:], xs[d]), (T.IDN64[:], sl(T.TQ, d))], ["BB", "X%d" % d, "IDN64", "TQ%d" % d], [b[1]])
+        act(sl(T.TS, d), b[0], ACT.Identity, [b[1], "T%d" % d, "TB%d" % d], ["TS%d" % d],
+            bias=COL[:, 10 + d:11 + d], scale=COL[:, 8 + d:9 + d])
+        mm(c[0], [(T.ID[:], xs[d]), (T.IDN[:], T.DVL[:, o:o + 128])], ["ID", "IDN", "X%d" % d], [c[1]],
+           xext(d) + [arrival(("db%d" if t else "da%d") % d, -1 - d, [1, 2])])
+        act(sl(T.ZZ, d), c[0], ACT.Abs, [c[1]], ["ZZ%d" % d])
+        act(sl(T.AZ, d), sl(T.ZZ, d), ACT.Abs, ["ZZ%d" % d], ["AZ%d" % d], bias=tgc[d], scale=-1.0)
+        mm(a[0], [(T.ID[:], sl(T.ZZ, d)), (T.IDN[:], xs[d])], ["ID", "IDN", "ZZ%d" % d, "X%d" % d], [a[1]])
+        mm(c[0], [(T.BN[:], sl(T.AX, d)), (T.BB[:], sl(T.AZ, d))], ["BB", "BN", "AZ%d" % d, "AX%d" % d], [c[1]])
+        tt(sl(T.OKZ, d), c[0], sl(T.TS, d), ALU.is_le, [c[1], "TS%d" % d], ["OKZ%d" % d])
+        tt(sl(T.MZ, d), a[0], sl(T.OKZ, d), ALU.mult, [a[1], "OKZ%d" % d], ["MZ%d" % d])
+
+    def job(d, t):
+        second = 0 if d == E else 1
+        b = 2 + second
+        blocks = BLOCKS[second]
+        win = T.H1[:, :] if t == 0 else T.H2[:, :]
+        o = 0
+        for k, n in enumerate(blocks):
+            src = win.indirect(T.OFF[:, 128 * d + o // 16:128 * d + (o + n) // 16])
+            r, w, x = ["OFF%d" % d] + (hall if t else []), ["Y%d_%d" % (d, k)], [("h1a", 16), ("h1b", 16)]
+            if (second, k) in ONV:
+                cp(YY[d][:, o:o + n], src, r, w, x, n * GAT)
+            else:
+                act(YY[d][:, o:o + n], src, ACT.Copy, r, w, x, n=n * GAT)
+                ops[-1]["line"] = "Y"
+            ops[-1]["pen"] = PEN
+            tt(MM[d][:, o:o + n], YY[d][:, o:o + n], PB[d][:, 0:n], ALU.max, w + [ps(d, s) for s in range(4)],
+               ["M%d_%d" % (d, k)], n=n)
+            ops[-1]["pen"] = PEN
+            mms([(PB[b][:, 15 - pos:128:16], [(sl(YY[d], pos), T.BS[:, 16:24]), (sl(MM[d], pos), T.BS[:, 8:16])])
+                 for pos in range(o // 128, (o + n) // 128)], w + ["M%d_%d" % (d, k), "BSP", "BSN"], [ps(b, 0)], n)
+            o += n
+        ys = ["Y%d_%d" % (d, k) for k in range(len(blocks))] + ["BOFF%d" % d]
+        ms = ["M%d_%d" % (d, k) for k in range(len(blocks))] + ["BOFF%d" % d]
+        off = T.BOFF[:, 8 * d:8 * d + 8]
+        o = 384 * t
+        key = KK[d][:, o + 128 * d:o + 128 * d + 128]
+        scan(sl(T.S1, d), T.D0[:], PB[b][:, 0:128], 0.0, ALU.add, ALU.max, ["D0", ps(b, 0)], ["S1%d" % d])
+        mms([(PB[d][0:8, a:128:16], [(T.IDF[:, a:128:16], T.S1[:, 128 * d + 15:128 * d + 128:16])]) for a in range(16)],
+            ["IDF", "S1%d" % d], [ps(d, 0)], 512)
+        tt(T.TT[0:8, 128 * d:128 * d + 128], PB[d][0:8, 0:128], T.CT[0:8, :], ALU.add, [ps(d, 0), "CT"], ["TT%d" % d])
+        mms([(PB[b][:, 0:8], [(T.TT[0:8, 128 * d:128 * d + 128], T.IDF[0:8, 0:8])])], ["TT%d" % d, "IDF"], [ps(b, 0)], 256)
+        cp(T.BI[:, 16 * d:16 * d + 8], PB[b][:, 0:8], [ps(b, 0)], ["BIa%d" % d], n=8)
+        t1(T.BI[:, 16 * d + 8:16 * d + 16], T.BI[:, 16 * d:16 * d + 8], 2047, ALU.bitwise_and, ["BIa%d" % d], ["BIb%d" % d], n=8)
+        cp(off, T.BI[:, 16 * d + 8:16 * d + 16], ["BIb%d" % d], ["BOFF%d" % d], n=8)
+        act(sl(T.AY, d), YY[d][:, :].indirect(off), ACT.Abs, ys, ["AY%d" % d], xext(d), tgc[d], -1.0, 128 * GAT)
+        cp(sl(T.YB, d), YY[d][:, :].indirect(off), ys, ["YB%d" % d], n=128 * GAT)
+        mm(sl(PB[d], 1), [(T.BN[:], sl(T.AX, d)), (T.BB[:], sl(T.AY, d))], ["BB", "BN", "AX%d" % d, "AY%d" % d], [ps(d, 1)])
+        act(sl(T.MB, d), MM[d][:, :].indirect(off), ACT.Copy, ms, ["MB%d" % d], n=128 * GAT)
+        mm(sl(PB[b], 1), [(T.IDN[:], xs[d]), (T.IDN[:], sl(T.MZ, d)), (T.ID[:], sl(T.YB, d))],
+           ["ID", "IDN", "X%d" % d, "MZ%d" % d, "YB%d" % d], [ps(b, 1)])
+        terms = [(T.ID[:], xs[d]), (T.ID[:], sl(T.MZ, d)), (T.BN512[:], sl(T.YB, d)), (T.B1024[:], sl(T.MB, d))]
+        if d == 0:
+            terms = [(T.BB[:], T.C16[:])] + terms
+        mm(sl(PB[7], 2 + d), terms, ["ID", "BB", "C16", "X%d" % d, "MZ%d" % d, "YB%d" % d, "MB%d" % d, "BN512", "B1024"],
+           [ps(7, 2 + d)])
+        tt(sl(T.OKY, d), sl(PB[d], 1), sl(T.TS, d), ALU.is_le, [ps(d, 1), "TS%d" % d], ["OKY%d" % d])
+        tt(sl(T.MY, d), sl(PB[b], 1), sl(T.OKY, d), ALU.mult, [ps(b, 1), "OKY%d" % d], ["MY%d" % d])
+        tt(key, sl(PB[7], 2 + d), sl(T.MY, d), ALU.add, [ps(7, 2 + d), "MY%d" % d], ["key%d_%d" % (d, t)])
+        land = {(0, 1): (1, "ka1"), (0, -1): (2, "ka2"), (1, -1): (0, "kb0"), (1, -2): (2, "kb2")}
+        items = []
+        for k in key_offs(d, t):
+            slot, sem = land[(d, k)]
+            items.append((k, key, KK[d][:, o + 128 * slot:o + 128 * slot + 128], "%s_%d" % (sem, t)))
+        send(items, 512, ["key%d_%d" % (d, t)])
+
+    POS, last = sl(PB[3], 2), PB[3][:, 383:384]
+
+    def own(t):
+        finish(2, t - 1, (0, 3, 3))
+        ring(2)
+        scan(POS, T.ONE[:], sl(T.EQ, 2), COL[:, 11 + t:12 + t], ALU.mult, ALU.add, ["ONE", "EQ2", "nm%d" % (t - 1)], ["#32"])
+
+    for t in range(STEPS):
+        for d in (E, Z):
+            if t:
+                finish(d, t - 1, (d, d, 2))
+            ring(d)
+            hashes(d, t)
+            xrep(d)
+            fallback(d, t)
+            counts(d, t, 1 if t else 0, 2)
+        if t:
+            own(t)
+            ts(T.RN[:, 16 * t:16 * t + 8], T.BS[:, 0:8], last, 128.0, ALU.mult, ALU.min, ["BS0", "#32"], ["RNn%d" % t], n=8)
+            tt(T.VV[:], sl(T.EQ, 2), POS, ALU.mult, ["EQ2", "#32"], ["VV"])
+            t1(COL[:, 12 + t:13 + t], last, 128.0, ALU.min, ["#32"], ["nm%d" % t], n=1)
+            mm(sl(PB[3], 1), [(T.IDBIG[:], T.MA[:]), (T.BK[:], sl(T.EQ, 2)), (T.BB[:], T.VV[:])],
+               ["IDBIG", "MA", "BK", "EQ2", "BB", "VV"], ["#31"])
+            scan(T.SC2[:], T.RS[:], sl(PB[3], 1), 0.0, ALU.mult, ALU.max, ["RS", "#31"], ["SC2"])
+            t1(T.SOFF[:], T.SC2[:, 15:128:16], 255.0 - 16384.0, ALU.add, ["SC2"], ["SOFF"], n=8)
+            cp(T.H2[:, :].indirect(T.SOFF[:, 0:8]), xs[2], ["SOFF", "X2"], hall, [("h2", 16 * BYDMA)], 128 * SCA)
+            counts(E, t, 0, 1)
+            counts(Z, t, 0, 1)
+        for d in (E, Z):
+            places(d)
+            job(d, t)
+
+    own(STEPS)
+    dma("y", T.yx[:], xs[2], "out0", r=["X2"], tail=2.5)
+    ts(T.YN[:, 0:1], last, 128.0, 256.0, ALU.min, ALU.add, ["#32"], ["YN"], n=1)
+    dma("y", T.yn[:], T.YN[:, 0:1], "out1", r=["YN"], tail=2.3)
+    return ops, sent[0]
+
+
+def rank_program(g, core, T, topo):
+    rank = T.rank_of(core)
+    if rank is None:
+        return
+    role = role_of(T, topo, rank)
+    mine, sent = program(T, topo, rank)
+    other = [r for r in range(NR) if role_of(T, topo, r) != role][0]
+    progs = [mine, program(T, topo, other)[0]]
+    emit(g, T, schedule(progs if role == 0 else progs[::-1])[role])
+    g.sync.wait_ge(T.sem.out0, 16)
+    g.sync.wait_ge(T.sem.out1, 16)
+    g.wait_ge(T.sem.sent, sent)

@@ -6,25 +6,30 @@ STEPS = 3
 RING = 320
 WIDE = 512
 BLOCKS = [[512, 512, 512, 512], [512, 512, 512, 256, 256]]
-ONV = []
+ONV = [[(0, 1)], [(0, 1)]]
+XR = 256
+WRAP = "asss"
+TURN = "sv"
+BEST = "vv"
 MAGIC = 128.5078125
+R64, R2048 = 1.5 * 2 ** 29, 1.5 * 2 ** 34
 HEAD = 2048
-BYDMA = 9
-BYS = 4
-CY, OVH, WAKE, GAT, SCA, PEC, HOP, ROW, RATE, CALL = 0.00104, 0.04, 0.06, 1.56, 3.8, 0.0006, 1.8, 0.05, 20e3, 0.5
-AT = {"ld0": 2.4, "ldt": 2.8, "ldc": 3.2, "go": 4.0, "h1a": 5.0, "h1b": 9.5, "ldv": 10.2, "h2": 18.5}
-LOOK, TOL, BETA, PEN = 0.6, 0.03, 0.3, 1.0
+FW = 272
+CY, OVH, WAKE, SELF, GAT, SCA, PEC, HOP, ROW, RATE, CALL = 0.0009, 0.01, 0.22, 0.2, 1.45, 3.8, 0.00045, 0.6, 0.03, 30e3, 0.3
+AT = {"ld0": 2.4, "ldt": 2.8, "ldc": 3.2, "go": 4.0, "h1a": 5.0, "h1b": 9.8, "ldv": 6.0, "h2": 16.0}
+LOOK, TOL, BETA, PEN, BOOST = 0.4, 0.03, 0.3, 0.5, (4.0, 1.0)
 
 SCRATCH = {}
 for _dt, _bufs in (
-    ("bfloat16", dict(H1=16 * RING, H2=16 * WIDE, IN0=144, X=416, DVS=392, DVL=784, ID=128, IDN=128, IDN64=128, IDBIG=128,
-                      BB=128, BN=128, B1024=128, BN512=128, BK=128, MA=128, C16=128, C256=128, ONE=128, RB=128, BS=24,
-                      RN=16 * STEPS, AX=384, KQ=384, EQ=384, VV=128, T2N=512, TQ=256, ZZ=256, AZ=256, OKZ=256, MZ=256,
-                      Y0=2048, Y1=2048, M0=2048, M1=2048, YB=256, AY=256, MB=256, OKY=256)),
-    ("int32", dict(CNI=4, TEI=4, TE2=4, PI=4, KI=128, RI=128, CI=256, TI1=128, TI2=128, TI3=128, TI4=128, MI=384, XI=384,
-                   UI=256, WI=256, PP=256, HI=256, AI=256, PL=256, CL=256, BI=32)),
-    ("float32", dict(COL=16, CC=256 * STEPS, IDF=128, RS=128, D0=128, CT=128, RF=128, SC2=128, T2S=256, TS=256, S1=256,
-                     TT=256, MY=256, KA=384 * STEPS, KB=384 * STEPS, YN=4)),
+    ("bfloat16", dict(H1=16 * RING, H2=16 * WIDE, IN0=144, X=416, DVS=392, DVL=784, ID=128, IDN=128, ID2=128, IDN64=128,
+                      IDBIG=128, IDW=128, BB=128, BN=128, B1024=128, BN512=128, BK=128, BR=128, BRN=128, BR2=128, CK=128, C16=128,
+                      TG=128, MA=128, ONE=128, RB=128, BS=24, RNB=16, RN=8 * STEPS, AX=384, EQ=384, VV=128, T2N=256, TQ=256,
+                      ZZ=256, AZ=256, OKZ=256, BT=256, SB=256, IX=16, TT=256, Y0=2048, Y1=2048, M0=2048, M1=2048, YB=256,
+                      AY=256, MB=256, OKY=256, MY=256, FB=2 * FW * STEPS)),
+    ("float16", dict(T2=256, RF=128, RG=128)),
+    ("int32", dict(CNI=4, TEI=4, TE2=4, PI=4, KI=128, RI=128, CI=128, TI1=128, TI2=128, TI3=128, TI4=128, PP=256, HI=256,
+                   AI=256, PL=256, MI=384, XI=384)),
+    ("float32", dict(COL=16, RS=128, D0=128, SC2=128, SQ=256, S1=256, RR=16, YN=4, KA=384 * STEPS, KB=384 * STEPS)),
     ("uint16", dict(SOFF=8, OFF=256, BOFF=16)),
 ):
     for _n, _c in _bufs.items():
@@ -32,10 +37,10 @@ for _dt, _bufs in (
 for _b in range(8):
     SCRATCH["PB%d" % _b] = ("psum", [128, 512], "float32")
 
-SEMAPHORES = ["qv", "qs", "qp", "qg", "ld0", "ldv", "ldt", "ldc", "h1a", "h1b", "h2", "go", "sent", "xa0", "xa1", "da0",
-              "da1", "db0", "db1", "out0", "out1"]
+SEMAPHORES = ["qv", "qs", "qp", "qg", "ld0", "ldv", "ldt", "ldc", "h1a", "h1b", "h2", "go", "sent", "xa0", "xa1", "dv0", "dv1",
+              "out0", "out1"]
 for _t in range(STEPS):
-    SEMAPHORES += ["ka1_%d" % _t, "ka2_%d" % _t, "kb0_%d" % _t, "kb2_%d" % _t]
+    SEMAPHORES += [_n + "_%d" % _t for _n in ("ka1", "ka2", "kb0", "kb2", "fa0", "fa1")]
 
 
 def banks(o):
@@ -65,14 +70,15 @@ def schedule(progs):
         for o in prog:
             k = len(ops)
             ops.append((role, o))
-            p = {d: WAKE for d in hazards(o, k, writer, readers)}
+            p = {d: (WAKE if ops[d][1]["e"] != o["e"] else 0.0 if o["e"] == "p" else SELF)
+                 for d in hazards(o, k, writer, readers)}
             line = o["e"] if o["e"] in "gy" or not o["inc"] else o["line"]
             if line:
                 if line in fixed:
                     p.setdefault(fixed[line], 0.0)
                 fixed[line] = k
             pred.append(p)
-            for s, lat in o["out"]:
+            for s, lat, rows in o["out"]:
                 sender[role, s] = (k, lat)
     base = [0.0] * len(ops)
     for k, (role, o) in enumerate(ops):
@@ -105,7 +111,7 @@ def schedule(progs):
     def start(k):
         role, o = ops[k]
         t = max([base[k], free.get((role, o["e"]), 0.0)]
-                + [end[d] + lat + late.get(d, 0.0) * (lat > 1) for d, lat in pred[k].items()])
+                + [end[d] + lat + late.get(d, 0.0) * (lat > HOP) for d, lat in pred[k].items()])
         for b in banks(o):
             for e2, t2 in bank.get((role, b), {}).items():
                 if e2 != o["e"]:
@@ -135,7 +141,7 @@ def schedule(progs):
         end[top] = free[q] = st[top] + o["c"]
         if o["out"]:
             late[top] = max(0.0, free.get((role, "d"), 0.0) - end[top])
-            free[role, "d"] = end[top] + late[top] + max(lat for s, lat in o["out"]) - HOP
+            free[role, "d"] = end[top] + late[top] + max(rows for s, lat, rows in o["out"])
         for b in banks(o):
             bank.setdefault((role, b), {})[o["e"]] = end[top]
         ready[q].remove(top)
@@ -256,297 +262,358 @@ def program(T, topo, rank):
             kw["scale"] = scale
         op("s", lambda q: q.activation(out, a, fn, **kw), r, w, x, cost(n))
 
-    def mms(groups, r, w, n, x=()):
+    def mms(groups, r, w, n, x=(), start=True, stop=True):
         def f(q):
             for out, terms in groups:
                 for i, (l, rh) in enumerate(terms):
-                    ins = q.matmul(out, l, rh, i == 0, i == len(terms) - 1)
+                    ins = q.matmul(out, l, rh, start and i == 0, stop and i == len(terms) - 1)
             return ins
-        op("p", f, r, w, x, n * PEC + 0.004 * sum(len(t) for o, t in groups))
+        state = ["G" + b for b in set(s[1] for s in w)]
+        r, w = (r + state, w) if start and stop else (r, w + state)
+        op("p", f, r, w, x, n * PEC)
+        ops[-1]["n"] = (n, sum(len(t) for o, t in groups))
 
-    def mm(out, terms, r, w, x=()):
-        mms([(out, terms)], r, w, 128 * len(terms), x)
+    def mm(out, terms, r, w, x=(), n=0, **kw):
+        mms([(out, terms)], r, w, n or 128 * len(terms), x, **kw)
 
     def dma(e, out, a, sem, r=(), x=(), tail=0.0):
         op(e, lambda q: q.dma_start(out, a).then_inc(T.sem[sem], 16), r, (), x, 0.06, False, (), tail)
+
+    def iota(out, pattern, base, step, w, c=0.4):
+        op("g", lambda q: q.iota(out, pattern, base, step), (), w, c=c)
 
     def plan(src_rank, offs):
         return engine_sets(topo, peer(0, src_rank), [peer(k, src_rank) for k in offs])
 
     def send(items, nbytes, r, x=(), first=0.0):
-        sets = plan(rank, [it[0] for it in items])
         trs, out = [], []
-        for (k, src, dst, sem), es in zip(items, sets):
+        for (k, src, dst, sem), es in zip(items, plan(rank, [it[0] for it in items])):
+            rows = 128 / len(es) * (ROW + nbytes / RATE)
             rid, pid, _ = topo.addr(peer(k))
-            m = 0
-            for e in es:
-                m |= 1 << e
-            trs.append(RemoteDMATransfer(dst_ids=[DstId(rid=rid, pnc=pid)], dma_engine_mask=m, remote_sem=T.sem[sem],
-                                         src=src, dst=dst))
+            trs.append(RemoteDMATransfer(dst_ids=[DstId(rid=rid, pnc=pid)], dma_engine_mask=sum(1 << e for e in es),
+                                         remote_sem=T.sem[sem], src=src, dst=dst))
             sent[0] += len(es)
-            out.append((sem, HOP + 128 / len(es) * (ROW + nbytes / RATE)))
+            out.append((sem, HOP + rows, rows))
         op("g", lambda q: q.remote_dma_fused(trs, local_sem=T.sem.sent), r, (), x, CALL + first, False, out)
 
     def arrival(sem, k, offs):
         return (sem, len(plan(rank + k, offs)[offs.index(-k)]), k)
 
     PB = [T["PB%d" % b] for b in range(8)]
-    X, COL = T.X, T.COL
+    X, COL, ID = T.X, T.COL, T.ID
     YY, MM, KK = [T.Y0, T.Y1], [T.M0, T.M1], [T.KA, T.KB]
     xcol = [8, 144, 272]
-    xs = [X[:, c:c + 128] for c in xcol]
     tgc = [X[:, 7:8], X[:, 143:144], T.IN0[:, 7:8]]
-    E, Z = (1, 0) if role_of(T, topo, rank) == 0 else (0, 1)
+    role = role_of(T, topo, rank)
+    E, Z = (1, 0) if role == 0 else (0, 1)
 
     def sl(buf, d, n=128):
         return buf[:, d * n:(d + 1) * n]
 
+    def col(k):
+        return COL[:, k:k + 1]
+
     def ps(b, s):
         return "#%d%d" % (b, s)
+
+    def slot(b, s):
+        return sl(PB[b], s), ps(b, s)
+
+    def xs(d):
+        return X[:, xcol[d]:xcol[d] + 128]
+
+    def xext(d):
+        return [("ld0", 32)] if d == 2 else [arrival("xa%d" % d, -1 - d, [1, 2])]
 
     def key_offs(d, t):
         if t == STEPS - 1:
             return [-1 - d]
         return [1, -1] if d == 0 else [-1, -2]
 
+    def kext(d, t, j):
+        s = [[None, ("kb0", 1)], [("ka1", -1), None], [("ka2", 1), ("kb2", 2)]][d][j]
+        return [] if s is None else [arrival("%s_%d" % (s[0], t), s[1], key_offs(j, t))]
+
+    def fmsg(d, t, lo, hi):
+        o = FW * (2 * t + d)
+        return T.FB[:, o + lo:o + hi]
+
+    def fext(d, t):
+        return [arrival("fa%d_%d" % (d, t), 1 - 2 * d, [2 * d - 1])] if role else []
+
     dma("y", T.IN0[:, 8:136], T.x0[:], "ld0")
     dma("s", T.IN0[:, 7:8], T.tg[:], "ld0", tail=999.0)
     dma("s", T.TEI[:, 0:1], T.te[:], "ldt", tail=999.0)
     dma("s", T.CNI[:, 0:1], T.cn[:], "ldc", tail=999.0)
     dma("y", T.H1[:, 0:HEAD], T.hs[:, 0:HEAD], "h1a")
-    op("g", lambda q: q.iota(T.PI[:, 0:1], [[0, 1]], 0, 1), (), ["PI0"], c=0.14)
-    op("g", lambda q: q.iota(T.KI[:], [[1, 128]], 0, 0), (), ["KI"], c=0.4)
-    op("g", lambda q: q.iota(T.RI[:], [[0, 16], [1, 8]], 0, -1), (), ["RI"], c=0.4)
-    op("g", lambda q: q.iota(T.CI[:], [[97 * 16, 2], [-97, 16], [80, 8]], 97 * 15, 0), (), ["CI"], c=0.66)
+    iota(T.PI[:, 0:1], [[0, 1]], 0, 1, ["PI0"], 0.14)
+    iota(T.KI[:], [[1, 128]], 0, 0, ["KI"])
+    iota(T.RI[:], [[0, 16], [1, 8]], 0, -1, ["RI"])
+    iota(T.CI[:], [[-97, 16], [80, 8]], 97 * 15, 0, ["CI"])
     send([(1, T.IN0[:, 7:136], X[:, 7:136], "xa0"), (2, T.IN0[:, 7:136], X[:, 143:272], "xa1")], 258, (), [("ld0", 32)], 1.0)
     op("g", lambda q: q.sem_inc(T.sem.go, 1), inc=False)
-    dma("y", T.H1[:, HEAD:5120], T.hs[:, HEAD:5120], "h1b", x=[("go", 1)])
-    dma("y", T.DVS[:, 8:392], T.dv[:], "ldv")
-    t1(T.TE2[:, 0:1], T.TEI[:, 0:1], 3, ALU.arith_shift_right, [], ["TE20"], [("ldt", 16)], 1)
-    t1(T.TE2[:, 1:2], T.TEI[:, 0:1], 7, ALU.bitwise_and, [], ["TE21"], [("ldt", 16)], 1)
-    cp(T.DVS[:, 6:8], T.TE2[:, 0:2], ["TE20", "TE21"], ["DVS"], n=2)
-    send([(1, T.DVS[:, 6:136], T.DVL[:, 6:136], "da0"), (2, T.DVS[:, 6:136], T.DVL[:, 398:528], "da1")], 260, ["DVS"],
-         [("ldv", 16)])
-    send([(1, T.DVS[:, 136:392], T.DVL[:, 136:392], "db0"), (2, T.DVS[:, 136:392], T.DVL[:, 528:784], "db1")], 512, [])
-    for k in range(BYDMA):
-        dma("y", T.H2[:, WIDE * k:WIDE * k + RING], T.hs[:, RING * k:RING * (k + 1)], "h2", x=[("ldv", 16)])
+    dma("y", T.DVS[:, 8:392], T.dv[:], "ldv", x=[("go", 1)])
+    dma("y", T.H1[:, HEAD:16 * RING], T.hs[:, HEAD:16 * RING], "h1b")
+    for k in range(16):
+        dma("y", T.H2[:, WIDE * k:WIDE * k + RING], T.hs[:, RING * k:RING * (k + 1)], "h2", x=[("h1b", 16)])
 
-    cp(COL[:, 0:1], T.PI[:, 0:1], ["PI0"], ["c0"], n=1)
+    cp(col(0), T.PI[:, 0:1], ["PI0"], ["c0"], n=1)
     t1(T.PI[:, 1:2], T.PI[:, 0:1], 4, ALU.arith_shift_right, ["PI0"], ["PI1"], n=1)
     t1(T.PI[:, 2:3], T.PI[:, 0:1], 15, ALU.bitwise_and, ["PI0"], ["PI2"], n=1)
-    t1(COL[:, 5:6], T.PI[:, 0:1], 16.0, ALU.mult, ["PI0"], ["c5"], n=1)
-    cp(COL[:, 1:2], T.PI[:, 1:2], ["PI1"], ["c1"], n=1)
-    t1(T.TI1[:], T.KI[:], COL[:, 0:1], ALU.subtract, ["KI", "c0"], ["TI1"])
+    cp(COL[:, 1:3], T.PI[:, 1:3], ["PI1", "PI2"], ["c1", "c2"], n=2)
+    t1(T.TE2[:, 0:1], T.TEI[:, 0:1], col(2), ALU.add, ["c2"], ["TE20"], [("ldt", 16)], 1)
+    t1(T.TE2[:, 1:2], T.TE2[:, 0:1], 4, ALU.arith_shift_right, ["TE20"], ["TE21"], n=1)
+    cp(T.DVS[:, 7:8], T.TE2[:, 1:2], ["TE21"], ["DVS"], n=1)
+    send([(2 - role, T.DVS[:, 7:392], T.DVL[:, 399 - 392 * role:784 - 392 * role], "dv%d" % (1 - role))], 770, ["DVS"],
+         [("ldv", 16)])
+    for k, src, v, o in ((4, 0, 8.0, ALU.is_lt), (5, 0, 32.0, ALU.is_ge), (6, 2, float(WIDE), ALU.mult), (7, 0, 16.0, ALU.mult)):
+        t1(col(k), T.PI[:, src:src + 1], v, o, ["PI%d" % src], ["c%d" % k], n=1)
+    ts(col(11), col(2), 15.0, col(2), ALU.is_lt, ALU.mult, ["c2"], ["c11"], n=1)
+    ts(col(3), col(11), 64.0, R64, ALU.mult, ALU.add, ["c11"], ["c3"], n=1)
+    ts(col(8), T.PI[:, 0:1], 32.0, -2048.0, ALU.is_lt, ALU.mult, ["PI0"], ["c8"], n=1)
+    t1(T.TI1[:], T.KI[:], col(0), ALU.subtract, ["KI", "c0"], ["TI1"])
     t1(T.TI2[:], T.KI[:], 4, ALU.arith_shift_right, ["KI"], ["TI2"])
     t1(T.TI3[:], T.KI[:], 15, ALU.bitwise_and, ["KI"], ["TI3"])
-    t1(T.ID[:], T.TI1[:], 0.0, ALU.is_equal, ["TI1"], ["ID"])
-    t1(T.BB[:], T.TI2[:], COL[:, 1:2], ALU.is_equal, ["TI2", "c1"], ["BB"])
-    for col, fac, o in ((3, 129.0, ALU.add), (4, 5.0, ALU.mult), (6, float(WIDE), ALU.mult), (7, float(RING), ALU.mult)):
-        t1(COL[:, col:col + 1], T.PI[:, 2:3], fac, o, ["PI2"], ["c%d" % col], n=1)
-    t1(T.RF[:], T.RI[:], 0.0, ALU.is_equal, ["RI"], ["RF"])
+    t1(ID[:], T.TI1[:], 0.0, ALU.is_equal, ["TI1"], ["ID"])
+    t1(T.BB[:], T.TI2[:], col(1), ALU.is_equal, ["TI2", "c1"], ["BB"])
+    t1(T.RI[:], T.RI[:], 7, ALU.bitwise_and, ["RI"], ["RI"])
+    ts(T.RF[:], T.RI[:], 0.0, col(4), ALU.is_equal, ALU.mult, ["RI", "c4"], ["RF"])
+    cp(T.RF[64:65, :], T.CI[64:65, :], ["CI"], ["RF"])
+    fill(T.RF[96:97, :], 1.0, ["RF"])
+    ts(T.RG[:], T.RI[:], 0.0, col(5), ALU.is_equal, ALU.mult, ["RI", "c5"], ["RG"])
     t1(T.RB[:], T.RI[:], 0.0, ALU.is_equal, ["RI"], ["RB"])
     cp(T.BS[:, 0:8], T.BB[:, 0:128:16], ["BB"], ["BS0"], n=8)
-    for buf, v in (("C256", 256.0), ("C16", 16.0), ("ONE", 1.0)):
-        fill(T[buf][:], v, [buf])
+    fill(T.ONE[:], 1.0, ["ONE"])
+    for d in (0, 1):
+        t1(sl(T.T2, d), T.ONE[:], 0.0, ALU.mult, ["ONE"], ["T2S%d" % d, "T2B%d" % d, "T2C%d" % d], n=64)
+        cp(T.T2[64:65, 128 * d:128 * d + 128], T.ONE[64:65, :], ["ONE"], ["T2C%d" % d], n=64)
+        t1(T.T2[96:97, 128 * d:128 * d + 128], T.TI3[96:97, :], 5.0, ALU.mult, ["TI3"], ["T2C%d" % d])
+        fill(PB[4 + d][0:32, 0:128], 0.0, [ps(4 + d, 0)])
+    fill(T.T2N[:], 256.0, ["T2N0", "T2N1"])
     t1(T.BS[:, 8:16], T.BS[:, 0:8], 4096.0, ALU.mult, ["BS0"], ["BSP"], n=8)
     t1(T.BS[:, 16:24], T.BS[:, 0:8], -2048.0, ALU.mult, ["BS0"], ["BSN"], n=8)
-    for buf, src, v in (("IDN", "ID", -1.0), ("IDN64", "ID", -64.0), ("IDBIG", "ID", 16384.0), ("BN", "BB", -1.0),
-                        ("B1024", "BB", 1024.0), ("BN512", "BB", -512.0)):
+    for k, v in enumerate((RING, WIDE)):
+        ts(sl(T.RNB, k, 8), T.BS[:, 0:8], col(2), float(v), ALU.mult, ALU.mult, ["BS0", "c2"], ["RNB"], n=8)
+    ts(T.CK[:], T.TI3[:], 15.0, -15.5 / 128, ALU.is_equal, ALU.mult, ["TI3"], ["CK"])
+    t1(T.CK[:], T.CK[:], -31.5 / 128, ALU.add, ["CK"], ["CK"], n=64)
+    cp(T.BR[:], T.BB[:], ["BB"], ["BR"], n=64)
+    t1(T.BR[:, 15:128:16], T.BB[:, 15:128:16], 1.0 / 64, ALU.mult, ["BB"], ["BR"], n=8)
+    fill(T.C16[:], 16.0, ["C16"])
+    t1(T.TG[:], T.ONE[:], tgc[2], ALU.mult, ["ONE"], ["TG"], xext(2), 64)
+    mats = [("IDN", "ID", -1.0), ("IDW", "ID", -2048.0), ("ID2", "ID", 2.0), ("BN", "BB", -1.0), ("B1024", "BB", 1024.0),
+            ("BN512", "BB", -512.0), ("IDBIG", "ID", 16384.0), ("BRN", "BR", -1.0), ("BR2", "BR", 2.0), ("IDN64", "ID", -64.0)]
+    for buf, src, v in mats[:len(mats) - role]:
         t1(T[buf][:], T[src][:], v, ALU.mult, [src], [buf], n=64)
-    cp(T.IDF[:], T.ID[:], ["ID"], ["IDF"])
     t1(T.RS[:], T.TI3[:], 0.0, ALU.is_gt, ["TI3"], ["RS"])
-    t1(T.CT[:], T.TI3[:], COL[:, 5:6], ALU.add, ["TI3", "c5"], ["CT"])
-    ts(T.D0[:], T.RS[:], float(2 ** 25 + 128), -float(2 ** 25), ALU.mult, ALU.add, ["RS"], ["D0"])
-    t1(COL[:, 12:13], T.CNI[:, 0:1], -256.0, ALU.add, [], ["nm0"], [("ldc", 16)], 1)
+    ts(T.D0[:], T.RS[:], float(2 ** 25 + 64), -float(2 ** 25), ALU.mult, ALU.add, ["RS"], ["D0"])
+    t1(col(12), T.CNI[:, 0:1], -256.0, ALU.add, [], ["nm0"], [("ldc", 16)], 1)
     t1(T.TI4[:], T.TI1[:], 15, ALU.bitwise_and, ["TI1"], ["TI4"])
-    t1(T.RN[:, 0:8], T.BS[:, 0:8], COL[:, 12:13], ALU.mult, ["BS0", "nm0"], ["RNn0"], n=8)
-    t1(T.BK[:], T.BB[:], COL[:, 6:7], ALU.mult, ["BB", "c6"], ["BK"], n=64)
+    t1(T.RN[:, 0:8], T.BS[:, 0:8], col(12), ALU.mult, ["BS0", "nm0"], ["RN0"], n=8)
+    t1(T.BK[:], T.BB[:], col(6), ALU.mult, ["BB", "c6"], ["BK"], n=64)
     t1(T.MA[:], T.TI4[:], 0.0, ALU.is_equal, ["TI4"], ["MA"])
-    for t in range(STEPS):
-        col = 6 if t else 7
-        ts(T.CC[:, 256 * t:256 * t + 256], T.CI[:], COL[:, 4:5], 31.0 * t, ALU.add, ALU.add, ["CI", "c4"], ["CC%d" % t], n=256)
-        t1(T.RN[:, 16 * t + 8:16 * t + 16], T.BS[:, 0:8], COL[:, col:col + 1], ALU.mult, ["BS0", "c%d" % col], ["RNb%d" % t], n=8)
-    for k in range(BYDMA, 16):
-        dst, src = T.H2[:, WIDE * k:WIDE * k + RING], T.H1[:, RING * k:RING * (k + 1)]
-        if k < BYDMA + BYS:
-            act(dst, src, ACT.Copy, [], ["H2r%d" % k], [("h1a", 16), ("h1b", 16)], n=RING)
+
+    def finish(d, t):
+        a = [sl(K, 3 * t + d) for K in KK]
+        if d == 2:
+            tt(sl(T.MI, d), a[0], a[1], ALU.max, [], ["MI2"], kext(d, t, 0) + kext(d, t, 1), 256)
         else:
-            cp(dst, src, [], ["H2r%d" % k], [("h1a", 16), ("h1b", 16)], RING // 2)
-    hall = ["H2r%d" % k for k in range(BYDMA, 16)] + ["H2"]
-
-    def kext(d, t, j):
-        s = [[None, ("kb0", 1)], [("ka1", -1), None], [("ka2", 1), ("kb2", 2)]][d][j]
-        return [] if s is None else [arrival("%s_%d" % (s[0], t), s[1], key_offs(j, t))]
-
-    def finish(d, t, park):
-        o = 384 * t + 128 * d
-        a, r = [T.KA[:, o:o + 128], T.KB[:, o:o + 128]], ["key%d_%d" % (d, t)]
-        j, b, slot = park
-        act(sl(PB[b], slot), a[j], ACT.Copy, r, [ps(b, slot)], kext(d, t, j))
-        a[j], r = sl(PB[b], slot), r + [ps(b, slot)]
-        tt(sl(T.MI, d), a[0], a[1], ALU.max, r, ["MI%d" % d], kext(d, t, 0) + kext(d, t, 1))
+            p, pn = slot(d, 2)
+            act(p, a[d], ACT.Copy, ["key%d_%d" % (d, t)], [pn])
+            tt(sl(T.MI, d), a[1 - d], p, ALU.max, [pn], ["MI%d" % d], kext(d, t, 1 - d))
         t1(sl(T.XI, d), sl(T.MI, d), 255, ALU.bitwise_and, ["MI%d" % d], ["XI%d" % d])
-        cp(xs[d], sl(T.XI, d), ["XI%d" % d], ["X%d" % d])
-
-    def xext(d):
-        return [("ld0", 32)] if d == 2 else [arrival("xa%d" % d, -1 - d, [1, 2])]
+        cp(xs(d), sl(T.XI, d), ["XI%d" % d], ["X%d" % d])
 
     def ring(d):
-        act(sl(T.AX, d), xs[d], ACT.Abs, ["X%d" % d], ["AX%d" % d], xext(d), tgc[d], -1.0)
-        mm(sl(PB[6], d), [(T.BB[:], sl(T.AX, d))], ["BB", "AX%d" % d], [ps(6, d)])
-        act(sl(T.KQ, d), sl(PB[6], d), ACT.Identity, [ps(6, d)], ["KQ%d" % d], bias=MAGIC, scale=1.0 / 64)
-        ts(sl(T.EQ, d), sl(T.KQ, d), 144.0, COL[:, 3:4], ALU.min, ALU.is_equal, ["KQ%d" % d, "c3"], ["EQ%d" % d], n=64)
+        u, un = slot(6, 0) if d == 2 else slot(4 + d, 2)
+        if d == 2:
+            mm(u, [(T.CK[:], T.ONE[:]), (T.BRN[:], T.TG[:])], ["CK", "ONE", "BRN", "TG"], [un], stop=False)
+            t1(sl(T.AX, d), xs(d), tgc[d], ALU.max, ["X2"], ["AX2"], n=64)
+            mm(u, [(T.BRN[:], xs(d)), (T.BR2[:], sl(T.AX, d))], ["BRN", "BR2", "X2", "AX2"], [un], start=False)
+        else:
+            act(sl(T.AX, d), xs(d), ACT.Abs, ["X%d" % d], ["AX%d" % d], xext(d), tgc[d], -1.0)
+            mm(u, [(T.CK[:], T.ONE[:]), (T.BR[:], sl(T.AX, d))], ["CK", "ONE", "BR", "AX%d" % d], [un])
+        ts(sl(T.EQ, d), u, R64, col(3), ALU.add, ALU.is_equal, [un, "c3"], ["EQ%d" % d])
 
     def hashes(d, t):
-        o, b = 256 * t + 128 * d, 4 + d
-        mms([(PB[b][0:8, 128 + a:256:16], [(X[:, xcol[d] + a:xcol[d] + 128:16], T.BS[:, 0:8])]) for a in range(16)],
-            ["X%d" % d, "BS0"], [ps(b, 1)], 128, xext(d))
-        act(T.T2S[0:8, 128 * d:128 * d + 128], PB[b][0:8, 128:256], ACT.Copy, [ps(b, 1)], ["T2S%d" % d])
-        mms([(sl(PB[b], 0), [(T.T2S[0:8, 128 * d:128 * d + 128], T.RF[0:8, :])])], ["T2S%d" % d, "RF"], [ps(b, 0)], 512)
-        tt(sl(T.UI, d), sl(PB[b], 0), T.CC[:, o:o + 128], ALU.add, [ps(b, 0), "CC%d" % t], ["UI%d" % d])
-        t1(sl(T.WI, d), sl(T.UI, d), 4095, ALU.bitwise_and, ["UI%d" % d], ["WI%d" % d])
-        t1(sl(PB[b], 1), sl(T.WI, d), 128.0, ALU.add, ["WI%d" % d], [ps(b, 1)])
-        tt(sl(T.PP, d), sl(T.WI, d), sl(PB[b], 1), ALU.mult, ["WI%d" % d, ps(b, 1)], ["PP%d" % d])
+        b, o, xo = 4 + d, 128 * d, xcol[d]
+        a0, n0 = PB[b], ps(b, 0)
+        mms([(a0[0:8, a:128:16], [(X[:, xo + a:xo + 128:16], T.BS[:, 0:8])]) for a in range(16)],
+            ["X%d" % d, "BS0"], [n0], 128, xext(d))
+        if t == 0:
+            t1(T.T2[0:8, o:o + 128], a0[0:8, 0:128], -2048.0, ALU.add, [n0], ["T2S%d" % d])
+        mms([(a0[32:40, a:128:16], [(T.EQ[:, o + a:o + 128:16], sl(T.RNB, min(t, 1), 8))]) for a in range(16)],
+            ["EQ%d" % d, "RNB"], [n0], 128)
+        if t == 0:
+            cp(T.T2[32:40, o:o + 128], a0[32:40, 0:128], [n0], ["T2B%d" % d])
+        else:
+            t1(T.T2[0:40, o:o + 128], a0[0:40, 0:128], COL[0:40, 8:9], ALU.add, [n0, "c8"], ["T2S%d" % d, "T2B%d" % d])
+        u, un = slot(b, 1)
+        c0 = 2048.0 + 31.0 * t + 97.0 * 16 * d
+        terms, r = [(T.T2[0:97, o:o + 128], T.RF[0:97, :])], ["T2S%d" % d, "T2C%d" % d, "RF"]
+        mm(u, terms, r, [un])
+        if WRAP[2 * min(t, 1) + (d != E)] == "a":
+            t1(sl(T.PP, d), u, c0, ALU.add, [un], ["PP%d" % d])
+            t1(sl(T.HI, d), sl(T.PP, d), 4095, ALU.bitwise_and, ["PP%d" % d], ["HI%d" % d])
+            t1(u, sl(T.HI, d), 128.0, ALU.add, ["HI%d" % d], [un])
+            tt(sl(T.PP, d), sl(T.HI, d), u, ALU.mult, ["HI%d" % d, un], ["PP%d" % d])
+        else:
+            act(sl(T.SB, d), u, ACT.Sign, [un], ["SB%d" % d], bias=c0 - 4095.5)
+            u, un = slot(b, 3)
+            mm(u, terms + [(T.IDW[:], sl(T.SB, d))], r + ["IDW", "SB%d" % d], [un])
+            act(sl(T.SQ, d), u, ACT.Square, [un], ["SQ%d" % d], bias=c0 - 2048.0 + 64.0)
+            t1(sl(T.PP, d), sl(T.SQ, d), -4096.0, ALU.add, ["SQ%d" % d], ["PP%d" % d])
         ts(sl(T.HI, d), sl(T.PP, d), 7, 4095, ALU.arith_shift_right, ALU.bitwise_and, ["PP%d" % d], ["HI%d" % d])
+        p, pn = slot(2 + (d != E), 1)
+        mm(p, [(T.T2[0:40, o:o + 128], T.RG[0:40, :])], ["T2S%d" % d, "T2B%d" % d, "RG"], [pn])
 
     def xrep(d):
-        mms([(sl(PB[d], k), [(T.ID[:], xs[d])]) for k in range(4)], ["ID", "X%d" % d], [ps(d, k) for k in range(4)], 512,
-            xext(d))
+        ks = range(XR // 128)
+        mms([(sl(PB[d], k), [(ID[:], xs(d))]) for k in ks], ["ID", "X%d" % d], [ps(d, k) for k in ks], XR, xext(d))
 
-    def counts(d, t, lo, hi):
-        o, b = 256 * d, 4 + d
-        slots = [ps(b, 2 + k) for k in range(lo, hi)]
-        mms([(PB[b][0:8, 256 + 128 * lo + a:256 + 128 * hi:16],
-              [(T.EQ[:, 128 * d + a:128 * d + 128:16], T.RN[:, 16 * t + 8 * lo:16 * t + 8 * hi])]) for a in range(16)],
-            ["EQ%d" % d] + ["RNn%d" % t, "RNb%d" % t][lo:hi], slots, 128 * (hi - lo))
-        names = ["T2N%d%d" % (d, k) for k in range(lo, hi)]
-        act(T.T2N[0:8, o + 128 * lo:o + 128 * hi], PB[b][0:8, 256 + 128 * lo:256 + 128 * hi], ACT.Copy, slots, names,
-            n=128 * (hi - lo))
-        if lo == 0:
-            mm(sl(PB[b], 2), [(T.C256[0:8, :], T.RB[0:8, :]), (T.T2N[0:8, o:o + 128], T.RB[0:8, :])],
-               ["C256", "RB", names[0]], [ps(b, 2)])
-        if hi == 2:
-            mm(sl(PB[b], 3), [(T.T2N[0:8, o + 128:o + 256], T.RB[0:8, :])], ["RB", names[-1]], [ps(b, 3)])
-
-    def places(d):
-        b = 4 + d
-        tt(sl(T.AI, d), sl(T.HI, d), sl(PB[b], 2), ALU.mult, ["HI%d" % d, ps(b, 2)], ["AI%d" % d])
+    def places(d, t):
+        o = 128 * d
+        a, an = slot(2 + (d != E), 2)
+        mms([(PB[2 + (d != E)][0:8, 256 + k:384:16], [(T.EQ[:, o + k:o + 128:16], sl(T.RN, t, 8))]) for k in range(16)],
+            ["EQ%d" % d, "RN%d" % t], [an], 128)
+        act(T.T2N[0:8, o:o + 128], a[0:8, :], ACT.Copy, [an], ["T2N%d" % d])
+        mm(a, [(T.T2N[0:16, o:o + 128], T.RB[0:16, :])], ["RB", "T2N%d" % d], [an])
+        p, pn = slot(2 + (d != E), 1)
+        tt(sl(T.AI, d), sl(T.HI, d), a, ALU.mult, ["HI%d" % d, an], ["AI%d" % d])
         t1(sl(T.PL, d), sl(T.AI, d), 12, ALU.arith_shift_right, ["AI%d" % d], ["PL%d" % d])
-        tt(sl(T.CL, d), sl(T.PL, d), sl(PB[b], 3), ALU.add, ["PL%d" % d, ps(b, 3)], ["CL%d" % d])
-        cp(sl(T.OFF, d), sl(T.CL, d), ["CL%d" % d], ["OFF%d" % d])
+        tt(sl(T.AI, d), sl(T.PL, d), p, ALU.add, ["PL%d" % d, pn], ["AI%d" % d])
+        cp(sl(T.OFF, d), sl(T.AI, d), ["AI%d" % d], ["OFF%d" % d])
+
+    def tmat(d):
+        ts(sl(T.BT, d), T.BB[:], fmsg(d, 0, 256, 257), -1.0, ALU.mult, ALU.mult, ["BB", "TP%d" % d], ["BT%d" % d], fext(d, 0), 64)
 
     def fallback(d, t):
-        o = 392 * d
+        b, o, xn = 4 + d, 392 * d, "X%d" % d
+        (a, an), (c, cn), (e, en) = slot(b, 1), slot(b, 2), slot(b, 3)
+        x, m, ext = xs(d), fmsg(d, t, 128, 256), [arrival("dv%d" % d, -1 - d, [1 + d])]
         if t == 0:
-            ts(COL[:, 8 + d:9 + d], T.DVL[:, o + 6:o + 7], 8.0, T.DVL[:, o + 7:o + 8], ALU.mult, ALU.add, [], ["T%d" % d],
-               [arrival("da%d" % d, -1 - d, [1, 2])], 1)
-            t1(COL[:, 10 + d:11 + d], COL[:, 8 + d:9 + d], 129.0 * 64, ALU.mult, ["T%d" % d], ["TB%d" % d], n=1)
+            cp(fmsg(d, 0, 256, 257), T.DVL[:, o + 7:o + 8], [], ["TP%d" % d], ext, 1)
+            tmat(d)
         o += 8 + 128 * t
-        a, b, c = (sl(PB[7], d), ps(7, d)), (sl(PB[7], 2 + d), ps(7, 2 + d)), (sl(PB[6], d), ps(6, d))
-        mm(a[0], [(T.BB[:], xs[d])], ["BB", "X%d" % d], [a[1]], xext(d))
-        act(sl(T.TQ, d), a[0], ACT.Identity, [a[1]], ["TQ%d" % d], bias=MAGIC, scale=1.0 / 64)
-        mm(b[0], [(T.BB[:], xs[d]), (T.IDN64[:], sl(T.TQ, d))], ["BB", "X%d" % d, "IDN64", "TQ%d" % d], [b[1]])
-        act(sl(T.TS, d), b[0], ACT.Identity, [b[1], "T%d" % d, "TB%d" % d], ["TS%d" % d],
-            bias=COL[:, 10 + d:11 + d], scale=COL[:, 8 + d:9 + d])
-        mm(c[0], [(T.ID[:], xs[d]), (T.IDN[:], T.DVL[:, o:o + 128])], ["ID", "IDN", "X%d" % d], [c[1]],
-           xext(d) + [arrival(("db%d" if t else "da%d") % d, -1 - d, [1, 2])])
-        act(sl(T.ZZ, d), c[0], ACT.Abs, [c[1]], ["ZZ%d" % d])
+        mm(a, [(T.BB[:], x)], ["BB", xn], [an], xext(d))
+        act(sl(T.TQ, d), a, ACT.Identity, [an], ["TQ%d" % d], bias=MAGIC, scale=1.0 / 64)
+        mm(e, [(T.BB[:], x), (T.IDN64[:], sl(T.TQ, d))], ["BB", xn, "IDN64", "TQ%d" % d], [en])
+        mm(c, [(ID[:], x), (T.IDN[:], T.DVL[:, o:o + 128])], ["ID", "IDN", xn], [cn], xext(d) + ext)
+        act(m, e, ACT.Identity, [en], ["SM%d%d" % (d, t)], bias=129.0 * 64)
+        act(sl(T.ZZ, d), c, ACT.Abs, [cn], ["ZZ%d" % d])
         act(sl(T.AZ, d), sl(T.ZZ, d), ACT.Abs, ["ZZ%d" % d], ["AZ%d" % d], bias=tgc[d], scale=-1.0)
-        mm(a[0], [(T.ID[:], sl(T.ZZ, d)), (T.IDN[:], xs[d])], ["ID", "IDN", "ZZ%d" % d, "X%d" % d], [a[1]])
-        mm(c[0], [(T.BN[:], sl(T.AX, d)), (T.BB[:], sl(T.AZ, d))], ["BB", "BN", "AZ%d" % d, "AX%d" % d], [c[1]])
-        tt(sl(T.OKZ, d), c[0], sl(T.TS, d), ALU.is_le, [c[1], "TS%d" % d], ["OKZ%d" % d])
-        tt(sl(T.MZ, d), a[0], sl(T.OKZ, d), ALU.mult, [a[1], "OKZ%d" % d], ["MZ%d" % d])
+        mm(a, [(ID[:], sl(T.ZZ, d)), (T.IDN[:], x)], ["ID", "IDN", "ZZ%d" % d, xn], [an])
+        mm(c, [(T.BN[:], sl(T.AX, d)), (sl(T.BT, d), m), (T.BB[:], sl(T.AZ, d))],
+           ["BB", "BN", "AX%d" % d, "AZ%d" % d, "BT%d" % d, "SM%d%d" % (d, t)], [cn])
+        t1(sl(T.OKZ, d), c, 0.0, ALU.is_le, [cn], ["OKZ%d" % d])
+        tt(fmsg(d, t, 0, 128), a, sl(T.OKZ, d), ALU.mult, [an, "OKZ%d" % d], ["MZ%d%d" % (d, t)])
+
+    def tell(d, t):
+        n = 256 if t else 257
+        send([(1 - 2 * d, fmsg(d, t, 0, n), fmsg(1 - d, t, 0, n), "fa%d_%d" % (1 - d, t))], 2 * n,
+             ["MZ%d%d" % (d, t), "SM%d%d" % (d, t), "TP%d" % d])
 
     def job(d, t):
         second = 0 if d == E else 1
         b = 2 + second
-        blocks = BLOCKS[second]
-        win = T.H1[:, :] if t == 0 else T.H2[:, :]
-        o = 0
-        for k, n in enumerate(blocks):
+        win = T.H2[:, :] if t else T.H1[:, :]
+        o, ys, ms = 0, ["BOFF%d" % d], ["BOFF%d" % d]
+        for k, n in enumerate(BLOCKS[second]):
             src = win.indirect(T.OFF[:, 128 * d + o // 16:128 * d + (o + n) // 16])
-            r, w, x = ["OFF%d" % d] + (hall if t else []), ["Y%d_%d" % (d, k)], [("h1a", 16), ("h1b", 16)]
-            if (second, k) in ONV:
-                cp(YY[d][:, o:o + n], src, r, w, x, n * GAT)
+            r, w, ex = ["OFF%d" % d, "H"], ["Y%d_%d" % (d, k)], [("h1a", 16), ("h1b", 16)]
+            if (second, k) in ONV[role]:
+                cp(YY[d][:, o:o + n], src, r, w, ex, 50 + n * GAT)
             else:
-                act(YY[d][:, o:o + n], src, ACT.Copy, r, w, x, n=n * GAT)
+                act(YY[d][:, o:o + n], src, ACT.Copy, r, w, ex, n=65 + n * GAT)
                 ops[-1]["line"] = "Y"
             ops[-1]["pen"] = PEN
-            tt(MM[d][:, o:o + n], YY[d][:, o:o + n], PB[d][:, 0:n], ALU.max, w + [ps(d, s) for s in range(4)],
-               ["M%d_%d" % (d, k)], n=n)
-            ops[-1]["pen"] = PEN
-            mms([(PB[b][:, 15 - pos:128:16], [(sl(YY[d], pos), T.BS[:, 16:24]), (sl(MM[d], pos), T.BS[:, 8:16])])
-                 for pos in range(o // 128, (o + n) // 128)], w + ["M%d_%d" % (d, k), "BSP", "BSN"], [ps(b, 0)], n)
+            ys += w
+            for u in range(o, o + n, XR):
+                m = "M%d_%d" % (d, u // XR)
+                ms.append(m)
+                tt(MM[d][:, u:u + XR], YY[d][:, u:u + XR], PB[d][:, 0:XR], ALU.max, w + [ps(d, s) for s in range(XR // 128)],
+                   [m], n=XR)
+                ops[-1]["pen"] = PEN
+                mms([(PB[b][:, 15 - pos:128:16], [(sl(YY[d], pos), T.BS[:, 16:24]), (sl(MM[d], pos), T.BS[:, 8:16])])
+                     for pos in range(u // 128, (u + XR) // 128)], w + [m, "BSP", "BSN"], [ps(b, 0)], XR)
             o += n
-        ys = ["Y%d_%d" % (d, k) for k in range(len(blocks))] + ["BOFF%d" % d]
-        ms = ["M%d_%d" % (d, k) for k in range(len(blocks))] + ["BOFF%d" % d]
-        off = T.BOFF[:, 8 * d:8 * d + 8]
-        o = 384 * t
-        key = KK[d][:, o + 128 * d:o + 128 * d + 128]
+        off, o = sl(T.BOFF, d, 8), 128 * d
+        key, mark = sl(KK[d], 3 * t + d), len(ops)
+        (cm, cn), (df, dfn), (kd, kn) = slot(4 + d, 2), slot(b, 3), slot(d, 3)
+        x, mz, r = xs(d), fmsg(d, t, 0, 128), ["ID", "IDN", "X%d" % d, "MZ%d%d" % (d, t), "YB%d" % d]
+        mm(cm, [(T.BN[:], sl(T.AX, d)), (sl(T.BT, d), fmsg(d, t, 128, 256))], ["BN", "AX%d" % d, "BT%d" % d, "SM%d%d" % (d, t)],
+           [cn], fext(d, t), stop=False)
         scan(sl(T.S1, d), T.D0[:], PB[b][:, 0:128], 0.0, ALU.add, ALU.max, ["D0", ps(b, 0)], ["S1%d" % d])
-        mms([(PB[d][0:8, a:128:16], [(T.IDF[:, a:128:16], T.S1[:, 128 * d + 15:128 * d + 128:16])]) for a in range(16)],
-            ["IDF", "S1%d" % d], [ps(d, 0)], 512)
-        tt(T.TT[0:8, 128 * d:128 * d + 128], PB[d][0:8, 0:128], T.CT[0:8, :], ALU.add, [ps(d, 0), "CT"], ["TT%d" % d])
-        mms([(PB[b][:, 0:8], [(T.TT[0:8, 128 * d:128 * d + 128], T.IDF[0:8, 0:8])])], ["TT%d" % d, "IDF"], [ps(b, 0)], 256)
-        cp(T.BI[:, 16 * d:16 * d + 8], PB[b][:, 0:8], [ps(b, 0)], ["BIa%d" % d], n=8)
-        t1(T.BI[:, 16 * d + 8:16 * d + 16], T.BI[:, 16 * d:16 * d + 8], 2047, ALU.bitwise_and, ["BIa%d" % d], ["BIb%d" % d], n=8)
-        cp(off, T.BI[:, 16 * d + 8:16 * d + 16], ["BIb%d" % d], ["BOFF%d" % d], n=8)
-        act(sl(T.AY, d), YY[d][:, :].indirect(off), ACT.Abs, ys, ["AY%d" % d], xext(d), tgc[d], -1.0, 128 * GAT)
-        cp(sl(T.YB, d), YY[d][:, :].indirect(off), ys, ["YB%d" % d], n=128 * GAT)
-        mm(sl(PB[d], 1), [(T.BN[:], sl(T.AX, d)), (T.BB[:], sl(T.AY, d))], ["BB", "BN", "AX%d" % d, "AY%d" % d], [ps(d, 1)])
-        act(sl(T.MB, d), MM[d][:, :].indirect(off), ACT.Copy, ms, ["MB%d" % d], n=128 * GAT)
-        mm(sl(PB[b], 1), [(T.IDN[:], xs[d]), (T.IDN[:], sl(T.MZ, d)), (T.ID[:], sl(T.YB, d))],
-           ["ID", "IDN", "X%d" % d, "MZ%d" % d, "YB%d" % d], [ps(b, 1)])
-        terms = [(T.ID[:], xs[d]), (T.ID[:], sl(T.MZ, d)), (T.BN512[:], sl(T.YB, d)), (T.B1024[:], sl(T.MB, d))]
-        if d == 0:
-            terms = [(T.BB[:], T.C16[:])] + terms
-        mm(sl(PB[7], 2 + d), terms, ["ID", "BB", "C16", "X%d" % d, "MZ%d" % d, "YB%d" % d, "MB%d" % d, "BN512", "B1024"],
-           [ps(7, 2 + d)])
-        tt(sl(T.OKY, d), sl(PB[d], 1), sl(T.TS, d), ALU.is_le, [ps(d, 1), "TS%d" % d], ["OKY%d" % d])
-        tt(sl(T.MY, d), sl(PB[b], 1), sl(T.OKY, d), ALU.mult, [ps(b, 1), "OKY%d" % d], ["MY%d" % d])
-        tt(key, sl(PB[7], 2 + d), sl(T.MY, d), ALU.add, [ps(7, 2 + d), "MY%d" % d], ["key%d_%d" % (d, t)])
+        last = T.S1[:, o + 15:o + 128:16]
+        ts(sl(T.RR, d, 8), last, R2048, R2048, ALU.add, ALU.subtract, ["S1%d" % d], ["RR%d" % d], n=8)
+        tt(sl(T.IX, d, 8), last, sl(T.RR, d, 8), ALU.subtract, ["S1%d" % d, "RR%d" % d], ["IX%d" % d], n=16)
+        mms([(PB[d][0:8, a:128:16], [(T.ID2[:, a:128:16], sl(T.IX, d, 8))]) for a in range(16)],
+            ["ID2", "IX%d" % d], [ps(d, 0)], 128)
+        if TURN[second] == "s":
+            act(T.TT[0:8, o:o + 128], PB[d][0:8, 0:128], ACT.Identity, [ps(d, 0), "c7"], ["TT%d" % d], bias=COL[0:8, 7:8])
+        else:
+            t1(T.TT[0:8, o:o + 128], PB[d][0:8, 0:128], COL[0:8, 7:8], ALU.add, [ps(d, 0), "c7"], ["TT%d" % d])
+        mm(PB[b][:, 0:8], [(T.TT[0:8, o:o + 128], ID[0:8, 0:8])], ["TT%d" % d, "ID"], [ps(b, 0)], n=64)
+        t1(off, PB[b][:, 0:8], col(2), ALU.add, [ps(b, 0), "c2"], ["BOFF%d" % d], n=8)
+        act(sl(T.AY, d), YY[d][:, :].indirect(off), ACT.Abs, ys, ["AY%d" % d], xext(d), tgc[d], -1.0, 65 + 128 * GAT)
+        cp(sl(T.YB, d), YY[d][:, :].indirect(off), ys, ["YB%d" % d], n=50 + 128 * GAT)
+        if BEST[second] == "s":
+            act(sl(T.MB, d), MM[d][:, :].indirect(off), ACT.Copy, ms, ["MB%d" % d], n=65 + 128 * GAT)
+        else:
+            cp(sl(T.MB, d), MM[d][:, :].indirect(off), ms, ["MB%d" % d], n=50 + 128 * GAT)
+        mm(cm, [(T.BB[:], sl(T.AY, d))], ["BB", "AY%d" % d], [cn], start=False)
+        mm(df, [(T.IDN[:], x), (T.IDN[:], mz), (ID[:], sl(T.YB, d))], r, [dfn], fext(d, t))
+        mm(kd, [(T.BB[:], T.C16[:])][d:] + [(ID[:], x), (ID[:], mz), (T.BN512[:], sl(T.YB, d)), (T.B1024[:], sl(T.MB, d))],
+           r + ["BB", "C16", "BN512", "B1024", "MB%d" % d], [kn], fext(d, t))
+        t1(sl(T.OKY, d), cm, 0.0, ALU.is_le, [cn], ["OKY%d" % d])
+        tt(sl(T.MY, d), df, sl(T.OKY, d), ALU.mult, [dfn, "OKY%d" % d], ["MY%d" % d])
+        tt(key, kd, sl(T.MY, d), ALU.add, [kn, "MY%d" % d], ["key%d_%d" % (d, t)])
+        for a in ops[mark:]:
+            a["pen"] = -BOOST[second]
         land = {(0, 1): (1, "ka1"), (0, -1): (2, "ka2"), (1, -1): (0, "kb0"), (1, -2): (2, "kb2")}
-        items = []
-        for k in key_offs(d, t):
-            slot, sem = land[(d, k)]
-            items.append((k, key, KK[d][:, o + 128 * slot:o + 128 * slot + 128], "%s_%d" % (sem, t)))
-        send(items, 512, ["key%d_%d" % (d, t)])
+        send([(k, key, sl(KK[d], 3 * t + land[d, k][0]), "%s_%d" % (land[d, k][1], t)) for k in key_offs(d, t)], 512,
+             ["key%d_%d" % (d, t)])
 
-    POS, last = sl(PB[3], 2), PB[3][:, 383:384]
+    POS, last = sl(PB[7], 1), PB[7][:, 255:256]
 
     def own(t):
-        finish(2, t - 1, (0, 3, 3))
+        finish(2, t - 1)
         ring(2)
-        scan(POS, T.ONE[:], sl(T.EQ, 2), COL[:, 11 + t:12 + t], ALU.mult, ALU.add, ["ONE", "EQ2", "nm%d" % (t - 1)], ["#32"])
+        scan(POS, T.ONE[:], sl(T.EQ, 2), col(11 + t), ALU.mult, ALU.add, ["ONE", "EQ2", "nm%d" % (t - 1)], ["#71"])
+
+    def append(t):
+        ts(sl(T.RN, t, 8), T.BS[:, 0:8], last, 128.0, ALU.mult, ALU.min, ["BS0", "#71"], ["RN%d" % t], n=8)
+        tt(T.VV[:], sl(T.EQ, 2), POS, ALU.mult, ["EQ2", "#71"], ["VV"])
+        t1(col(12 + t), last, 128.0, ALU.min, ["#71"], ["nm%d" % t], n=1)
+        mm(sl(PB[7], 2), [(T.IDBIG[:], T.MA[:]), (T.BK[:], sl(T.EQ, 2)), (T.BB[:], T.VV[:])],
+           ["IDBIG", "MA", "BK", "EQ2", "BB", "VV"], ["#72"])
+        scan(T.SC2[:], T.RS[:], sl(PB[7], 2), 0.0, ALU.mult, ALU.max, ["RS", "#72"], ["SC2"])
+        t1(T.SOFF[:], T.SC2[:, 15:128:16], 255.0 - 16384.0, ALU.add, ["SC2"], ["SOFF"], n=8)
+        cp(T.H2[:, :].indirect(T.SOFF[:, 0:8]), xs(2), ["SOFF", "X2"], ["H"], [("h2", 256)], 50 + 128 * SCA)
 
     for t in range(STEPS):
         for d in (E, Z):
             if t:
-                finish(d, t - 1, (d, d, 2))
+                finish(d, t - 1)
             ring(d)
             hashes(d, t)
             xrep(d)
-            fallback(d, t)
-            counts(d, t, 1 if t else 0, 2)
+            if role == 0:
+                fallback(d, t)
+            elif t == 0:
+                tmat(d)
         if t:
             own(t)
-            ts(T.RN[:, 16 * t:16 * t + 8], T.BS[:, 0:8], last, 128.0, ALU.mult, ALU.min, ["BS0", "#32"], ["RNn%d" % t], n=8)
-            tt(T.VV[:], sl(T.EQ, 2), POS, ALU.mult, ["EQ2", "#32"], ["VV"])
-            t1(COL[:, 12 + t:13 + t], last, 128.0, ALU.min, ["#32"], ["nm%d" % t], n=1)
-            mm(sl(PB[3], 1), [(T.IDBIG[:], T.MA[:]), (T.BK[:], sl(T.EQ, 2)), (T.BB[:], T.VV[:])],
-               ["IDBIG", "MA", "BK", "EQ2", "BB", "VV"], ["#31"])
-            scan(T.SC2[:], T.RS[:], sl(PB[3], 1), 0.0, ALU.mult, ALU.max, ["RS", "#31"], ["SC2"])
-            t1(T.SOFF[:], T.SC2[:, 15:128:16], 255.0 - 16384.0, ALU.add, ["SC2"], ["SOFF"], n=8)
-            cp(T.H2[:, :].indirect(T.SOFF[:, 0:8]), xs[2], ["SOFF", "X2"], hall, [("h2", 16 * BYDMA)], 128 * SCA)
-            counts(E, t, 0, 1)
-            counts(Z, t, 0, 1)
+            append(t)
         for d in (E, Z):
-            places(d)
+            places(d, t)
+        for d in (E, Z):
+            for k in ((d,) if t else (E, Z) if d == E else ()) if role == 0 else ():
+                tell(k, t)
             job(d, t)
 
     own(STEPS)
-    dma("y", T.yx[:], xs[2], "out0", r=["X2"], tail=2.5)
-    ts(T.YN[:, 0:1], last, 128.0, 256.0, ALU.min, ALU.add, ["#32"], ["YN"], n=1)
+    dma("y", T.yx[:], xs(2), "out0", r=["X2"], tail=2.5)
+    ts(T.YN[:, 0:1], last, 128.0, 256.0, ALU.min, ALU.add, ["#71"], ["YN"], n=1)
     dma("y", T.yn[:], T.YN[:, 0:1], "out1", r=["YN"], tail=2.3)
     return ops, sent[0]
 

@@ -5,31 +5,35 @@ NR = 8
 STEPS = 3
 RING = 320
 WIDE = 512
-BLOCKS = [[512, 512, 512, 512], [512, 512, 512, 256, 256]]
-ONV = [[(0, 1)], [(0, 1)]]
+BLOCKS = [[256, 256, 512, 512, 512], [512, 512, 512, 384, 128]]
+ONV = [[(0, 0), (0, 2)], [(0, 1), (0, 3)]]
 XR = 256
-WRAP = "asss"
-TURN = "sv"
-BEST = "vv"
+WRAP = "aass"
+TURN = "zz"
+BEST = "ss"
 MAGIC = 128.5078125
-R64, R2048 = 1.5 * 2 ** 29, 1.5 * 2 ** 34
+R64 = 1.5 * 2 ** 29
+EPS = 2.0 ** -13
 HEAD = 2048
 FW = 272
-CY, OVH, WAKE, SELF, GAT, SCA, PEC, HOP, ROW, RATE, CALL = 0.0009, 0.01, 0.22, 0.2, 1.45, 3.8, 0.00045, 0.6, 0.03, 30e3, 0.3
-AT = {"ld0": 2.4, "ldt": 2.8, "ldc": 3.2, "go": 4.0, "h1a": 5.0, "h1b": 9.8, "ldv": 6.0, "h2": 16.0}
-LOOK, TOL, BETA, PEN, BOOST = 0.4, 0.03, 0.3, 0.5, (4.0, 1.0)
+CY, OVH, WAKE, SELF, GAT, SCA, PEC, HOP, ROW, RATE, CALL = 0.00095, 0.01, 0.21, 0.2, 1.5, 3.8, 0.00045, 1.0, 0.025, 30e3, 0.3
+AT = {"ld0": 2.4, "ldt": 2.8, "ldc": 3.2, "go": 4.0, "h1a": 5.0, "h1b": 8.5, "ldv": 6.0, "h2": 16.0}
+LOOK, TOL, BETA, PEN, BOOST = 0.1, 0.05, 0.3, 0.5, (0.0, 0.0)
+ROUNDS, NUDGE = 0, 0.3
+MARGIN = 2.0
 
 SCRATCH = {}
 for _dt, _bufs in (
     ("bfloat16", dict(H1=16 * RING, H2=16 * WIDE, IN0=144, X=416, DVS=392, DVL=784, ID=128, IDN=128, ID2=128, IDN64=128,
                       IDBIG=128, IDW=128, BB=128, BN=128, B1024=128, BN512=128, BK=128, BR=128, BRN=128, BR2=128, CK=128, C16=128,
-                      TG=128, MA=128, ONE=128, RB=128, BS=24, RNB=16, RN=8 * STEPS, AX=384, EQ=384, VV=128, T2N=256, TQ=256,
-                      ZZ=256, AZ=256, OKZ=256, BT=256, SB=256, IX=16, TT=256, Y0=2048, Y1=2048, M0=2048, M1=2048, YB=256,
-                      AY=256, MB=256, OKY=256, MY=256, FB=2 * FW * STEPS)),
-    ("float16", dict(T2=256, RF=128, RG=128)),
+                      TG=128, MA=128, ONE=128, RB=128, BS=24, CB=8, RNB=16, RN=8 * STEPS, AX=384, EQ=384, VV=128, T2N=256,
+                      TQ=256, ZZ=256, AZ=256, OKZ=256, BT=256, SB=256, ZW=288, TT=256, Y0=2048, Y1=2048, M0=2048, M1=2048,
+                      YB=256, AY=256, MB=256, OKY=256, MY=256, FB=2 * FW * STEPS)),
+    ("float16", dict(T2=256, RF=128, RG=128, IH=128, PL=256)),
     ("int32", dict(CNI=4, TEI=4, TE2=4, PI=4, KI=128, RI=128, CI=128, TI1=128, TI2=128, TI3=128, TI4=128, PP=256, HI=256,
-                   AI=256, PL=256, MI=384, XI=384)),
-    ("float32", dict(COL=16, RS=128, D0=128, SC2=128, SQ=256, S1=256, RR=16, YN=4, KA=384 * STEPS, KB=384 * STEPS)),
+                   MI=384, XI=384)),
+    ("float32", dict(COL=16, RS=128, D0=128, D1=128, CAP=128, SC2=128, SQ=256, AI=256, S1=256, S2=256, YN=128, KA=384 * STEPS,
+                     KB=384 * STEPS)),
     ("uint16", dict(SOFF=8, OFF=256, BOFF=16)),
 ):
     for _n, _c in _bufs.items():
@@ -37,10 +41,10 @@ for _dt, _bufs in (
 for _b in range(8):
     SCRATCH["PB%d" % _b] = ("psum", [128, 512], "float32")
 
-SEMAPHORES = ["qv", "qs", "qp", "qg", "ld0", "ldv", "ldt", "ldc", "h1a", "h1b", "h2", "go", "sent", "xa0", "xa1", "dv0", "dv1",
+SEMAPHORES = ["qv", "qs", "qp", "qg", "ld0", "ldv", "ldt", "ldc", "h1a", "h1b", "h2", "go", "sent", "xa0", "xa1", "dv0",
               "out0", "out1"]
 for _t in range(STEPS):
-    SEMAPHORES += [_n + "_%d" % _t for _n in ("ka1", "ka2", "kb0", "kb2", "fa0", "fa1")]
+    SEMAPHORES += [_n + "_%d" % _t for _n in ("ka1", "ka2", "kb0", "kb2", "fa1")]
 
 
 def banks(o):
@@ -102,54 +106,73 @@ def schedule(progs):
     for k, p in enumerate(pred):
         for d in p:
             succ[d].append(k)
-    left = [len(p) for p in pred]
-    ready, free, bank, end, late, order = {}, {}, {}, {}, {}, [[] for _ in progs]
-    for k, (role, o) in enumerate(ops):
-        if not left[k]:
-            ready.setdefault((role, o["e"]), []).append(k)
+    bk = [banks(o) for role, o in ops]
 
-    def start(k):
-        role, o = ops[k]
-        t = max([base[k], free.get((role, o["e"]), 0.0)]
-                + [end[d] + lat + late.get(d, 0.0) * (lat > HOP) for d, lat in pred[k].items()])
-        for b in banks(o):
-            for e2, t2 in bank.get((role, b), {}).items():
-                if e2 != o["e"]:
-                    t = max(t, t2 + WAKE)
-        return t
-
-    while True:
-        pick = None
-        for q, cand in ready.items():
-            if cand:
-                st = {k: start(k) for k in cand}
-                t0 = min(st.values())
-                if pick is None or t0 < pick[0]:
-                    pick = (t0, q, st)
-        if pick is None:
-            return order
-        t0, q, st = pick
-        top = max((k for k in st if st[k] <= t0 + LOOK), key=lambda k: (prio[k], -k))
-        if st[top] > t0 + 0.02:
-            fit = [k for k in st if st[k] + ops[k][1]["c"] <= st[top] + TOL]
-            now = max((k for k in st if st[k] <= t0 + 0.02), key=lambda k: (prio[k], -k))
-            if fit:
-                top = max(fit, key=lambda k: (prio[k], -k))
-            elif st[top] - t0 >= BETA * ops[now][1]["c"]:
-                top = now
-        role, o = ops[top]
-        end[top] = free[q] = st[top] + o["c"]
-        if o["out"]:
-            late[top] = max(0.0, free.get((role, "d"), 0.0) - end[top])
-            free[role, "d"] = end[top] + late[top] + max(rows for s, lat, rows in o["out"])
-        for b in banks(o):
-            bank.setdefault((role, b), {})[o["e"]] = end[top]
-        ready[q].remove(top)
-        order[role].append(o)
-        for k in succ[top]:
-            left[k] -= 1
+    def one_round():
+        left = [len(p) for p in pred]
+        ready, free, bank, end, late, held, order = {}, {}, {}, {}, {}, {}, [[] for _ in progs]
+        for k, (role, o) in enumerate(ops):
             if not left[k]:
-                ready.setdefault((ops[k][0], ops[k][1]["e"]), []).append(k)
+                ready.setdefault((role, o["e"]), []).append(k)
+
+        def start(k):
+            role, o = ops[k]
+            t = [(base[k], -1), free.get((role, o["e"]), (0.0, -1))]
+            t += [(end[d] + lat + late.get(d, 0.0) * (lat > HOP), d) for d, lat in pred[k].items()]
+            t += [(t2 + WAKE, d) for b in bk[k] for e2, (t2, d) in bank.get((role, b), {}).items() if e2 != o["e"]]
+            return max(t)
+
+        while True:
+            pick = None
+            for q, cand in ready.items():
+                if cand:
+                    st = {k: start(k)[0] for k in cand}
+                    t0 = min(st.values())
+                    if pick is None or t0 < pick[0]:
+                        pick = (t0, q, st)
+            if pick is None:
+                break
+            t0, q, st = pick
+            top = max((k for k in st if st[k] <= t0 + LOOK), key=lambda k: (prio[k], -k))
+            if st[top] > t0 + 0.02:
+                fit = [k for k in st if st[k] + ops[k][1]["c"] <= st[top] + TOL]
+                now = max((k for k in st if st[k] <= t0 + 0.02), key=lambda k: (prio[k], -k))
+                if fit:
+                    top = max(fit, key=lambda k: (prio[k], -k))
+                elif st[top] - t0 >= BETA * ops[now][1]["c"]:
+                    top = now
+            role, o = ops[top]
+            held[top] = start(top)[1]
+            end[top] = st[top] + o["c"]
+            free[q] = (end[top], top)
+            if o["out"]:
+                late[top] = max(0.0, free.get((role, "d"), 0.0) - end[top])
+                free[role, "d"] = end[top] + late[top] + max(rows for s, lat, rows in o["out"])
+            for b in bk[top]:
+                bank.setdefault((role, b), {})[o["e"]] = (end[top], top)
+            ready[q].remove(top)
+            order[role].append(o)
+            for k in succ[top]:
+                left[k] -= 1
+                if not left[k]:
+                    ready.setdefault((ops[k][0], ops[k][1]["e"]), []).append(k)
+        span, k = max((end[k] + o["tail"], k) for k, (role, o) in enumerate(ops) if o["tail"] < 99)
+        return span, order, k, held
+
+    best = None
+    for n in range(ROUNDS + 1):
+        span, order, k, held = one_round()
+        if best is None or span < best[0]:
+            best = (span, order)
+        waits = []
+        while held[k] >= 0:
+            if held[k] not in pred[k]:
+                waits.append((k, held[k]))
+            k = held[k]
+        for k, d in waits[n % 3::3]:
+            prio[k] += NUDGE
+            prio[d] -= NUDGE
+    return best[1]
 
 
 def emit(g, T, ops):
@@ -339,7 +362,7 @@ def program(T, topo, rank):
         return T.FB[:, o + lo:o + hi]
 
     def fext(d, t):
-        return [arrival("fa%d_%d" % (d, t), 1 - 2 * d, [2 * d - 1])] if role else []
+        return [arrival("fa1_%d" % t, -1, [1])] if d else []
 
     dma("y", T.IN0[:, 8:136], T.x0[:], "ld0")
     dma("s", T.IN0[:, 7:8], T.tg[:], "ld0", tail=999.0)
@@ -364,8 +387,7 @@ def program(T, topo, rank):
     t1(T.TE2[:, 0:1], T.TEI[:, 0:1], col(2), ALU.add, ["c2"], ["TE20"], [("ldt", 16)], 1)
     t1(T.TE2[:, 1:2], T.TE2[:, 0:1], 4, ALU.arith_shift_right, ["TE20"], ["TE21"], n=1)
     cp(T.DVS[:, 7:8], T.TE2[:, 1:2], ["TE21"], ["DVS"], n=1)
-    send([(2 - role, T.DVS[:, 7:392], T.DVL[:, 399 - 392 * role:784 - 392 * role], "dv%d" % (1 - role))], 770, ["DVS"],
-         [("ldv", 16)])
+    send([(1, T.DVS[:, 7:392], T.DVL[:, 7:392], "dv0")], 770, ["DVS"], [("ldv", 16)])
     for k, src, v, o in ((4, 0, 8.0, ALU.is_lt), (5, 0, 32.0, ALU.is_ge), (6, 2, float(WIDE), ALU.mult), (7, 0, 16.0, ALU.mult)):
         t1(col(k), T.PI[:, src:src + 1], v, o, ["PI%d" % src], ["c%d" % k], n=1)
     ts(col(11), col(2), 15.0, col(2), ALU.is_lt, ALU.mult, ["c2"], ["c11"], n=1)
@@ -381,19 +403,22 @@ def program(T, topo, rank):
     cp(T.RF[64:65, :], T.CI[64:65, :], ["CI"], ["RF"])
     fill(T.RF[96:97, :], 1.0, ["RF"])
     ts(T.RG[:], T.RI[:], 0.0, col(5), ALU.is_equal, ALU.mult, ["RI", "c5"], ["RG"])
-    t1(T.RB[:], T.RI[:], 0.0, ALU.is_equal, ["RI"], ["RB"])
+    ts(T.RB[:], T.RI[:], 0.0, 2.0 ** -12, ALU.is_equal, ALU.mult, ["RI"], ["RB"])
     cp(T.BS[:, 0:8], T.BB[:, 0:128:16], ["BB"], ["BS0"], n=8)
     fill(T.ONE[:], 1.0, ["ONE"])
+    fill(T.ZW[:], 0.0, ["IX0", "IX1"])
+    fill(T.CAP[:], 384.0, ["CAP"])
     for d in (0, 1):
-        t1(sl(T.T2, d), T.ONE[:], 0.0, ALU.mult, ["ONE"], ["T2S%d" % d, "T2B%d" % d, "T2C%d" % d], n=64)
+        t1(sl(T.T2, d), T.ONE[:], 0.0, ALU.mult, ["ONE"], ["T2S%d" % d, "T2B%d" % d, "T2C%d" % d, "T2D%d" % d], n=64)
         cp(T.T2[64:65, 128 * d:128 * d + 128], T.ONE[64:65, :], ["ONE"], ["T2C%d" % d], n=64)
-        t1(T.T2[96:97, 128 * d:128 * d + 128], T.TI3[96:97, :], 5.0, ALU.mult, ["TI3"], ["T2C%d" % d])
+        t1(T.T2[96:97, 128 * d:128 * d + 128], T.TI3[96:97, :], 5.0, ALU.mult, ["TI3"], ["T2D%d" % d])
         fill(PB[4 + d][0:32, 0:128], 0.0, [ps(4 + d, 0)])
     fill(T.T2N[:], 256.0, ["T2N0", "T2N1"])
     t1(T.BS[:, 8:16], T.BS[:, 0:8], 4096.0, ALU.mult, ["BS0"], ["BSP"], n=8)
     t1(T.BS[:, 16:24], T.BS[:, 0:8], -2048.0, ALU.mult, ["BS0"], ["BSN"], n=8)
     for k, v in enumerate((RING, WIDE)):
-        ts(sl(T.RNB, k, 8), T.BS[:, 0:8], col(2), float(v), ALU.mult, ALU.mult, ["BS0", "c2"], ["RNB"], n=8)
+        ts(sl(T.RNB, k, 8), T.BS[:, 0:8], col(2), float(v), ALU.mult, ALU.mult, ["BS0", "c2"], ["RNB%d" % k], n=8)
+    t1(T.CB[:], T.KI[:, 0:8], 0.125, ALU.mult, ["KI"], ["CB"], n=8)
     ts(T.CK[:], T.TI3[:], 15.0, -15.5 / 128, ALU.is_equal, ALU.mult, ["TI3"], ["CK"])
     t1(T.CK[:], T.CK[:], -31.5 / 128, ALU.add, ["CK"], ["CK"], n=64)
     cp(T.BR[:], T.BB[:], ["BB"], ["BR"], n=64)
@@ -401,11 +426,13 @@ def program(T, topo, rank):
     fill(T.C16[:], 16.0, ["C16"])
     t1(T.TG[:], T.ONE[:], tgc[2], ALU.mult, ["ONE"], ["TG"], xext(2), 64)
     mats = [("IDN", "ID", -1.0), ("IDW", "ID", -2048.0), ("ID2", "ID", 2.0), ("BN", "BB", -1.0), ("B1024", "BB", 1024.0),
-            ("BN512", "BB", -512.0), ("IDBIG", "ID", 16384.0), ("BRN", "BR", -1.0), ("BR2", "BR", 2.0), ("IDN64", "ID", -64.0)]
-    for buf, src, v in mats[:len(mats) - role]:
+            ("BN512", "BB", -512.0), ("IDBIG", "ID", 16384.0), ("BRN", "BR", -1.0), ("BR2", "BR", 2.0), ("IH", "ID", 1.0),
+            ("IDN64", "ID", -64.0)]
+    for buf, src, v in mats:
         t1(T[buf][:], T[src][:], v, ALU.mult, [src], [buf], n=64)
     t1(T.RS[:], T.TI3[:], 0.0, ALU.is_gt, ["TI3"], ["RS"])
     ts(T.D0[:], T.RS[:], float(2 ** 25 + 64), -float(2 ** 25), ALU.mult, ALU.add, ["RS"], ["D0"])
+    ts(T.D1[:], T.RS[:], float(2 ** 25), -float(2 ** 25), ALU.mult, ALU.add, ["RS"], ["D1"])
     t1(col(12), T.CNI[:, 0:1], -256.0, ALU.add, [], ["nm0"], [("ldc", 16)], 1)
     t1(T.TI4[:], T.TI1[:], 15, ALU.bitwise_and, ["TI1"], ["TI4"])
     t1(T.RN[:, 0:8], T.BS[:, 0:8], col(12), ALU.mult, ["BS0", "nm0"], ["RN0"], n=8)
@@ -427,7 +454,7 @@ def program(T, topo, rank):
         u, un = slot(6, 0) if d == 2 else slot(4 + d, 2)
         if d == 2:
             mm(u, [(T.CK[:], T.ONE[:]), (T.BRN[:], T.TG[:])], ["CK", "ONE", "BRN", "TG"], [un], stop=False)
-            t1(sl(T.AX, d), xs(d), tgc[d], ALU.max, ["X2"], ["AX2"], n=64)
+            t1(sl(T.AX, d), sl(T.XI, d), tgc[d], ALU.max, ["XI2"], ["AX2"])
             mm(u, [(T.BRN[:], xs(d)), (T.BR2[:], sl(T.AX, d))], ["BRN", "BR2", "X2", "AX2"], [un], start=False)
         else:
             act(sl(T.AX, d), xs(d), ACT.Abs, ["X%d" % d], ["AX%d" % d], xext(d), tgc[d], -1.0)
@@ -442,14 +469,14 @@ def program(T, topo, rank):
         if t == 0:
             t1(T.T2[0:8, o:o + 128], a0[0:8, 0:128], -2048.0, ALU.add, [n0], ["T2S%d" % d])
         mms([(a0[32:40, a:128:16], [(T.EQ[:, o + a:o + 128:16], sl(T.RNB, min(t, 1), 8))]) for a in range(16)],
-            ["EQ%d" % d, "RNB"], [n0], 128)
+            ["EQ%d" % d, "RNB%d" % min(t, 1)], [n0], 128)
         if t == 0:
             cp(T.T2[32:40, o:o + 128], a0[32:40, 0:128], [n0], ["T2B%d" % d])
         else:
             t1(T.T2[0:40, o:o + 128], a0[0:40, 0:128], COL[0:40, 8:9], ALU.add, [n0, "c8"], ["T2S%d" % d, "T2B%d" % d])
         u, un = slot(b, 1)
         c0 = 2048.0 + 31.0 * t + 97.0 * 16 * d
-        terms, r = [(T.T2[0:97, o:o + 128], T.RF[0:97, :])], ["T2S%d" % d, "T2C%d" % d, "RF"]
+        terms, r = [(T.T2[0:97, o:o + 128], T.RF[0:97, :])], ["T2S%d" % d, "T2C%d" % d, "T2D%d" % d, "RF"]
         mm(u, terms, r, [un])
         if WRAP[2 * min(t, 1) + (d != E)] == "a":
             t1(sl(T.PP, d), u, c0, ALU.add, [un], ["PP%d" % d])
@@ -463,25 +490,23 @@ def program(T, topo, rank):
             act(sl(T.SQ, d), u, ACT.Square, [un], ["SQ%d" % d], bias=c0 - 2048.0 + 64.0)
             t1(sl(T.PP, d), sl(T.SQ, d), -4096.0, ALU.add, ["SQ%d" % d], ["PP%d" % d])
         ts(sl(T.HI, d), sl(T.PP, d), 7, 4095, ALU.arith_shift_right, ALU.bitwise_and, ["PP%d" % d], ["HI%d" % d])
-        p, pn = slot(2 + (d != E), 1)
-        mm(p, [(T.T2[0:40, o:o + 128], T.RG[0:40, :])], ["T2S%d" % d, "T2B%d" % d, "RG"], [pn])
 
     def xrep(d):
         ks = range(XR // 128)
         mms([(sl(PB[d], k), [(ID[:], xs(d))]) for k in ks], ["ID", "X%d" % d], [ps(d, k) for k in ks], XR, xext(d))
 
     def places(d, t):
-        o = 128 * d
-        a, an = slot(2 + (d != E), 2)
-        mms([(PB[2 + (d != E)][0:8, 256 + k:384:16], [(T.EQ[:, o + k:o + 128:16], sl(T.RN, t, 8))]) for k in range(16)],
+        o, b = 128 * d, 2 + (d != E)
+        (a, an), (p, pn) = slot(b, 2), slot(6 + (d != E), 3)
+        mm(p, [(T.T2[0:40, o:o + 128], T.RG[0:40, :])], ["T2S%d" % d, "T2B%d" % d, "RG"], [pn], stop=False)
+        mms([(PB[b][0:8, 256 + k:384:16], [(T.EQ[:, o + k:o + 128:16], sl(T.RN, t, 8))]) for k in range(16)],
             ["EQ%d" % d, "RN%d" % t], [an], 128)
         act(T.T2N[0:8, o:o + 128], a[0:8, :], ACT.Copy, [an], ["T2N%d" % d])
         mm(a, [(T.T2N[0:16, o:o + 128], T.RB[0:16, :])], ["RB", "T2N%d" % d], [an])
-        p, pn = slot(2 + (d != E), 1)
         tt(sl(T.AI, d), sl(T.HI, d), a, ALU.mult, ["HI%d" % d, an], ["AI%d" % d])
-        t1(sl(T.PL, d), sl(T.AI, d), 12, ALU.arith_shift_right, ["AI%d" % d], ["PL%d" % d])
-        tt(sl(T.AI, d), sl(T.PL, d), p, ALU.add, ["PL%d" % d, pn], ["AI%d" % d])
-        cp(sl(T.OFF, d), sl(T.AI, d), ["AI%d" % d], ["OFF%d" % d])
+        t1(sl(T.PL, d), sl(T.AI, d), 1023.5 + EPS, ALU.add, ["AI%d" % d], ["PL%d" % d])
+        mm(p, [(T.IH[:], sl(T.PL, d))], ["IH", "PL%d" % d], [pn], start=False)
+        t1(sl(T.OFF, d), p, -1024.0, ALU.add, [pn], ["OFF%d" % d])
 
     def tmat(d):
         ts(sl(T.BT, d), T.BB[:], fmsg(d, 0, 256, 257), -1.0, ALU.mult, ALU.mult, ["BB", "TP%d" % d], ["BT%d" % d], fext(d, 0), 64)
@@ -494,10 +519,10 @@ def program(T, topo, rank):
             cp(fmsg(d, 0, 256, 257), T.DVL[:, o + 7:o + 8], [], ["TP%d" % d], ext, 1)
             tmat(d)
         o += 8 + 128 * t
-        mm(a, [(T.BB[:], x)], ["BB", xn], [an], xext(d))
+        mm(a, [(T.BB[:], x)], ["BB", xn, "HI%d" % d], [an], xext(d))
         act(sl(T.TQ, d), a, ACT.Identity, [an], ["TQ%d" % d], bias=MAGIC, scale=1.0 / 64)
         mm(e, [(T.BB[:], x), (T.IDN64[:], sl(T.TQ, d))], ["BB", xn, "IDN64", "TQ%d" % d], [en])
-        mm(c, [(ID[:], x), (T.IDN[:], T.DVL[:, o:o + 128])], ["ID", "IDN", xn], [cn], xext(d) + ext)
+        mm(c, [(ID[:], x), (T.IDN[:], T.DVL[:, o:o + 128])], ["ID", "IDN", xn, "HI%d" % d], [cn], xext(d) + ext)
         act(m, e, ACT.Identity, [en], ["SM%d%d" % (d, t)], bias=129.0 * 64)
         act(sl(T.ZZ, d), c, ACT.Abs, [cn], ["ZZ%d" % d])
         act(sl(T.AZ, d), sl(T.ZZ, d), ACT.Abs, ["ZZ%d" % d], ["AZ%d" % d], bias=tgc[d], scale=-1.0)
@@ -511,6 +536,7 @@ def program(T, topo, rank):
         n = 256 if t else 257
         send([(1 - 2 * d, fmsg(d, t, 0, n), fmsg(1 - d, t, 0, n), "fa%d_%d" % (1 - d, t))], 2 * n,
              ["MZ%d%d" % (d, t), "SM%d%d" % (d, t), "TP%d" % d])
+        ops[-1]["out"] = [(s, lat + MARGIN, rows) for s, lat, rows in ops[-1]["out"]]
 
     def job(d, t):
         second = 0 if d == E else 1
@@ -528,31 +554,31 @@ def program(T, topo, rank):
             ops[-1]["pen"] = PEN
             ys += w
             for u in range(o, o + n, XR):
-                m = "M%d_%d" % (d, u // XR)
+                m, c = "M%d_%d" % (d, u // 128), min(XR, o + n - u)
                 ms.append(m)
-                tt(MM[d][:, u:u + XR], YY[d][:, u:u + XR], PB[d][:, 0:XR], ALU.max, w + [ps(d, s) for s in range(XR // 128)],
-                   [m], n=XR)
+                tt(MM[d][:, u:u + c], YY[d][:, u:u + c], PB[d][:, 0:c], ALU.max, w + [ps(d, s) for s in range(XR // 128)], [m], n=c)
                 ops[-1]["pen"] = PEN
                 mms([(PB[b][:, 15 - pos:128:16], [(sl(YY[d], pos), T.BS[:, 16:24]), (sl(MM[d], pos), T.BS[:, 8:16])])
-                     for pos in range(u // 128, (u + XR) // 128)], w + [m, "BSP", "BSN"], [ps(b, 0)], XR)
+                     for pos in range(u // 128, (u + c) // 128)], w + [m, "BSP", "BSN"], [ps(b, 0)], c)
             o += n
-        off, o = sl(T.BOFF, d, 8), 128 * d
+        off, o, z = sl(T.BOFF, d, 8), 128 * d, 144 * d
         key, mark = sl(KK[d], 3 * t + d), len(ops)
-        (cm, cn), (df, dfn), (kd, kn) = slot(4 + d, 2), slot(b, 3), slot(d, 3)
-        x, mz, r = xs(d), fmsg(d, t, 0, 128), ["ID", "IDN", "X%d" % d, "MZ%d%d" % (d, t), "YB%d" % d]
+        (cm, cn), (df, dfn), (kd, kn) = slot(4 + d, 2), slot(d, 3), slot(6 + second, 3)
+        x, mz, r = xs(d), fmsg(d, t, 0, 128), ["ID", "IDN", "X%d" % d, "MZ%d%d" % (d, t)]
         mm(cm, [(T.BN[:], sl(T.AX, d)), (sl(T.BT, d), fmsg(d, t, 128, 256))], ["BN", "AX%d" % d, "BT%d" % d, "SM%d%d" % (d, t)],
            [cn], fext(d, t), stop=False)
+        mm(kd, [(T.BB[:], T.C16[:])][d:] + [(ID[:], x), (ID[:], mz)], r + ["BB", "C16"], [kn], fext(d, t), stop=False)
         scan(sl(T.S1, d), T.D0[:], PB[b][:, 0:128], 0.0, ALU.add, ALU.max, ["D0", ps(b, 0)], ["S1%d" % d])
-        last = T.S1[:, o + 15:o + 128:16]
-        ts(sl(T.RR, d, 8), last, R2048, R2048, ALU.add, ALU.subtract, ["S1%d" % d], ["RR%d" % d], n=8)
-        tt(sl(T.IX, d, 8), last, sl(T.RR, d, 8), ALU.subtract, ["S1%d" % d, "RR%d" % d], ["IX%d" % d], n=16)
-        mms([(PB[d][0:8, a:128:16], [(T.ID2[:, a:128:16], sl(T.IX, d, 8))]) for a in range(16)],
-            ["ID2", "IX%d" % d], [ps(d, 0)], 128)
-        if TURN[second] == "s":
-            act(T.TT[0:8, o:o + 128], PB[d][0:8, 0:128], ACT.Identity, [ps(d, 0), "c7"], ["TT%d" % d], bias=COL[0:8, 7:8])
+        scan(sl(T.S2, d), T.D1[:], PB[b][:, 0:128], 0.0, ALU.add, ALU.max, ["D1", ps(b, 0)], ["S2%d" % d])
+        ix = T.ZW[:, z + 15:z + 143:16]
+        tt(ix, T.S1[:, o + 15:o + 128:16], T.S2[:, o + 15:o + 128:16], ALU.subtract, ["S1%d" % d, "S2%d" % d], ["IX%d" % d], n=16)
+        if TURN[second] == "z":
+            mm(PB[b][:, 0:8], [(T.ONE[:], T.CB[:])] + [(T.ZW[:, z + 15 - a:z + 143 - a], T.ID2[:, a:128:16]) for a in range(16)],
+               ["ONE", "CB", "ID2", "IX%d" % d], [ps(b, 0)], n=17 * 64)
         else:
+            mms([(PB[d][0:8, a:128:16], [(T.ID2[:, a:128:16], ix)]) for a in range(16)], ["ID2", "IX%d" % d], [ps(d, 0)], 128)
             t1(T.TT[0:8, o:o + 128], PB[d][0:8, 0:128], COL[0:8, 7:8], ALU.add, [ps(d, 0), "c7"], ["TT%d" % d])
-        mm(PB[b][:, 0:8], [(T.TT[0:8, o:o + 128], ID[0:8, 0:8])], ["TT%d" % d, "ID"], [ps(b, 0)], n=64)
+            mm(PB[b][:, 0:8], [(T.TT[0:8, o:o + 128], ID[0:8, 0:8])], ["TT%d" % d, "ID"], [ps(b, 0)], n=64)
         t1(off, PB[b][:, 0:8], col(2), ALU.add, [ps(b, 0), "c2"], ["BOFF%d" % d], n=8)
         act(sl(T.AY, d), YY[d][:, :].indirect(off), ACT.Abs, ys, ["AY%d" % d], xext(d), tgc[d], -1.0, 65 + 128 * GAT)
         cp(sl(T.YB, d), YY[d][:, :].indirect(off), ys, ["YB%d" % d], n=50 + 128 * GAT)
@@ -561,9 +587,9 @@ def program(T, topo, rank):
         else:
             cp(sl(T.MB, d), MM[d][:, :].indirect(off), ms, ["MB%d" % d], n=50 + 128 * GAT)
         mm(cm, [(T.BB[:], sl(T.AY, d))], ["BB", "AY%d" % d], [cn], start=False)
-        mm(df, [(T.IDN[:], x), (T.IDN[:], mz), (ID[:], sl(T.YB, d))], r, [dfn], fext(d, t))
-        mm(kd, [(T.BB[:], T.C16[:])][d:] + [(ID[:], x), (ID[:], mz), (T.BN512[:], sl(T.YB, d)), (T.B1024[:], sl(T.MB, d))],
-           r + ["BB", "C16", "BN512", "B1024", "MB%d" % d], [kn], fext(d, t))
+        mm(df, [(T.IDN[:], x), (T.IDN[:], mz), (ID[:], sl(T.YB, d))], r + ["YB%d" % d], [dfn], fext(d, t))
+        mm(kd, [(T.BN512[:], sl(T.YB, d)), (T.B1024[:], sl(T.MB, d))], ["BN512", "B1024", "YB%d" % d, "MB%d" % d], [kn],
+           start=False)
         t1(sl(T.OKY, d), cm, 0.0, ALU.is_le, [cn], ["OKY%d" % d])
         tt(sl(T.MY, d), df, sl(T.OKY, d), ALU.mult, [dfn, "OKY%d" % d], ["MY%d" % d])
         tt(key, kd, sl(T.MY, d), ALU.add, [kn, "MY%d" % d], ["key%d_%d" % (d, t)])
@@ -573,20 +599,14 @@ def program(T, topo, rank):
         send([(k, key, sl(KK[d], 3 * t + land[d, k][0]), "%s_%d" % (land[d, k][1], t)) for k in key_offs(d, t)], 512,
              ["key%d_%d" % (d, t)])
 
-    POS, last = sl(PB[7], 1), PB[7][:, 255:256]
-
-    def own(t):
-        finish(2, t - 1)
-        ring(2)
-        scan(POS, T.ONE[:], sl(T.EQ, 2), col(11 + t), ALU.mult, ALU.add, ["ONE", "EQ2", "nm%d" % (t - 1)], ["#71"])
-
     def append(t):
-        ts(sl(T.RN, t, 8), T.BS[:, 0:8], last, 128.0, ALU.mult, ALU.min, ["BS0", "#71"], ["RN%d" % t], n=8)
-        tt(T.VV[:], sl(T.EQ, 2), POS, ALU.mult, ["EQ2", "#71"], ["VV"])
-        t1(col(12 + t), last, 128.0, ALU.min, ["#71"], ["nm%d" % t], n=1)
-        mm(sl(PB[7], 2), [(T.IDBIG[:], T.MA[:]), (T.BK[:], sl(T.EQ, 2)), (T.BB[:], T.VV[:])],
-           ["IDBIG", "MA", "BK", "EQ2", "BB", "VV"], ["#72"])
-        scan(T.SC2[:], T.RS[:], sl(PB[7], 2), 0.0, ALU.mult, ALU.max, ["RS", "#72"], ["SC2"])
+        (pos, pn), (a, an), last = slot(7, 1), slot(6, 1), PB[7][:, 255:256]
+        scan(pos, T.ONE[:], sl(T.EQ, 2), col(11 + t), ALU.mult, ALU.add, ["ONE", "EQ2", "nm%d" % (t - 1)], [pn])
+        ts(sl(T.RN, t, 8), T.BS[:, 0:8], last, 128.0, ALU.mult, ALU.min, ["BS0", pn], ["RN%d" % t], n=8)
+        tt(T.VV[:], sl(T.EQ, 2), pos, ALU.mult, ["EQ2", pn], ["VV"])
+        ts(col(12 + t), last, 128.0, 256.0 * (t == STEPS - 1), ALU.min, ALU.add, [pn], ["nm%d" % t], n=1)
+        mm(a, [(T.IDBIG[:], T.MA[:]), (T.BK[:], sl(T.EQ, 2)), (T.BB[:], T.VV[:])], ["IDBIG", "MA", "BK", "EQ2", "BB", "VV"], [an])
+        scan(T.SC2[:], T.RS[:], a, 0.0, ALU.mult, ALU.max, ["RS", an], ["SC2"])
         t1(T.SOFF[:], T.SC2[:, 15:128:16], 255.0 - 16384.0, ALU.add, ["SC2"], ["SOFF"], n=8)
         cp(T.H2[:, :].indirect(T.SOFF[:, 0:8]), xs(2), ["SOFF", "X2"], ["H"], [("h2", 256)], 50 + 128 * SCA)
 
@@ -597,24 +617,25 @@ def program(T, topo, rank):
             ring(d)
             hashes(d, t)
             xrep(d)
-            if role == 0:
+            if d == 0:
                 fallback(d, t)
             elif t == 0:
                 tmat(d)
         if t:
-            own(t)
+            finish(2, t - 1)
+            ring(2)
             append(t)
         for d in (E, Z):
             places(d, t)
+        tell(0, t)
         for d in (E, Z):
-            for k in ((d,) if t else (E, Z) if d == E else ()) if role == 0 else ():
-                tell(k, t)
             job(d, t)
 
-    own(STEPS)
+    finish(2, STEPS - 1)
+    ring(2)
     dma("y", T.yx[:], xs(2), "out0", r=["X2"], tail=2.5)
-    ts(T.YN[:, 0:1], last, 128.0, 256.0, ALU.min, ALU.add, ["#71"], ["YN"], n=1)
-    dma("y", T.yn[:], T.YN[:, 0:1], "out1", r=["YN"], tail=2.3)
+    scan(T.YN[:], sl(T.EQ, 2), T.CAP[:], col(11 + STEPS), ALU.add, ALU.min, ["CAP", "EQ2", "nm%d" % (STEPS - 1)], ["YN"])
+    dma("y", T.yn[:], T.YN[:, 127:128], "out1", r=["YN"], tail=2.3)
     return ops, sent[0]
 
 

@@ -4,35 +4,51 @@ from concourse.mybir import AluOpType as ALU, ActivationFunctionType as ACT
 NR = 8
 STEPS = 3
 RING = 320
-WIDE = 512
+OVER = 4800
 BLOCKS = [[256, 256, 512, 512, 512], [512, 512, 512, 384, 128]]
 ONV = [[(0, 0), (0, 2)], [(0, 1), (0, 3)]]
 XR = 256
-WRAP = "aass"
+WRAP = "ssss"
 TURN = "zz"
-BEST = "ss"
+BEST = "sv"
+PICK = "vv"
+TEST = "vv"
+LEAN = False
 MAGIC = 128.5078125
 R64 = 1.5 * 2 ** 29
 EPS = 2.0 ** -13
+BIG = 2.0 ** 17
 HEAD = 2048
 FW = 272
-CY, OVH, WAKE, SELF, GAT, SCA, PEC, HOP, ROW, RATE, CALL = 0.00095, 0.01, 0.21, 0.2, 1.5, 3.8, 0.00045, 1.0, 0.025, 30e3, 0.3
-AT = {"ld0": 2.4, "ldt": 2.8, "ldc": 3.2, "go": 4.0, "h1a": 5.0, "h1b": 8.5, "ldv": 6.0, "h2": 16.0}
-LOOK, TOL, BETA, PEN, BOOST = 0.1, 0.05, 0.3, 0.5, (0.0, 0.0)
+CY, OVH, WAKE, SELF, GAT, SCA, PEC, HOP, ROW, RATE, CALL = 0.00105, 0.01, 0.21, 0.2, 1.5, 3.8, 0.00045, 1.0, 0.025, 30e3, 0.3
+AT = {"ld0": 2.4, "ldt": 2.8, "ldc": 3.2, "h1a": 5.0, "h1b": 7.0, "ldv": 4.5}
+LOOK, TOL, BETA, PEN, BOOST = 0.15, 0.03, 0.6, 1.0, (0.0, 0.0)
 ROUNDS, NUDGE = 0, 0.3
-MARGIN = 2.0
+AHEAD = (2.0, 2.0)
+OVS = 0.04
+EASE = ""
+ONS = ""
+FIRST = 0
+GATE = "S2%d"
+HASTE = 0.0
+LATER = ("TI4", "MA", "IDBIG", "BK", "IDO")
+HALVED = ("MI", "XI", "X0", "X1", "X2", "AX2", "EQ2", "#71", "AI", "PL", "OFF", "OKY", "MY", "key")
+CUT = "fFepk"
+MARGIN = 3.0
 
 SCRATCH = {}
 for _dt, _bufs in (
-    ("bfloat16", dict(H1=16 * RING, H2=16 * WIDE, IN0=144, X=416, DVS=392, DVL=784, ID=128, IDN=128, ID2=128, IDN64=128,
+    ("bfloat16", dict(H1=31 * RING + 192, IDO=128, SD=256, DO=128, IN0=144, X=416, DVS=392, DVL=784, ID=128, IDN=128, ID2=128, IDN64=128,
                       IDBIG=128, IDW=128, BB=128, BN=128, B1024=128, BN512=128, BK=128, BR=128, BRN=128, BR2=128, CK=128, C16=128,
-                      TG=128, MA=128, ONE=128, RB=128, BS=24, CB=8, RNB=16, RN=8 * STEPS, AX=384, EQ=384, VV=128, T2N=256,
+                      TG=128, MA=128, ONE=128, RB=128, BS=24, CB=8, RNB=8, RN=144 * STEPS, AX=384, EQ=400, MK=16, VV=128, T2N=256,
                       TQ=256, ZZ=256, AZ=256, OKZ=256, BT=256, SB=256, ZW=288, TT=256, Y0=2048, Y1=2048, M0=2048, M1=2048,
-                      YB=256, AY=256, MB=256, OKY=256, MY=256, FB=2 * FW * STEPS)),
-    ("float16", dict(T2=256, RF=128, RG=128, IH=128, PL=256)),
+                      YB=256, AY=256, MB=256, OKY=256, IDH=128, IDHN=128, RG=128, FB=2 * FW * STEPS)),
+    ("float16", dict(T2=256, RF=128, RH=128, IH=128, PL=256)),
+    ("bfloat16", dict(KQ=256)),
+    ("float32", dict(MY=256, IDF=128, REP=128, FAR=256, T4=256, RF4=128)),
     ("int32", dict(CNI=4, TEI=4, TE2=4, PI=4, KI=128, RI=128, CI=128, TI1=128, TI2=128, TI3=128, TI4=128, PP=256, HI=256,
-                   MI=384, XI=384)),
-    ("float32", dict(COL=16, RS=128, D0=128, D1=128, CAP=128, SC2=128, SQ=256, AI=256, S1=256, S2=256, YN=128, KA=384 * STEPS,
+                   HS=256, MI=384, XI=384)),
+    ("float32", dict(COL=16, RS=128, D0=128, D1=128, CAP=144, SC2=128, SQ=256, AI=256, S1=256, S2=256, YN=144, KA=384 * STEPS,
                      KB=384 * STEPS)),
     ("uint16", dict(SOFF=8, OFF=256, BOFF=16)),
 ):
@@ -41,10 +57,10 @@ for _dt, _bufs in (
 for _b in range(8):
     SCRATCH["PB%d" % _b] = ("psum", [128, 512], "float32")
 
-SEMAPHORES = ["qv", "qs", "qp", "qg", "ld0", "ldv", "ldt", "ldc", "h1a", "h1b", "h2", "go", "sent", "xa0", "xa1", "dv0",
-              "out0", "out1"]
+SEMAPHORES = ["qv", "qs", "qp", "qg", "ld0", "ldv", "ldt", "ldc", "h1a", "h1b", "sent", "xa0", "xa1", "dv0",
+              "ha0", "ha1", "out0", "out1"]
 for _t in range(STEPS):
-    SEMAPHORES += [_n + "_%d" % _t for _n in ("ka1", "ka2", "kb0", "kb2", "fa1")]
+    SEMAPHORES += [_n + "_%d" % _t for _n in ("ka1", "ka2", "kb0", "kb2", "ke", "fa1")]
 
 
 def banks(o):
@@ -253,7 +269,9 @@ def program(T, topo, rank):
 
     def op(e, f, r=(), w=(), x=(), c=0.0, inc=True, out=(), tail=0.0):
         x = [(s[0], s[1], role_of(T, topo, rank + s[2]) if len(s) > 2 else 0) for s in x]
-        ops.append({"e": e, "f": f, "r": list(r), "w": list(w), "x": x, "c": c, "inc": inc, "out": out, "tail": tail,
+        r, w = [[m for n in names for m in ([n + "<", n + ">"] if n.startswith(HALVED) and n[-1] not in "<>" else [n])]
+                for names in (r, w)]
+        ops.append({"e": e, "f": f, "r": r, "w": w, "x": x, "c": c, "inc": inc, "out": out, "tail": tail,
                     "line": None, "pen": 0.0})
 
     def cost(n):
@@ -274,8 +292,11 @@ def program(T, topo, rank):
     def fill(out, v, w):
         op("v", lambda q: q.memset(out, v), (), w, (), cost(64))
 
-    def scan(out, d0, d1, init, o0, o1, r, w):
-        op("v", lambda q: q.tensor_tensor_scan(out, d0, d1, init, o0, o1), r, w, (), cost(128))
+    def scan(out, d0, d1, init, o0, o1, r, w, n=128):
+        op("v", lambda q: q.tensor_tensor_scan(out, d0, d1, init, o0, o1), r, w, (), cost(n))
+
+    def cut(on):
+        return [(slice(0, 64), "<", 64), (slice(64, 128), ">", 64)] if on else [(slice(0, 128), "", 128)]
 
     def act(out, a, fn, r, w, x=(), bias=None, scale=None, n=128):
         kw = {}
@@ -283,7 +304,7 @@ def program(T, topo, rank):
             kw["bias"] = bias
         if scale is not None:
             kw["scale"] = scale
-        op("s", lambda q: q.activation(out, a, fn, **kw), r, w, x, cost(n))
+        op("s", lambda q: q.activation(out, a, fn, **kw), r, w, x, OVS + cost(n))
 
     def mms(groups, r, w, n, x=(), start=True, stop=True):
         def f(q):
@@ -355,7 +376,12 @@ def program(T, topo, rank):
 
     def kext(d, t, j):
         s = [[None, ("kb0", 1)], [("ka1", -1), None], [("ka2", 1), ("kb2", 2)]][d][j]
+        if s and both_off(rank + s[1], j, t):
+            return [("ke_%d" % t, len(plan(rank + s[1], key_offs(j, t)[:1])[0]), s[1])]
         return [] if s is None else [arrival("%s_%d" % (s[0], t), s[1], key_offs(j, t))]
+
+    def both_off(r, j, t):
+        return len([k for k in key_offs(j, t) if topo.chip(peer(k, r)) != topo.chip(peer(0, r))]) > 1
 
     def fmsg(d, t, lo, hi):
         o = FW * (2 * t + d)
@@ -368,17 +394,14 @@ def program(T, topo, rank):
     dma("s", T.IN0[:, 7:8], T.tg[:], "ld0", tail=999.0)
     dma("s", T.TEI[:, 0:1], T.te[:], "ldt", tail=999.0)
     dma("s", T.CNI[:, 0:1], T.cn[:], "ldc", tail=999.0)
+    dma("s", T.DVS[:, 8:392], T.dv[:], "ldv", tail=999.0)
     dma("y", T.H1[:, 0:HEAD], T.hs[:, 0:HEAD], "h1a")
     iota(T.PI[:, 0:1], [[0, 1]], 0, 1, ["PI0"], 0.14)
     iota(T.KI[:], [[1, 128]], 0, 0, ["KI"])
     iota(T.RI[:], [[0, 16], [1, 8]], 0, -1, ["RI"])
     iota(T.CI[:], [[-97, 16], [80, 8]], 97 * 15, 0, ["CI"])
     send([(1, T.IN0[:, 7:136], X[:, 7:136], "xa0"), (2, T.IN0[:, 7:136], X[:, 143:272], "xa1")], 258, (), [("ld0", 32)], 1.0)
-    op("g", lambda q: q.sem_inc(T.sem.go, 1), inc=False)
-    dma("y", T.DVS[:, 8:392], T.dv[:], "ldv", x=[("go", 1)])
-    dma("y", T.H1[:, HEAD:16 * RING], T.hs[:, HEAD:16 * RING], "h1b")
-    for k in range(16):
-        dma("y", T.H2[:, WIDE * k:WIDE * k + RING], T.hs[:, RING * k:RING * (k + 1)], "h2", x=[("h1b", 16)])
+    dma("y", T.H1[:, HEAD:16 * RING], T.hs[:, HEAD:16 * RING], "h1b", x=[("ld0", 32)])
 
     cp(col(0), T.PI[:, 0:1], ["PI0"], ["c0"], n=1)
     t1(T.PI[:, 1:2], T.PI[:, 0:1], 4, ALU.arith_shift_right, ["PI0"], ["PI1"], n=1)
@@ -387,12 +410,10 @@ def program(T, topo, rank):
     t1(T.TE2[:, 0:1], T.TEI[:, 0:1], col(2), ALU.add, ["c2"], ["TE20"], [("ldt", 16)], 1)
     t1(T.TE2[:, 1:2], T.TE2[:, 0:1], 4, ALU.arith_shift_right, ["TE20"], ["TE21"], n=1)
     cp(T.DVS[:, 7:8], T.TE2[:, 1:2], ["TE21"], ["DVS"], n=1)
-    send([(1, T.DVS[:, 7:392], T.DVL[:, 7:392], "dv0")], 770, ["DVS"], [("ldv", 16)])
-    for k, src, v, o in ((4, 0, 8.0, ALU.is_lt), (5, 0, 32.0, ALU.is_ge), (6, 2, float(WIDE), ALU.mult), (7, 0, 16.0, ALU.mult)):
+    for k, src, v, o in ((4, 0, 8.0, ALU.is_lt), (5, 0, 32.0, ALU.is_ge), (6, 2, float(RING), ALU.mult)):
         t1(col(k), T.PI[:, src:src + 1], v, o, ["PI%d" % src], ["c%d" % k], n=1)
     ts(col(11), col(2), 15.0, col(2), ALU.is_lt, ALU.mult, ["c2"], ["c11"], n=1)
     ts(col(3), col(11), 64.0, R64, ALU.mult, ALU.add, ["c11"], ["c3"], n=1)
-    ts(col(8), T.PI[:, 0:1], 32.0, -2048.0, ALU.is_lt, ALU.mult, ["PI0"], ["c8"], n=1)
     t1(T.TI1[:], T.KI[:], col(0), ALU.subtract, ["KI", "c0"], ["TI1"])
     t1(T.TI2[:], T.KI[:], 4, ALU.arith_shift_right, ["KI"], ["TI2"])
     t1(T.TI3[:], T.KI[:], 15, ALU.bitwise_and, ["KI"], ["TI3"])
@@ -403,21 +424,23 @@ def program(T, topo, rank):
     cp(T.RF[64:65, :], T.CI[64:65, :], ["CI"], ["RF"])
     fill(T.RF[96:97, :], 1.0, ["RF"])
     ts(T.RG[:], T.RI[:], 0.0, col(5), ALU.is_equal, ALU.mult, ["RI", "c5"], ["RG"])
+    if "s" in EASE:
+        t1(T.RH[:], T.RF[:], col(5), ALU.mult, ["RF", "c5"], ["RH"], n=64)
+        cp(T.RF4[0:32, :], T.RF[0:32, :], ["RF"], ["RF4"])
     ts(T.RB[:], T.RI[:], 0.0, 2.0 ** -12, ALU.is_equal, ALU.mult, ["RI"], ["RB"])
     cp(T.BS[:, 0:8], T.BB[:, 0:128:16], ["BB"], ["BS0"], n=8)
     fill(T.ONE[:], 1.0, ["ONE"])
     fill(T.ZW[:], 0.0, ["IX0", "IX1"])
-    fill(T.CAP[:], 384.0, ["CAP"])
+    fill(T.CAP[:], 8 * BIG, ["CAP"])
+    fill(T.CAP[:, 0:128], 128.0, ["CAP"])
     for d in (0, 1):
-        t1(sl(T.T2, d), T.ONE[:], 0.0, ALU.mult, ["ONE"], ["T2S%d" % d, "T2B%d" % d, "T2C%d" % d, "T2D%d" % d], n=64)
+        t1(sl(T.T2, d), T.ONE[:], 0.0, ALU.mult, ["ONE"], ["T2S%d" % d, "T2C%d" % d, "T2D%d" % d], n=64)
         cp(T.T2[64:65, 128 * d:128 * d + 128], T.ONE[64:65, :], ["ONE"], ["T2C%d" % d], n=64)
         t1(T.T2[96:97, 128 * d:128 * d + 128], T.TI3[96:97, :], 5.0, ALU.mult, ["TI3"], ["T2D%d" % d])
-        fill(PB[4 + d][0:32, 0:128], 0.0, [ps(4 + d, 0)])
-    fill(T.T2N[:], 256.0, ["T2N0", "T2N1"])
+        fill(PB[2 + d][0:32, 256:384], 256.0, [ps(2 + d, 2)])
     t1(T.BS[:, 8:16], T.BS[:, 0:8], 4096.0, ALU.mult, ["BS0"], ["BSP"], n=8)
     t1(T.BS[:, 16:24], T.BS[:, 0:8], -2048.0, ALU.mult, ["BS0"], ["BSN"], n=8)
-    for k, v in enumerate((RING, WIDE)):
-        ts(sl(T.RNB, k, 8), T.BS[:, 0:8], col(2), float(v), ALU.mult, ALU.mult, ["BS0", "c2"], ["RNB%d" % k], n=8)
+    t1(T.RNB[:], T.BS[:, 0:8], col(6), ALU.mult, ["BS0", "c6"], ["RNB"], n=8)
     t1(T.CB[:], T.KI[:, 0:8], 0.125, ALU.mult, ["KI"], ["CB"], n=8)
     ts(T.CK[:], T.TI3[:], 15.0, -15.5 / 128, ALU.is_equal, ALU.mult, ["TI3"], ["CK"])
     t1(T.CK[:], T.CK[:], -31.5 / 128, ALU.add, ["CK"], ["CK"], n=64)
@@ -427,69 +450,98 @@ def program(T, topo, rank):
     t1(T.TG[:], T.ONE[:], tgc[2], ALU.mult, ["ONE"], ["TG"], xext(2), 64)
     mats = [("IDN", "ID", -1.0), ("IDW", "ID", -2048.0), ("ID2", "ID", 2.0), ("BN", "BB", -1.0), ("B1024", "BB", 1024.0),
             ("BN512", "BB", -512.0), ("IDBIG", "ID", 16384.0), ("BRN", "BR", -1.0), ("BR2", "BR", 2.0), ("IH", "ID", 1.0),
-            ("IDN64", "ID", -64.0)]
+            ("IDN64", "ID", -64.0), ("IDO", "ID", OVER / 2.0)] + [("IDH", "ID", 0.5), ("IDHN", "ID", -0.5)] * ("s" in TEST)
     for buf, src, v in mats:
         t1(T[buf][:], T[src][:], v, ALU.mult, [src], [buf], n=64)
+    if "p" in BEST:
+        cp(T.IDF[:], ID[:], ["ID"], ["IDF"])
+        ts(T.REP[0:32, :], T.TI2[0:32, :], COL[0:32, 0:1], 0.25, ALU.is_equal, ALU.mult, ["TI2", "c0"], ["REP"])
     t1(T.RS[:], T.TI3[:], 0.0, ALU.is_gt, ["TI3"], ["RS"])
     ts(T.D0[:], T.RS[:], float(2 ** 25 + 64), -float(2 ** 25), ALU.mult, ALU.add, ["RS"], ["D0"])
     ts(T.D1[:], T.RS[:], float(2 ** 25), -float(2 ** 25), ALU.mult, ALU.add, ["RS"], ["D1"])
-    t1(col(12), T.CNI[:, 0:1], -256.0, ALU.add, [], ["nm0"], [("ldc", 16)], 1)
+    t1(T.RN[:, 127:128], T.CNI[:, 0:1], -256.0, ALU.add, [], ["nm0"], [("ldc", 16)], 1)
     t1(T.TI4[:], T.TI1[:], 15, ALU.bitwise_and, ["TI1"], ["TI4"])
-    t1(T.RN[:, 0:8], T.BS[:, 0:8], col(12), ALU.mult, ["BS0", "nm0"], ["RN0"], n=8)
+    t1(T.RN[:, 128:136], T.BS[:, 0:8], T.RN[:, 127:128], ALU.mult, ["BS0", "nm0"], ["RN0"], n=8)
+    fill(T.MK[:], 0.0, ["MK"])
+    ts(T.MK[:, 1:9], T.BS[:, 0:8], -BIG, BIG, ALU.mult, ALU.add, ["BS0"], ["MK"], n=8)
+    tt(T.EQ[:, 384:393], T.MK[:, 1:10], T.MK[:, 0:9], ALU.subtract, ["MK"], ["EQX"], n=18)
+    fill(T.EQ[:, 393:394], 256.0, ["EQX"])
+    t1(col(8), col(4), -7 * BIG, ALU.mult, ["c4"], ["c8"], n=1)
     t1(T.BK[:], T.BB[:], col(6), ALU.mult, ["BB", "c6"], ["BK"], n=64)
     t1(T.MA[:], T.TI4[:], 0.0, ALU.is_equal, ["TI4"], ["MA"])
+    later = [o for o in ops if o["w"] and o["w"][0] in LATER]
+    ops[:] = [o for o in ops if o not in later]
 
     def finish(d, t):
         a = [sl(K, 3 * t + d) for K in KK]
-        if d == 2:
-            tt(sl(T.MI, d), a[0], a[1], ALU.max, [], ["MI2"], kext(d, t, 0) + kext(d, t, 1), 256)
-        else:
+        mi, xi = sl(T.MI, d), sl(T.XI, d)
+        if d < 2:
             p, pn = slot(d, 2)
             act(p, a[d], ACT.Copy, ["key%d_%d" % (d, t)], [pn])
-            tt(sl(T.MI, d), a[1 - d], p, ALU.max, [pn], ["MI%d" % d], kext(d, t, 1 - d))
-        t1(sl(T.XI, d), sl(T.MI, d), 255, ALU.bitwise_and, ["MI%d" % d], ["XI%d" % d])
-        cp(xs(d), sl(T.XI, d), ["XI%d" % d], ["X%d" % d])
+        for c, h, n in cut("f" in CUT if d == 2 else "F" in CUT):
+            if d == 2:
+                tt(mi[:, c], a[0][:, c], a[1][:, c], ALU.max, [], ["MI2" + h], kext(d, t, 0) + kext(d, t, 1), 2 * n)
+            else:
+                tt(mi[:, c], a[1 - d][:, c], p[:, c], ALU.max, [pn], ["MI%d" % d + h], kext(d, t, 1 - d), n)
+            t1(xi[:, c], mi[:, c], 255, ALU.bitwise_and, ["MI%d" % d + h], ["XI%d" % d + h], n=n)
+            cp(xs(d)[:, c], xi[:, c], ["XI%d" % d + h], ["X%d" % d + h], n=n)
+            if d == 2:
+                t1(sl(T.AX, d)[:, c], xi[:, c], tgc[d], ALU.max, ["XI2" + h], ["AX2" + h], n=n)
 
-    def ring(d):
-        u, un = slot(6, 0) if d == 2 else slot(4 + d, 2)
+    def ring(d, t=1):
+        u, un = slot(6, 0) if d == 2 else slot(d, 3)
         if d == 2:
             mm(u, [(T.CK[:], T.ONE[:]), (T.BRN[:], T.TG[:])], ["CK", "ONE", "BRN", "TG"], [un], stop=False)
-            t1(sl(T.AX, d), sl(T.XI, d), tgc[d], ALU.max, ["XI2"], ["AX2"])
             mm(u, [(T.BRN[:], xs(d)), (T.BR2[:], sl(T.AX, d))], ["BRN", "BR2", "X2", "AX2"], [un], start=False)
         else:
             act(sl(T.AX, d), xs(d), ACT.Abs, ["X%d" % d], ["AX%d" % d], xext(d), tgc[d], -1.0)
+            if t and "r" in EASE:
+                mm(u, [(T.BB[:], sl(T.AX, d))], ["BB", "AX%d" % d], [un])
+                act(sl(T.KQ, d), u, ACT.Identity, [un], ["KQ%d" % d], bias=MAGIC, scale=1.0 / 64)
+                return ts(sl(T.EQ, d), sl(T.KQ, d), 144.0, col(7), ALU.min, ALU.is_equal, ["KQ%d" % d, "c7"], ["EQ%d" % d], n=64)
             mm(u, [(T.CK[:], T.ONE[:]), (T.BR[:], sl(T.AX, d))], ["CK", "ONE", "BR", "AX%d" % d], [un])
-        ts(sl(T.EQ, d), u, R64, col(3), ALU.add, ALU.is_equal, [un, "c3"], ["EQ%d" % d])
+        for c, h, n in cut(d == 2 and "e" in CUT):
+            ts(sl(T.EQ, d)[:, c], u[:, c], R64, col(3), ALU.add, ALU.is_equal, [un, "c3"], ["EQ%d" % d + h], n=n)
 
     def hashes(d, t):
         b, o, xo = 4 + d, 128 * d, xcol[d]
         a0, n0 = PB[b], ps(b, 0)
-        mms([(a0[0:8, a:128:16], [(X[:, xo + a:xo + 128:16], T.BS[:, 0:8])]) for a in range(16)],
-            ["X%d" % d, "BS0"], [n0], 128, xext(d))
-        if t == 0:
-            t1(T.T2[0:8, o:o + 128], a0[0:8, 0:128], -2048.0, ALU.add, [n0], ["T2S%d" % d])
-        mms([(a0[32:40, a:128:16], [(T.EQ[:, o + a:o + 128:16], sl(T.RNB, min(t, 1), 8))]) for a in range(16)],
-            ["EQ%d" % d, "RNB%d" % min(t, 1)], [n0], 128)
-        if t == 0:
-            cp(T.T2[32:40, o:o + 128], a0[32:40, 0:128], [n0], ["T2B%d" % d])
+        mms([(a0[0:8, a:128:16], [(X[:, xo + a:xo + 128:16], T.BS[:, 0:8])]) for a in range(16)], ["X%d" % d, "BS0"], [n0], 128)
+        if "s" in EASE:
+            act(T.T4[0:8, o:o + 128], a0[0:8, 0:128], ACT.Identity, [n0], ["T4%d" % d], bias=-2048.0)
         else:
-            t1(T.T2[0:40, o:o + 128], a0[0:40, 0:128], COL[0:40, 8:9], ALU.add, [n0, "c8"], ["T2S%d" % d, "T2B%d" % d])
+            t1(T.T2[0:8, o:o + 128], a0[0:8, 0:128], -2048.0, ALU.add, [n0], ["T2S%d" % d])
+        mix(d, t, d, sl(T.HI, d), "HI%d" % d)
+
+    def mix(d, t, k, hi, name):
+        b = 4 + d
         u, un = slot(b, 1)
         c0 = 2048.0 + 31.0 * t + 97.0 * 16 * d
-        terms, r = [(T.T2[0:97, o:o + 128], T.RF[0:97, :])], ["T2S%d" % d, "T2C%d" % d, "T2D%d" % d, "RF"]
-        mm(u, terms, r, [un])
+        terms, r = [(T.T2[0:97, 128 * k:128 * k + 128], T.RF[0:97, :])], ["T2S%d" % k, "T2C%d" % k, "T2D%d" % k, "RF"]
+        n = 128
+        if t and "s" in EASE:
+            terms = [(T.T2[0:97, 0:128], T.RH[0:97, :]), (T.T4[0:8, 128 * k:128 * k + 128], T.RF4[0:8, :])]
+            r, n = ["T2C0", "T2D0", "RH", "RF4", "T4%d" % k], 640
+        mm(u, terms, r, [un], n=n)
         if WRAP[2 * min(t, 1) + (d != E)] == "a":
             t1(sl(T.PP, d), u, c0, ALU.add, [un], ["PP%d" % d])
-            t1(sl(T.HI, d), sl(T.PP, d), 4095, ALU.bitwise_and, ["PP%d" % d], ["HI%d" % d])
-            t1(u, sl(T.HI, d), 128.0, ALU.add, ["HI%d" % d], [un])
-            tt(sl(T.PP, d), sl(T.HI, d), u, ALU.mult, ["HI%d" % d, un], ["PP%d" % d])
+            t1(hi, sl(T.PP, d), 4095, ALU.bitwise_and, ["PP%d" % d], [name])
+            t1(u, hi, 128.0, ALU.add, [name], [un])
+            tt(sl(T.PP, d), hi, u, ALU.mult, [name, un], ["PP%d" % d])
         else:
             act(sl(T.SB, d), u, ACT.Sign, [un], ["SB%d" % d], bias=c0 - 4095.5)
             u, un = slot(b, 3)
-            mm(u, terms + [(T.IDW[:], sl(T.SB, d))], r + ["IDW", "SB%d" % d], [un])
+            mm(u, terms + [(T.IDW[:], sl(T.SB, d))], r + ["IDW", "SB%d" % d], [un], n=n + 128)
             act(sl(T.SQ, d), u, ACT.Square, [un], ["SQ%d" % d], bias=c0 - 2048.0 + 64.0)
             t1(sl(T.PP, d), sl(T.SQ, d), -4096.0, ALU.add, ["SQ%d" % d], ["PP%d" % d])
-        ts(sl(T.HI, d), sl(T.PP, d), 7, 4095, ALU.arith_shift_right, ALU.bitwise_and, ["PP%d" % d], ["HI%d" % d])
+        ts(hi, sl(T.PP, d), 7, 4095, ALU.arith_shift_right, ALU.bitwise_and, ["PP%d" % d], [name])
+
+    def first_hashes():
+        mms([(PB[6][0:8, a:128:16], [(T.IN0[:, 8 + a:136:16], T.BS[:, 0:8])]) for a in range(16)], ["BS0"], ["#60"], 128, xext(2))
+        t1(T.T2[0:8, 0:128], PB[6][0:8, 0:128], -2048.0, ALU.add, ["#60"], ["T2S0"])
+        for d in (0, 1):
+            mix(d, 0, 0, sl(T.HS, d), "HS%d" % d)
+        send([(1 + d, sl(T.HS, d), sl(T.HI, d), "ha%d" % d) for d in (0, 1)], 512, ["HS0", "HS1"])
 
     def xrep(d):
         ks = range(XR // 128)
@@ -497,16 +549,34 @@ def program(T, topo, rank):
 
     def places(d, t):
         o, b = 128 * d, 2 + (d != E)
-        (a, an), (p, pn) = slot(b, 2), slot(6 + (d != E), 3)
-        mm(p, [(T.T2[0:40, o:o + 128], T.RG[0:40, :])], ["T2S%d" % d, "T2B%d" % d, "RG"], [pn], stop=False)
-        mms([(PB[b][0:8, 256 + k:384:16], [(T.EQ[:, o + k:o + 128:16], sl(T.RN, t, 8))]) for k in range(16)],
-            ["EQ%d" % d, "RN%d" % t], [an], 128)
-        act(T.T2N[0:8, o:o + 128], a[0:8, :], ACT.Copy, [an], ["T2N%d" % d])
+        (a, an), (p, pn), cn = slot(b, 3), slot(6 + (d != E), 3), ps(b, 2)
+        for rows, rhs, name in ((slice(32, 40), T.RNB[:], "RNB"), (slice(0, 8), T.RN[:, 144 * t + 128:144 * t + 136], "RN%d" % t)):
+            mms([(PB[b][rows, 256 + k:384:16], [(T.EQ[:, o + k:o + 128:16], rhs)]) for k in range(16)], ["EQ%d" % d, name], [cn], 128)
+        if "nN"[d != E] in ONS:
+            t1(T.T2N[0:40, o:o + 128], PB[b][0:40, 256:384], COL[0:40, 8:9] if t else 0.0, ALU.add, [cn, "c8"][:1 + min(t, 1)],
+               ["T2N%d" % d])
+        elif t:
+            act(T.T2N[0:40, o:o + 128], PB[b][0:40, 256:384], ACT.Identity, [cn, "c8"], ["T2N%d" % d], bias=COL[0:40, 8:9])
+        else:
+            act(T.T2N[0:40, o:o + 128], PB[b][0:40, 256:384], ACT.Copy, [cn], ["T2N%d" % d])
         mm(a, [(T.T2N[0:16, o:o + 128], T.RB[0:16, :])], ["RB", "T2N%d" % d], [an])
-        tt(sl(T.AI, d), sl(T.HI, d), a, ALU.mult, ["HI%d" % d, an], ["AI%d" % d])
-        t1(sl(T.PL, d), sl(T.AI, d), 1023.5 + EPS, ALU.add, ["AI%d" % d], ["PL%d" % d])
-        mm(p, [(T.IH[:], sl(T.PL, d))], ["IH", "PL%d" % d], [pn], start=False)
-        t1(sl(T.OFF, d), p, -1024.0, ALU.add, [pn], ["OFF%d" % d])
+        mm(p, [(T.T2N[0:40, o:o + 128], T.RG[0:40, :])], ["T2N%d" % d, "RG"], [pn], stop=False)
+        on = "pP"[d != E] in CUT
+        for c, h, n in cut(on):
+            tt(sl(T.AI, d)[:, c], sl(T.HI, d)[:, c], a[:, c], ALU.mult, ["HI%d" % d, an], ["AI%d" % d + h],
+               [] if t else [arrival("ha%d" % d, -1 - d, [1, 2])], n)
+            t1(sl(T.PL, d)[:, c], sl(T.AI, d)[:, c], 1023.5 + EPS, ALU.add, ["AI%d" % d + h], ["PL%d" % d + h], n=n)
+        lift = OVER / 2.0 if t else 0.0
+        if t and "dD"[d != E] in ONS:
+            ts(sl(T.SD, d), sl(T.AI, d), float(RING), 2.0, ALU.is_ge, ALU.mult, ["AI%d" % d], ["SD%d" % d])
+            lift = 0.0
+        elif t:
+            act(sl(T.SD, d), sl(T.AI, d), ACT.Sign, ["AI%d" % d], ["SD%d" % d], bias=EPS - RING)
+        mm(p, [(T.IH[:], sl(T.PL, d))], ["IH", "PL%d" % d], [pn], start=False, stop=t == 0)
+        if t:
+            mm(p, [(T.IDO[:], sl(T.SD, d))], ["IDO", "SD%d" % d], [pn], start=False)
+        for c, h, n in cut(on):
+            t1(sl(T.OFF, d)[:, c], p[:, c], lift - 1024.0, ALU.add, [pn], ["OFF%d" % d + h], n=n)
 
     def tmat(d):
         ts(sl(T.BT, d), T.BB[:], fmsg(d, 0, 256, 257), -1.0, ALU.mult, ALU.mult, ["BB", "TP%d" % d], ["BT%d" % d], fext(d, 0), 64)
@@ -514,16 +584,22 @@ def program(T, topo, rank):
     def fallback(d, t):
         b, o, xn = 4 + d, 392 * d, "X%d" % d
         (a, an), (c, cn), (e, en) = slot(b, 1), slot(b, 2), slot(b, 3)
-        x, m, ext = xs(d), fmsg(d, t, 128, 256), [arrival("dv%d" % d, -1 - d, [1 + d])]
+        x, m, ext = xs(d), fmsg(d, t, 128, 256), [arrival("dv0", -1, [1])]
         if t == 0:
             cp(fmsg(d, 0, 256, 257), T.DVL[:, o + 7:o + 8], [], ["TP%d" % d], ext, 1)
             tmat(d)
         o += 8 + 128 * t
         mm(a, [(T.BB[:], x)], ["BB", xn, "HI%d" % d], [an], xext(d))
-        act(sl(T.TQ, d), a, ACT.Identity, [an], ["TQ%d" % d], bias=MAGIC, scale=1.0 / 64)
+        if "f" in ONS:
+            ts(sl(T.TQ, d), a, 1.0 / 64, MAGIC, ALU.mult, ALU.add, [an], ["TQ%d" % d])
+        else:
+            act(sl(T.TQ, d), a, ACT.Identity, [an], ["TQ%d" % d], bias=MAGIC, scale=1.0 / 64)
         mm(e, [(T.BB[:], x), (T.IDN64[:], sl(T.TQ, d))], ["BB", xn, "IDN64", "TQ%d" % d], [en])
         mm(c, [(ID[:], x), (T.IDN[:], T.DVL[:, o:o + 128])], ["ID", "IDN", xn, "HI%d" % d], [cn], xext(d) + ext)
-        act(m, e, ACT.Identity, [en], ["SM%d%d" % (d, t)], bias=129.0 * 64)
+        if "f" in ONS:
+            t1(m, e, 129.0 * 64, ALU.add, [en], ["SM%d%d" % (d, t)])
+        else:
+            act(m, e, ACT.Identity, [en], ["SM%d%d" % (d, t)], bias=129.0 * 64)
         act(sl(T.ZZ, d), c, ACT.Abs, [cn], ["ZZ%d" % d])
         act(sl(T.AZ, d), sl(T.ZZ, d), ACT.Abs, ["ZZ%d" % d], ["AZ%d" % d], bias=tgc[d], scale=-1.0)
         mm(a, [(ID[:], sl(T.ZZ, d)), (T.IDN[:], x)], ["ID", "IDN", "ZZ%d" % d, xn], [an])
@@ -541,12 +617,12 @@ def program(T, topo, rank):
     def job(d, t):
         second = 0 if d == E else 1
         b = 2 + second
-        win = T.H2[:, :] if t else T.H1[:, :]
+        win = T.H1[:, :] if t else T.H1[:, 0:16 * RING]
         o, ys, ms = 0, ["BOFF%d" % d], ["BOFF%d" % d]
         for k, n in enumerate(BLOCKS[second]):
             src = win.indirect(T.OFF[:, 128 * d + o // 16:128 * d + (o + n) // 16])
-            r, w, ex = ["OFF%d" % d, "H"], ["Y%d_%d" % (d, k)], [("h1a", 16), ("h1b", 16)]
-            if (second, k) in ONV[role]:
+            r, w, ex = ["OFF%d" % d + "<" * (o + n <= 1024) + ">" * (o >= 1024), "H"], ["Y%d_%d" % (d, k)], [("h1a", 16), ("h1b", 16)]
+            if (second, k) in (ONV[role] if t else ONV[role][FIRST:]):
                 cp(YY[d][:, o:o + n], src, r, w, ex, 50 + n * GAT)
             else:
                 act(YY[d][:, o:o + n], src, ACT.Copy, r, w, ex, n=65 + n * GAT)
@@ -564,59 +640,111 @@ def program(T, topo, rank):
         off, o, z = sl(T.BOFF, d, 8), 128 * d, 144 * d
         key, mark = sl(KK[d], 3 * t + d), len(ops)
         (cm, cn), (df, dfn), (kd, kn) = slot(4 + d, 2), slot(d, 3), slot(6 + second, 3)
-        x, mz, r = xs(d), fmsg(d, t, 0, 128), ["ID", "IDN", "X%d" % d, "MZ%d%d" % (d, t)]
-        mm(cm, [(T.BN[:], sl(T.AX, d)), (sl(T.BT, d), fmsg(d, t, 128, 256))], ["BN", "AX%d" % d, "BT%d" % d, "SM%d%d" % (d, t)],
-           [cn], fext(d, t), stop=False)
-        mm(kd, [(T.BB[:], T.C16[:])][d:] + [(ID[:], x), (ID[:], mz)], r + ["BB", "C16"], [kn], fext(d, t), stop=False)
+        x, mz, r = xs(d), fmsg(d, t, 0, 128), ["ID", "IDN", "IDH", "IDHN", "X%d" % d, "MZ%d%d" % (d, t)]
+        sign = int(TEST[second] == "s")
+        one, neg = (T.IDH[:], T.IDHN[:]) if sign else (ID[:], T.IDN[:])
+        def bound():
+            mm(cm, [(T.BN[:], sl(T.AX, d)), (sl(T.BT, d), fmsg(d, t, 128, 256))],
+               ["BN", "AX%d" % d, "BT%d" % d, "SM%d%d" % (d, t)], [cn], fext(d, t), stop=False)
+
+        if BEST[second] != "p":
+            bound()
+        mm(kd, [(T.BB[:], T.C16[:])][d:] + [(one, x), (one, mz)], r + ["BB", "C16"], [kn], fext(d, t), stop=False)
         scan(sl(T.S1, d), T.D0[:], PB[b][:, 0:128], 0.0, ALU.add, ALU.max, ["D0", ps(b, 0)], ["S1%d" % d])
         scan(sl(T.S2, d), T.D1[:], PB[b][:, 0:128], 0.0, ALU.add, ALU.max, ["D1", ps(b, 0)], ["S2%d" % d])
         ix = T.ZW[:, z + 15:z + 143:16]
         tt(ix, T.S1[:, o + 15:o + 128:16], T.S2[:, o + 15:o + 128:16], ALU.subtract, ["S1%d" % d, "S2%d" % d], ["IX%d" % d], n=16)
         if TURN[second] == "z":
-            mm(PB[b][:, 0:8], [(T.ONE[:], T.CB[:])] + [(T.ZW[:, z + 15 - a:z + 143 - a], T.ID2[:, a:128:16]) for a in range(16)],
-               ["ONE", "CB", "ID2", "IX%d" % d], [ps(b, 0)], n=17 * 64)
+            terms = [(T.ONE[:], T.CB[:])] + [(T.ZW[:, z + 15 - a:z + 143 - a], T.ID2[:, a:128:16]) for a in range(16)]
+            step = 17 if second else 5
+            for a in range(0, 17, step):
+                mm(PB[b][:, 0:8], terms[a:a + step], ["ONE", "CB", "ID2", "IX%d" % d], [ps(b, 0)], n=64 * len(terms[a:a + step]),
+                   start=a == 0, stop=a + step >= 17)
         else:
             mms([(PB[d][0:8, a:128:16], [(T.ID2[:, a:128:16], ix)]) for a in range(16)], ["ID2", "IX%d" % d], [ps(d, 0)], 128)
             t1(T.TT[0:8, o:o + 128], PB[d][0:8, 0:128], COL[0:8, 7:8], ALU.add, [ps(d, 0), "c7"], ["TT%d" % d])
             mm(PB[b][:, 0:8], [(T.TT[0:8, o:o + 128], ID[0:8, 0:8])], ["TT%d" % d, "ID"], [ps(b, 0)], n=64)
         t1(off, PB[b][:, 0:8], col(2), ALU.add, [ps(b, 0), "c2"], ["BOFF%d" % d], n=8)
-        act(sl(T.AY, d), YY[d][:, :].indirect(off), ACT.Abs, ys, ["AY%d" % d], xext(d), tgc[d], -1.0, 65 + 128 * GAT)
-        cp(sl(T.YB, d), YY[d][:, :].indirect(off), ys, ["YB%d" % d], n=50 + 128 * GAT)
-        if BEST[second] == "s":
+        if second or not LEAN:
+            act(sl(T.AY, d), YY[d][:, :].indirect(off), ACT.Abs, ys, ["AY%d" % d], xext(d), tgc[d], -1.0, 65 + 128 * GAT)
+        if PICK[second] == "s":
+            act(sl(T.YB, d), YY[d][:, :].indirect(off), ACT.Copy, ys, ["YB%d" % d], n=65 + 128 * GAT)
+        else:
+            cp(sl(T.YB, d), YY[d][:, :].indirect(off), ys, ["YB%d" % d], n=50 + 128 * GAT)
+        if LEAN and not second:
+            act(sl(T.AY, d), sl(T.YB, d), ACT.Abs, ["YB%d" % d], ["AY%d" % d], xext(d), tgc[d], -1.0)
+        if BEST[second] == "p":
+            (far, fn) = slot(4 + d, 0)
+            mm(far[0:8, :], [(T.S2[:, o + 15:o + 128:16], T.IDF[:])], ["S2%d" % d, "IDF"], [fn], n=512)
+            act(T.FAR[0:8, o:o + 128], far[0:8, :], ACT.Copy, [fn], ["MB%d" % d])
+            bound()
+        elif BEST[second] == "s":
             act(sl(T.MB, d), MM[d][:, :].indirect(off), ACT.Copy, ms, ["MB%d" % d], n=65 + 128 * GAT)
         else:
             cp(sl(T.MB, d), MM[d][:, :].indirect(off), ms, ["MB%d" % d], n=50 + 128 * GAT)
         mm(cm, [(T.BB[:], sl(T.AY, d))], ["BB", "AY%d" % d], [cn], start=False)
-        mm(df, [(T.IDN[:], x), (T.IDN[:], mz), (ID[:], sl(T.YB, d))], r + ["YB%d" % d], [dfn], fext(d, t))
-        mm(kd, [(T.BN512[:], sl(T.YB, d)), (T.B1024[:], sl(T.MB, d))], ["BN512", "B1024", "YB%d" % d, "MB%d" % d], [kn],
-           start=False)
-        t1(sl(T.OKY, d), cm, 0.0, ALU.is_le, [cn], ["OKY%d" % d])
-        tt(sl(T.MY, d), df, sl(T.OKY, d), ALU.mult, [dfn, "OKY%d" % d], ["MY%d" % d])
-        tt(key, kd, sl(T.MY, d), ALU.add, [kn, "MY%d" % d], ["key%d_%d" % (d, t)])
+        mm(df, [(neg, x), (neg, mz), (one, sl(T.YB, d))], r + ["YB%d" % d], [dfn], fext(d, t))
+        if BEST[second] == "p":
+            mm(kd, [(one, sl(T.YB, d))][sign ^ 1:] + [(T.REP[0:8, :], T.FAR[0:8, o:o + 128])],
+               ["IDH", "REP", "MB%d" % d] + ["YB%d" % d] * sign, [kn], n=512 + 128 * sign, start=False)
+        else:
+            mm(kd, [(one, sl(T.YB, d))][sign ^ 1:] + [(T.BN512[:], sl(T.YB, d)), (T.B1024[:], sl(T.MB, d))],
+               ["IDH", "BN512", "B1024", "YB%d" % d, "MB%d" % d], [kn], start=False)
+        for c, h, n in cut("kK"[second ^ 1] in CUT):
+            ok, my = sl(T.OKY, d)[:, c], sl(T.MY, d)[:, c]
+            if sign:
+                act(ok, cm[:, c], ACT.Sign, [cn], ["OKY%d" % d + h], bias=0.5, scale=-1.0, n=n)
+            else:
+                t1(ok, cm[:, c], 0.0, ALU.is_le, [cn], ["OKY%d" % d + h], n=n)
+            tt(my, df[:, c], ok, ALU.mult, [dfn, "OKY%d" % d + h], ["MY%d" % d + h], n=n)
+            tt(key[:, c], kd[:, c], my, ALU.add, [kn, "MY%d" % d + h], ["key%d_%d" % (d, t) + h], n=n)
         for a in ops[mark:]:
             a["pen"] = -BOOST[second]
         land = {(0, 1): (1, "ka1"), (0, -1): (2, "ka2"), (1, -1): (0, "kb0"), (1, -2): (2, "kb2")}
-        send([(k, key, sl(KK[d], 3 * t + land[d, k][0]), "%s_%d" % (land[d, k][1], t)) for k in key_offs(d, t)], 512,
-             ["key%d_%d" % (d, t)])
+        items = [(k, key, sl(KK[d], 3 * t + land[d, k][0]), "%s_%d" % (land[d, k][1], t)) for k in key_offs(d, t)]
+        if both_off(rank, d, t):
+            es = plan(rank, [items[0][0]])[0]
+            tr = RemoteDMATransfer(dst_ids=[DstId(rid=topo.addr(peer(it[0]))[0], pnc=topo.addr(peer(it[0]))[1]) for it in items],
+                                   dma_engine_mask=sum(1 << e for e in es), remote_sem=T.sem["ke_%d" % t], srcs=[key],
+                                   dsts=[it[2] for it in items])
+            sent[0] += len(es)
+            rows = 256 / len(es) * (ROW + 512 / RATE)
+            op("g", lambda q: q.remote_dma_fused([tr], local_sem=T.sem.sent), ["key%d_%d" % (d, t)], (), (), CALL, False,
+               [("ke_%d" % t, HOP + rows, rows)])
+        else:
+            send(items, 512, ["key%d_%d" % (d, t)])
+
+    def before(t):
+        return T.RN[:, 144 * t - 17:144 * t - 16]
 
     def append(t):
-        (pos, pn), (a, an), last = slot(7, 1), slot(6, 1), PB[7][:, 255:256]
-        scan(pos, T.ONE[:], sl(T.EQ, 2), col(11 + t), ALU.mult, ALU.add, ["ONE", "EQ2", "nm%d" % (t - 1)], [pn])
-        ts(sl(T.RN, t, 8), T.BS[:, 0:8], last, 128.0, ALU.mult, ALU.min, ["BS0", pn], ["RN%d" % t], n=8)
+        (pos, pn), (a, an) = slot(7, 1), slot(6, 1)
+        scan(T.RN[:, 144 * t:144 * t + 136], T.EQ[:, 256:392], T.CAP[:, 0:136], before(t), ALU.add, ALU.min,
+             ["CAP", "EQ2", "EQX", "RN%d" % (t - 1)], ["RN%d" % t], 136)
+        scan(pos, T.ONE[:], sl(T.EQ, 2), before(t), ALU.mult, ALU.add, ["ONE", "EQ2", "RN%d" % (t - 1)], [pn])
         tt(T.VV[:], sl(T.EQ, 2), pos, ALU.mult, ["EQ2", pn], ["VV"])
-        ts(col(12 + t), last, 128.0, 256.0 * (t == STEPS - 1), ALU.min, ALU.add, [pn], ["nm%d" % t], n=1)
-        mm(a, [(T.IDBIG[:], T.MA[:]), (T.BK[:], sl(T.EQ, 2)), (T.BB[:], T.VV[:])], ["IDBIG", "MA", "BK", "EQ2", "BB", "VV"], [an])
+        ts(T.DO[:], T.VV[:], RING - 255.0, float(OVER), ALU.is_ge, ALU.mult, ["VV"], ["DO"], n=64)
+        ops[-1]["pen"] = ops[-2]["pen"] = ops[-3]["pen"] = -HASTE
+        mm(a, [(T.IDBIG[:], T.MA[:]), (T.BK[:], sl(T.EQ, 2)), (T.BB[:], T.VV[:])], ["IDBIG", "MA", "BK", "EQ2", "BB", "VV"], [an],
+           stop=False)
+        mm(a, [(T.BB[:], T.DO[:])], ["BB", "DO"], [an], start=False)
         scan(T.SC2[:], T.RS[:], a, 0.0, ALU.mult, ALU.max, ["RS", an], ["SC2"])
         t1(T.SOFF[:], T.SC2[:, 15:128:16], 255.0 - 16384.0, ALU.add, ["SC2"], ["SOFF"], n=8)
-        cp(T.H2[:, :].indirect(T.SOFF[:, 0:8]), xs(2), ["SOFF", "X2"], ["H"], [("h2", 256)], 50 + 128 * SCA)
+        cp(T.H1[:, :].indirect(T.SOFF[:, 0:8]), xs(2), ["SOFF", "X2"], ["H"], (), 50 + 128 * SCA)
 
+    first_hashes()
+    send([(1, T.DVS[:, 7:392], T.DVL[:, 7:392], "dv0")], 770, ["DVS"], [("ldv", 16)])
     for t in range(STEPS):
         for d in (E, Z):
+            mark = len(ops)
             if t:
                 finish(d, t - 1)
-            ring(d)
-            hashes(d, t)
+            ring(d, t)
+            if t:
+                hashes(d, t)
             xrep(d)
+            for a in ops[mark:]:
+                a["pen"] = -AHEAD[role] * (d == Z)
             if d == 0:
                 fallback(d, t)
             elif t == 0:
@@ -626,16 +754,24 @@ def program(T, topo, rank):
             ring(2)
             append(t)
         for d in (E, Z):
+            mark = len(ops)
             places(d, t)
+            for a in ops[mark:]:
+                a["pen"] = -AHEAD[role] * (d == Z)
         tell(0, t)
         for d in (E, Z):
             job(d, t)
+        if t == 0:
+            for o in later:
+                o["r"].append(GATE % Z)
+            ops.extend(later)
 
     finish(2, STEPS - 1)
     ring(2)
     dma("y", T.yx[:], xs(2), "out0", r=["X2"], tail=2.5)
-    scan(T.YN[:], sl(T.EQ, 2), T.CAP[:], col(11 + STEPS), ALU.add, ALU.min, ["CAP", "EQ2", "nm%d" % (STEPS - 1)], ["YN"])
-    dma("y", T.yn[:], T.YN[:, 127:128], "out1", r=["YN"], tail=2.3)
+    scan(T.YN[:, 0:138], T.EQ[:, 256:394], T.CAP[:, 0:138], before(STEPS), ALU.add, ALU.min,
+         ["CAP", "EQ2", "EQX", "RN%d" % (STEPS - 1)], ["YN"], 138)
+    dma("y", T.yn[:], T.YN[:, 137:138], "out1", r=["YN"], tail=2.3)
     return ops, sent[0]
 
 

from concourse.bass import DstId, RemoteDMATransfer
from concourse.mybir import AluOpType as ALU, ActivationFunctionType as ACT

NR = 8
STEPS = 3
RING = 320
OVER = 4800
BLOCKS = [[256, 256, 512, 512, 512], [512, 512, 512, 384, 128]]
ONV = [[(0, 0), (0, 2)], [(0, 1), (0, 3)]]
XR = 256
WRAP = "ssss"
TURN = "zz"
BEST = "sv"
PICK = "vv"
TEST = "vv"
LEAN = False
MAGIC = 128.5078125
R64 = 1.5 * 2 ** 29
EPS = 2.0 ** -13
BIG = 2.0 ** 17
HEAD = 2048
FW = 272
CY, OVH, WAKE, SELF, GAT, SCA, PEC, HOP, ROW, RATE, CALL = 0.00105, 0.01, 0.21, 0.2, 1.5, 3.8, 0.00045, 1.0, 0.025, 30e3, 0.3
AT = {"ld0": 2.4, "ldt": 2.8, "ldc": 3.2, "h1a": 5.0, "h1b": 7.0, "ldv": 4.5}
LOOK, TOL, BETA, PEN, BOOST = 0.15, 0.03, 0.6, 1.0, (0.0, 0.0)
ROUNDS, NUDGE = 0, 0.3
AHEAD = (2.0, 2.0)
OVS = 0.04
EASE = ""
ONS = ""
FIRST = 0
GATE = "S2%d"
HASTE = 0.0
LATER = ("TI4", "MA", "IDBIG", "BK", "IDO")
HALVED = ("MI", "XI", "X0", "X1", "X2", "AX2", "EQ2", "#71", "AI", "PL", "OFF", "OKY", "MY", "key")
CUT = "fFepk"
MARGIN = 3.0

SCRATCH = {}
for _dt, _bufs in (
    ("bfloat16", dict(H1=31 * RING + 192, IDO=128, SD=256, DO=128, IN0=144, X=416, DVS=392, DVL=784, ID=128, IDN=128, ID2=128, IDN64=128,
                      IDBIG=128, IDW=128, BB=128, BN=128, B1024=128, BN512=128, BK=128, BR=128, BRN=128, BR2=128, CK=128, C16=128,
                      TG=128, MA=128, ONE=128, RB=128, BS=24, CB=8, RNB=8, RN=144 * STEPS, AX=384, EQ=400, MK=16, VV=128, T2N=256,
                      TQ=256, ZZ=256, AZ=256, OKZ=256, BT=256, SB=256, ZW=288, TT=256, Y0=2048, Y1=2048, M0=2048, M1=2048,
                      YB=256, AY=256, MB=256, OKY=256, IDH=128, IDHN=128, RG=128, FB=2 * FW * STEPS)),
    ("float16", dict(T2=256, RF=128, RH=128, IH=128, PL=256)),
    ("bfloat16", dict(KQ=256)),
    ("float32", dict(MY=256, IDF=128, REP=128, FAR=256, T4=256, RF4=128)),
    ("int32", dict(CNI=4, TEI=4, TE2=4, PI=4, KI=128, RI=128, CI=128, TI1=128, TI2=128, TI3=128, TI4=128, PP=256, HI=256,
                   HS=256, MI=384, XI=384)),
    ("float32", dict(COL=16, RS=128, D0=128, D1=128, CAP=144, SC2=128, SQ=256, AI=256, S1=256, S2=256, YN=144, KA=384 * STEPS,
                     KB=384 * STEPS)),
    ("uint16", dict(SOFF=8, OFF=256, BOFF=16)),
):
    for _n, _c in _bufs.items():
        SCRATCH[_n] = ("sbuf", [128, _c], _dt)
for _b in range(8):
    SCRATCH["PB%d" % _b] = ("psum", [128, 512], "float32")

SEMAPHORES = ["qv", "qs", "qp", "qg", "ld0", "ldv", "ldt", "ldc", "h1a", "h1b", "sent", "xa0", "xa1", "dv0",
              "ha0", "ha1", "out0", "out1"]
for _t in range(STEPS):
    SEMAPHORES += [_n + "_%d" % _t for _n in ("ka1", "ka2", "kb0", "kb2", "ke", "fa1")]


def banks(o):
    return set(n[1] for n in o["r"] + o["w"] if n[0] == "#")


def hazards(o, k, writer, readers):
    deps = set(writer[r] for r in o["r"] if r in writer)
    for w in o["w"]:
        if w in writer:
            deps.add(writer[w])
        deps.update(readers.get(w, []))
    for r in o["r"]:
        if o["inc"]:
            readers.setdefault(r, []).append(k)
    for w in o["w"]:
        writer[w] = k
        readers[w] = []
    deps.discard(k)
    return deps


def schedule(progs):
    ops, pred, sender = [], [], {}
    for role, prog in enumerate(progs):
        writer, readers, fixed = {}, {}, {}
        for o in prog:
            k = len(ops)
            ops.append((role, o))
            p = {d: (WAKE if ops[d][1]["e"] != o["e"] else 0.0 if o["e"] == "p" else SELF)
                 for d in hazards(o, k, writer, readers)}
            line = o["e"] if o["e"] in "gy" or not o["inc"] else o["line"]
            if line:
                if line in fixed:
                    p.setdefault(fixed[line], 0.0)
                fixed[line] = k
            pred.append(p)
            for s, lat, rows in o["out"]:
                sender[role, s] = (k, lat)
    base = [0.0] * len(ops)
    for k, (role, o) in enumerate(ops):
        for s, v, frm in o["x"]:
            if s in AT:
                base[k] = max(base[k], AT[s])
            else:
                d, lat = sender[frm, s]
                pred[k][d] = lat
    prio = [o["c"] + o["tail"] for role, o in ops]
    moved = True
    while moved:
        moved = False
        for k in range(len(ops) - 1, -1, -1):
            for d, lat in pred[k].items():
                v = prio[k] + lat + ops[d][1]["c"]
                if v > prio[d] + 1e-9:
                    prio[d], moved = v, True
    prio = [p - o["pen"] for p, (role, o) in zip(prio, ops)]
    succ = [[] for _ in ops]
    for k, p in enumerate(pred):
        for d in p:
            succ[d].append(k)
    bk = [banks(o) for role, o in ops]

    def one_round():
        left = [len(p) for p in pred]
        ready, free, bank, end, late, held, order = {}, {}, {}, {}, {}, {}, [[] for _ in progs]
        for k, (role, o) in enumerate(ops):
            if not left[k]:
                ready.setdefault((role, o["e"]), []).append(k)

        def start(k):
            role, o = ops[k]
            t = [(base[k], -1), free.get((role, o["e"]), (0.0, -1))]
            t += [(end[d] + lat + late.get(d, 0.0) * (lat > HOP), d) for d, lat in pred[k].items()]
            t += [(t2 + WAKE, d) for b in bk[k] for e2, (t2, d) in bank.get((role, b), {}).items() if e2 != o["e"]]
            return max(t)

        while True:
            pick = None
            for q, cand in ready.items():
                if cand:
                    st = {k: start(k)[0] for k in cand}
                    t0 = min(st.values())
                    if pick is None or t0 < pick[0]:
                        pick = (t0, q, st)
            if pick is None:
                break
            t0, q, st = pick
            top = max((k for k in st if st[k] <= t0 + LOOK), key=lambda k: (prio[k], -k))
            if st[top] > t0 + 0.02:
                fit = [k for k in st if st[k] + ops[k][1]["c"] <= st[top] + TOL]
                now = max((k for k in st if st[k] <= t0 + 0.02), key=lambda k: (prio[k], -k))
                if fit:
                    top = max(fit, key=lambda k: (prio[k], -k))
                elif st[top] - t0 >= BETA * ops[now][1]["c"]:
                    top = now
            role, o = ops[top]
            held[top] = start(top)[1]
            end[top] = st[top] + o["c"]
            free[q] = (end[top], top)
            if o["out"]:
                late[top] = max(0.0, free.get((role, "d"), 0.0) - end[top])
                free[role, "d"] = end[top] + late[top] + max(rows for s, lat, rows in o["out"])
            for b in bk[top]:
                bank.setdefault((role, b), {})[o["e"]] = (end[top], top)
            ready[q].remove(top)
            order[role].append(o)
            for k in succ[top]:
                left[k] -= 1
                if not left[k]:
                    ready.setdefault((ops[k][0], ops[k][1]["e"]), []).append(k)
        span, k = max((end[k] + o["tail"], k) for k, (role, o) in enumerate(ops) if o["tail"] < 99)
        return span, order, k, held

    best = None
    for n in range(ROUNDS + 1):
        span, order, k, held = one_round()
        if best is None or span < best[0]:
            best = (span, order)
        waits = []
        while held[k] >= 0:
            if held[k] not in pred[k]:
                waits.append((k, held[k]))
            k = held[k]
        for k, d in waits[n % 3::3]:
            prio[k] += NUDGE
            prio[d] -= NUDGE
    return best[1]


def emit(g, T, ops):
    queue = {"v": g.vector, "s": g.scalar, "p": g.tensor, "g": g, "y": g.sync}
    semof = {"v": T.sem.qv, "s": T.sem.qs, "p": T.sem.qp, "g": T.sem.qg}
    writer, readers, bank = {}, {}, {}
    known = {e: {} for e in queue}
    clock, waits, needed = [], [], set()
    for k, o in enumerate(ops):
        e = o["e"]
        deps = hazards(o, k, writer, readers)
        for b in banks(o):
            deps.update(k2 for e2, k2 in bank.get(b, {}).items() if e2 != e)
            bank.setdefault(b, {})[e] = k
        kn = known[e]
        mine = []
        for d in sorted(deps, reverse=True):
            e2 = ops[d]["e"]
            if (e2 == "p" and e == "p") or kn.get("@" + e2, -1) >= d:
                continue
            mine.append(("@", d))
            needed.add(d)
            for key, val in clock[d].items():
                if kn.get(key, -1) < val:
                    kn[key] = val
        for s, v, frm in o["x"]:
            if kn.get(s, 0) < v:
                mine.append((s, v))
                kn[s] = v
        c = dict(kn)
        if o["inc"]:
            c["@" + e] = k
        clock.append(c)
        waits.append(mine)
    count, n = {}, {e: 0 for e in queue}
    for k, o in enumerate(ops):
        if k in needed:
            n[o["e"]] += 1
            count[k] = n[o["e"]]
    for k, o in enumerate(ops):
        q = queue[o["e"]]
        for s, v in waits[k]:
            if s == "@":
                q.wait_ge(semof[ops[v]["e"]], count[v])
            else:
                q.wait_ge(T.sem[s], v)
        ins = o["f"](q)
        if k in needed:
            ins.then_inc(semof[o["e"]], 1)


def engine_sets(topo, src, dsts):
    open_to = [topo.engines(src, d) for d in dsts]
    order = sorted(range(len(dsts)), key=lambda i: len(open_to[i]))
    res, used = [None] * len(dsts), []
    for pos, i in enumerate(order):
        free = [e for e in open_to[i] if e not in used]
        rivals = len([j for j in order[pos:] if len(open_to[j]) == len(open_to[i])])
        share = len(free) // rivals
        n = 1
        while 2 * n <= share:
            n *= 2
        res[i] = free[:n]
        used += res[i]
    return res


def role_of(T, topo, rank):
    return 0 if topo.chip(T.cores[rank % NR]) == topo.chip(T.cores[(rank + 1) % NR]) else 1


def program(T, topo, rank):
    ops = []
    sent = [0]

    def peer(k, of=rank):
        return T.cores[(of + k) % NR]

    def op(e, f, r=(), w=(), x=(), c=0.0, inc=True, out=(), tail=0.0):
        x = [(s[0], s[1], role_of(T, topo, rank + s[2]) if len(s) > 2 else 0) for s in x]
        r, w = [[m for n in names for m in ([n + "<", n + ">"] if n.startswith(HALVED) and n[-1] not in "<>" else [n])]
                for names in (r, w)]
        ops.append({"e": e, "f": f, "r": r, "w": w, "x": x, "c": c, "inc": inc, "out": out, "tail": tail,
                    "line": None, "pen": 0.0})

    def cost(n):
        return OVH + max(64, n) * CY

    def ts(out, in0, s1, s2, o0, o1, r, w, x=(), n=128):
        op("v", lambda q: q.tensor_scalar(out, in0, s1, s2, o0, o1), r, w, x, cost(n))

    def t1(out, in0, s1, o0, r, w, x=(), n=128):
        op("v", lambda q: q.tensor_scalar(out, in0, s1, None, o0), r, w, x, cost(n))

    def tt(out, a, c, o, r, w, x=(), n=128):
        op("v", lambda q: q.tensor_tensor(out, a, c, o), r, w, x, cost(n))

    def cp(out, a, r, w, x=(), n=128):
        op("v", lambda q: q.tensor_copy(out, a), r, w, x, cost(n))

    def fill(out, v, w):
        op("v", lambda q: q.memset(out, v), (), w, (), cost(64))

    def scan(out, d0, d1, init, o0, o1, r, w, n=128):
        op("v", lambda q: q.tensor_tensor_scan(out, d0, d1, init, o0, o1), r, w, (), cost(n))

    def cut(on):
        return [(slice(0, 64), "<", 64), (slice(64, 128), ">", 64)] if on else [(slice(0, 128), "", 128)]

    def act(out, a, fn, r, w, x=(), bias=None, scale=None, n=128):
        kw = {}
        if bias is not None:
            kw["bias"] = bias
        if scale is not None:
            kw["scale"] = scale
        op("s", lambda q: q.activation(out, a, fn, **kw), r, w, x, OVS + cost(n))

    def mms(groups, r, w, n, x=(), start=True, stop=True):
        def f(q):
            for out, terms in groups:
                for i, (l, rh) in enumerate(terms):
                    ins = q.matmul(out, l, rh, start and i == 0, stop and i == len(terms) - 1)
            return ins
        state = ["G" + b for b in set(s[1] for s in w)]
        r, w = (r + state, w) if start and stop else (r, w + state)
        op("p", f, r, w, x, n * PEC)
        ops[-1]["n"] = (n, sum(len(t) for o, t in groups))

    def mm(out, terms, r, w, x=(), n=0, **kw):
        mms([(out, terms)], r, w, n or 128 * len(terms), x, **kw)

    def dma(e, out, a, sem, r=(), x=(), tail=0.0):
        op(e, lambda q: q.dma_start(out, a).then_inc(T.sem[sem], 16), r, (), x, 0.06, False, (), tail)

    def iota(out, pattern, base, step, w, c=0.4):
        op("g", lambda q: q.iota(out, pattern, base, step), (), w, c=c)

    def plan(src_rank, offs):
        return engine_sets(topo, peer(0, src_rank), [peer(k, src_rank) for k in offs])

    def send(items, nbytes, r, x=(), first=0.0):
        trs, out = [], []
        for (k, src, dst, sem), es in zip(items, plan(rank, [it[0] for it in items])):
            rows = 128 / len(es) * (ROW + nbytes / RATE)
            rid, pid, _ = topo.addr(peer(k))
            trs.append(RemoteDMATransfer(dst_ids=[DstId(rid=rid, pnc=pid)], dma_engine_mask=sum(1 << e for e in es),
                                         remote_sem=T.sem[sem], src=src, dst=dst))
            sent[0] += len(es)
            out.append((sem, HOP + rows, rows))
        op("g", lambda q: q.remote_dma_fused(trs, local_sem=T.sem.sent), r, (), x, CALL + first, False, out)

    def arrival(sem, k, offs):
        return (sem, len(plan(rank + k, offs)[offs.index(-k)]), k)

    PB = [T["PB%d" % b] for b in range(8)]
    X, COL, ID = T.X, T.COL, T.ID
    YY, MM, KK = [T.Y0, T.Y1], [T.M0, T.M1], [T.KA, T.KB]
    xcol = [8, 144, 272]
    tgc = [X[:, 7:8], X[:, 143:144], T.IN0[:, 7:8]]
    role = role_of(T, topo, rank)
    E, Z = (1, 0) if role == 0 else (0, 1)

    def sl(buf, d, n=128):
        return buf[:, d * n:(d + 1) * n]

    def col(k):
        return COL[:, k:k + 1]

    def ps(b, s):
        return "#%d%d" % (b, s)

    def slot(b, s):
        return sl(PB[b], s), ps(b, s)

    def xs(d):
        return X[:, xcol[d]:xcol[d] + 128]

    def xext(d):
        return [("ld0", 32)] if d == 2 else [arrival("xa%d" % d, -1 - d, [1, 2])]

    def key_offs(d, t):
        if t == STEPS - 1:
            return [-1 - d]
        return [1, -1] if d == 0 else [-1, -2]

    def kext(d, t, j):
        s = [[None, ("kb0", 1)], [("ka1", -1), None], [("ka2", 1), ("kb2", 2)]][d][j]
        if s and both_off(rank + s[1], j, t):
            return [("ke_%d" % t, len(plan(rank + s[1], key_offs(j, t)[:1])[0]), s[1])]
        return [] if s is None else [arrival("%s_%d" % (s[0], t), s[1], key_offs(j, t))]

    def both_off(r, j, t):
        return len([k for k in key_offs(j, t) if topo.chip(peer(k, r)) != topo.chip(peer(0, r))]) > 1

    def fmsg(d, t, lo, hi):
        o = FW * (2 * t + d)
        return T.FB[:, o + lo:o + hi]

    def fext(d, t):
        return [arrival("fa1_%d" % t, -1, [1])] if d else []

    dma("y", T.IN0[:, 8:136], T.x0[:], "ld0")
    dma("s", T.IN0[:, 7:8], T.tg[:], "ld0", tail=999.0)
    dma("s", T.TEI[:, 0:1], T.te[:], "ldt", tail=999.0)
    dma("s", T.CNI[:, 0:1], T.cn[:], "ldc", tail=999.0)
    dma("s", T.DVS[:, 8:392], T.dv[:], "ldv", tail=999.0)
    dma("y", T.H1[:, 0:HEAD], T.hs[:, 0:HEAD], "h1a")
    iota(T.PI[:, 0:1], [[0, 1]], 0, 1, ["PI0"], 0.14)
    iota(T.KI[:], [[1, 128]], 0, 0, ["KI"])
    iota(T.RI[:], [[0, 16], [1, 8]], 0, -1, ["RI"])
    iota(T.CI[:], [[-97, 16], [80, 8]], 97 * 15, 0, ["CI"])
    send([(1, T.IN0[:, 7:136], X[:, 7:136], "xa0"), (2, T.IN0[:, 7:136], X[:, 143:272], "xa1")], 258, (), [("ld0", 32)], 1.0)
    dma("y", T.H1[:, HEAD:16 * RING], T.hs[:, HEAD:16 * RING], "h1b", x=[("ld0", 32)])

    cp(col(0), T.PI[:, 0:1], ["PI0"], ["c0"], n=1)
    t1(T.PI[:, 1:2], T.PI[:, 0:1], 4, ALU.arith_shift_right, ["PI0"], ["PI1"], n=1)
    t1(T.PI[:, 2:3], T.PI[:, 0:1], 15, ALU.bitwise_and, ["PI0"], ["PI2"], n=1)
    cp(COL[:, 1:3], T.PI[:, 1:3], ["PI1", "PI2"], ["c1", "c2"], n=2)
    t1(T.TE2[:, 0:1], T.TEI[:, 0:1], col(2), ALU.add, ["c2"], ["TE20"], [("ldt", 16)], 1)
    t1(T.TE2[:, 1:2], T.TE2[:, 0:1], 4, ALU.arith_shift_right, ["TE20"], ["TE21"], n=1)
    cp(T.DVS[:, 7:8], T.TE2[:, 1:2], ["TE21"], ["DVS"], n=1)
    for k, src, v, o in ((4, 0, 8.0, ALU.is_lt), (5, 0, 32.0, ALU.is_ge), (6, 2, float(RING), ALU.mult)):
        t1(col(k), T.PI[:, src:src + 1], v, o, ["PI%d" % src], ["c%d" % k], n=1)
    ts(col(11), col(2), 15.0, col(2), ALU.is_lt, ALU.mult, ["c2"], ["c11"], n=1)
    ts(col(3), col(11), 64.0, R64, ALU.mult, ALU.add, ["c11"], ["c3"], n=1)
    t1(T.TI1[:], T.KI[:], col(0), ALU.subtract, ["KI", "c0"], ["TI1"])
    t1(T.TI2[:], T.KI[:], 4, ALU.arith_shift_right, ["KI"], ["TI2"])
    t1(T.TI3[:], T.KI[:], 15, ALU.bitwise_and, ["KI"], ["TI3"])
    t1(ID[:], T.TI1[:], 0.0, ALU.is_equal, ["TI1"], ["ID"])
    t1(T.BB[:], T.TI2[:], col(1), ALU.is_equal, ["TI2", "c1"], ["BB"])
    t1(T.RI[:], T.RI[:], 7, ALU.bitwise_and, ["RI"], ["RI"])
    ts(T.RF[:], T.RI[:], 0.0, col(4), ALU.is_equal, ALU.mult, ["RI", "c4"], ["RF"])
    cp(T.RF[64:65, :], T.CI[64:65, :], ["CI"], ["RF"])
    fill(T.RF[96:97, :], 1.0, ["RF"])
    ts(T.RG[:], T.RI[:], 0.0, col(5), ALU.is_equal, ALU.mult, ["RI", "c5"], ["RG"])
    if "s" in EASE:
        t1(T.RH[:], T.RF[:], col(5), ALU.mult, ["RF", "c5"], ["RH"], n=64)
        cp(T.RF4[0:32, :], T.RF[0:32, :], ["RF"], ["RF4"])
    ts(T.RB[:], T.RI[:], 0.0, 2.0 ** -12, ALU.is_equal, ALU.mult, ["RI"], ["RB"])
    cp(T.BS[:, 0:8], T.BB[:, 0:128:16], ["BB"], ["BS0"], n=8)
    fill(T.ONE[:], 1.0, ["ONE"])
    fill(T.ZW[:], 0.0, ["IX0", "IX1"])
    fill(T.CAP[:], 8 * BIG, ["CAP"])
    fill(T.CAP[:, 0:128], 128.0, ["CAP"])
    for d in (0, 1):
        t1(sl(T.T2, d), T.ONE[:], 0.0, ALU.mult, ["ONE"], ["T2S%d" % d, "T2C%d" % d, "T2D%d" % d], n=64)
        cp(T.T2[64:65, 128 * d:128 * d + 128], T.ONE[64:65, :], ["ONE"], ["T2C%d" % d], n=64)
        t1(T.T2[96:97, 128 * d:128 * d + 128], T.TI3[96:97, :], 5.0, ALU.mult, ["TI3"], ["T2D%d" % d])
        fill(PB[2 + d][0:32, 256:384], 256.0, [ps(2 + d, 2)])
    t1(T.BS[:, 8:16], T.BS[:, 0:8], 4096.0, ALU.mult, ["BS0"], ["BSP"], n=8)
    t1(T.BS[:, 16:24], T.BS[:, 0:8], -2048.0, ALU.mult, ["BS0"], ["BSN"], n=8)
    t1(T.RNB[:], T.BS[:, 0:8], col(6), ALU.mult, ["BS0", "c6"], ["RNB"], n=8)
    t1(T.CB[:], T.KI[:, 0:8], 0.125, ALU.mult, ["KI"], ["CB"], n=8)
    ts(T.CK[:], T.TI3[:], 15.0, -15.5 / 128, ALU.is_equal, ALU.mult, ["TI3"], ["CK"])
    t1(T.CK[:], T.CK[:], -31.5 / 128, ALU.add, ["CK"], ["CK"], n=64)
    cp(T.BR[:], T.BB[:], ["BB"], ["BR"], n=64)
    t1(T.BR[:, 15:128:16], T.BB[:, 15:128:16], 1.0 / 64, ALU.mult, ["BB"], ["BR"], n=8)
    fill(T.C16[:], 16.0, ["C16"])
    t1(T.TG[:], T.ONE[:], tgc[2], ALU.mult, ["ONE"], ["TG"], xext(2), 64)
    mats = [("IDN", "ID", -1.0), ("IDW", "ID", -2048.0), ("ID2", "ID", 2.0), ("BN", "BB", -1.0), ("B1024", "BB", 1024.0),
            ("BN512", "BB", -512.0), ("IDBIG", "ID", 16384.0), ("BRN", "BR", -1.0), ("BR2", "BR", 2.0), ("IH", "ID", 1.0),
            ("IDN64", "ID", -64.0), ("IDO", "ID", OVER / 2.0)] + [("IDH", "ID", 0.5), ("IDHN", "ID", -0.5)] * ("s" in TEST)
    for buf, src, v in mats:
        t1(T[buf][:], T[src][:], v, ALU.mult, [src], [buf], n=64)
    if "p" in BEST:
        cp(T.IDF[:], ID[:], ["ID"], ["IDF"])
        ts(T.REP[0:32, :], T.TI2[0:32, :], COL[0:32, 0:1], 0.25, ALU.is_equal, ALU.mult, ["TI2", "c0"], ["REP"])
    t1(T.RS[:], T.TI3[:], 0.0, ALU.is_gt, ["TI3"], ["RS"])
    ts(T.D0[:], T.RS[:], float(2 ** 25 + 64), -float(2 ** 25), ALU.mult, ALU.add, ["RS"], ["D0"])
    ts(T.D1[:], T.RS[:], float(2 ** 25), -float(2 ** 25), ALU.mult, ALU.add, ["RS"], ["D1"])
    t1(T.RN[:, 127:128], T.CNI[:, 0:1], -256.0, ALU.add, [], ["nm0"], [("ldc", 16)], 1)
    t1(T.TI4[:], T.TI1[:], 15, ALU.bitwise_and, ["TI1"], ["TI4"])
    t1(T.RN[:, 128:136], T.BS[:, 0:8], T.RN[:, 127:128], ALU.mult, ["BS0", "nm0"], ["RN0"], n=8)
    fill(T.MK[:], 0.0, ["MK"])
    ts(T.MK[:, 1:9], T.BS[:, 0:8], -BIG, BIG, ALU.mult, ALU.add, ["BS0"], ["MK"], n=8)
    tt(T.EQ[:, 384:393], T.MK[:, 1:10], T.MK[:, 0:9], ALU.subtract, ["MK"], ["EQX"], n=18)
    fill(T.EQ[:, 393:394], 256.0, ["EQX"])
    t1(col(8), col(4), -7 * BIG, ALU.mult, ["c4"], ["c8"], n=1)
    t1(T.BK[:], T.BB[:], col(6), ALU.mult, ["BB", "c6"], ["BK"], n=64)
    t1(T.MA[:], T.TI4[:], 0.0, ALU.is_equal, ["TI4"], ["MA"])
    later = [o for o in ops if o["w"] and o["w"][0] in LATER]
    ops[:] = [o for o in ops if o not in later]

    def finish(d, t):
        a = [sl(K, 3 * t + d) for K in KK]
        mi, xi = sl(T.MI, d), sl(T.XI, d)
        if d < 2:
            p, pn = slot(d, 2)
            act(p, a[d], ACT.Copy, ["key%d_%d" % (d, t)], [pn])
        for c, h, n in cut("f" in CUT if d == 2 else "F" in CUT):
            if d == 2:
                tt(mi[:, c], a[0][:, c], a[1][:, c], ALU.max, [], ["MI2" + h], kext(d, t, 0) + kext(d, t, 1), 2 * n)
            else:
                tt(mi[:, c], a[1 - d][:, c], p[:, c], ALU.max, [pn], ["MI%d" % d + h], kext(d, t, 1 - d), n)
            t1(xi[:, c], mi[:, c], 255, ALU.bitwise_and, ["MI%d" % d + h], ["XI%d" % d + h], n=n)
            cp(xs(d)[:, c], xi[:, c], ["XI%d" % d + h], ["X%d" % d + h], n=n)
            if d == 2:
                t1(sl(T.AX, d)[:, c], xi[:, c], tgc[d], ALU.max, ["XI2" + h], ["AX2" + h], n=n)

    def ring(d, t=1):
        u, un = slot(6, 0) if d == 2 else slot(d, 3)
        if d == 2:
            mm(u, [(T.CK[:], T.ONE[:]), (T.BRN[:], T.TG[:])], ["CK", "ONE", "BRN", "TG"], [un], stop=False)
            mm(u, [(T.BRN[:], xs(d)), (T.BR2[:], sl(T.AX, d))], ["BRN", "BR2", "X2", "AX2"], [un], start=False)
        else:
            act(sl(T.AX, d), xs(d), ACT.Abs, ["X%d" % d], ["AX%d" % d], xext(d), tgc[d], -1.0)
            if t and "r" in EASE:
                mm(u, [(T.BB[:], sl(T.AX, d))], ["BB", "AX%d" % d], [un])
                act(sl(T.KQ, d), u, ACT.Identity, [un], ["KQ%d" % d], bias=MAGIC, scale=1.0 / 64)
                return ts(sl(T.EQ, d), sl(T.KQ, d), 144.0, col(7), ALU.min, ALU.is_equal, ["KQ%d" % d, "c7"], ["EQ%d" % d], n=64)
            mm(u, [(T.CK[:], T.ONE[:]), (T.BR[:], sl(T.AX, d))], ["CK", "ONE", "BR", "AX%d" % d], [un])
        for c, h, n in cut(d == 2 and "e" in CUT):
            ts(sl(T.EQ, d)[:, c], u[:, c], R64, col(3), ALU.add, ALU.is_equal, [un, "c3"], ["EQ%d" % d + h], n=n)

    def hashes(d, t):
        b, o, xo = 4 + d, 128 * d, xcol[d]
        a0, n0 = PB[b], ps(b, 0)
        mms([(a0[0:8, a:128:16], [(X[:, xo + a:xo + 128:16], T.BS[:, 0:8])]) for a in range(16)], ["X%d" % d, "BS0"], [n0], 128)
        if "s" in EASE:
            act(T.T4[0:8, o:o + 128], a0[0:8, 0:128], ACT.Identity, [n0], ["T4%d" % d], bias=-2048.0)
        else:
            t1(T.T2[0:8, o:o + 128], a0[0:8, 0:128], -2048.0, ALU.add, [n0], ["T2S%d" % d])
        mix(d, t, d, sl(T.HI, d), "HI%d" % d)

    def mix(d, t, k, hi, name):
        b = 4 + d
        u, un = slot(b, 1)
        c0 = 2048.0 + 31.0 * t + 97.0 * 16 * d
        terms, r = [(T.T2[0:97, 128 * k:128 * k + 128], T.RF[0:97, :])], ["T2S%d" % k, "T2C%d" % k, "T2D%d" % k, "RF"]
        n = 128
        if t and "s" in EASE:
            terms = [(T.T2[0:97, 0:128], T.RH[0:97, :]), (T.T4[0:8, 128 * k:128 * k + 128], T.RF4[0:8, :])]
            r, n = ["T2C0", "T2D0", "RH", "RF4", "T4%d" % k], 640
        mm(u, terms, r, [un], n=n)
        if WRAP[2 * min(t, 1) + (d != E)] == "a":
            t1(sl(T.PP, d), u, c0, ALU.add, [un], ["PP%d" % d])
            t1(hi, sl(T.PP, d), 4095, ALU.bitwise_and, ["PP%d" % d], [name])
            t1(u, hi, 128.0, ALU.add, [name], [un])
            tt(sl(T.PP, d), hi, u, ALU.mult, [name, un], ["PP%d" % d])
        else:
            act(sl(T.SB, d), u, ACT.Sign, [un], ["SB%d" % d], bias=c0 - 4095.5)
            u, un = slot(b, 3)
            mm(u, terms + [(T.IDW[:], sl(T.SB, d))], r + ["IDW", "SB%d" % d], [un], n=n + 128)
            act(sl(T.SQ, d), u, ACT.Square, [un], ["SQ%d" % d], bias=c0 - 2048.0 + 64.0)
            t1(sl(T.PP, d), sl(T.SQ, d), -4096.0, ALU.add, ["SQ%d" % d], ["PP%d" % d])
        ts(hi, sl(T.PP, d), 7, 4095, ALU.arith_shift_right, ALU.bitwise_and, ["PP%d" % d], [name])

    def first_hashes():
        mms([(PB[6][0:8, a:128:16], [(T.IN0[:, 8 + a:136:16], T.BS[:, 0:8])]) for a in range(16)], ["BS0"], ["#60"], 128, xext(2))
        t1(T.T2[0:8, 0:128], PB[6][0:8, 0:128], -2048.0, ALU.add, ["#60"], ["T2S0"])
        for d in (0, 1):
            mix(d, 0, 0, sl(T.HS, d), "HS%d" % d)
        send([(1 + d, sl(T.HS, d), sl(T.HI, d), "ha%d" % d) for d in (0, 1)], 512, ["HS0", "HS1"])

    def xrep(d):
        ks = range(XR // 128)
        mms([(sl(PB[d], k), [(ID[:], xs(d))]) for k in ks], ["ID", "X%d" % d], [ps(d, k) for k in ks], XR, xext(d))

    def places(d, t):
        o, b = 128 * d, 2 + (d != E)
        (a, an), (p, pn), cn = slot(b, 3), slot(6 + (d != E), 3), ps(b, 2)
        for rows, rhs, name in ((slice(32, 40), T.RNB[:], "RNB"), (slice(0, 8), T.RN[:, 144 * t + 128:144 * t + 136], "RN%d" % t)):
            mms([(PB[b][rows, 256 + k:384:16], [(T.EQ[:, o + k:o + 128:16], rhs)]) for k in range(16)], ["EQ%d" % d, name], [cn], 128)
        if "nN"[d != E] in ONS:
            t1(T.T2N[0:40, o:o + 128], PB[b][0:40, 256:384], COL[0:40, 8:9] if t else 0.0, ALU.add, [cn, "c8"][:1 + min(t, 1)],
               ["T2N%d" % d])
        elif t:
            act(T.T2N[0:40, o:o + 128], PB[b][0:40, 256:384], ACT.Identity, [cn, "c8"], ["T2N%d" % d], bias=COL[0:40, 8:9])
        else:
            act(T.T2N[0:40, o:o + 128], PB[b][0:40, 256:384], ACT.Copy, [cn], ["T2N%d" % d])
        mm(a, [(T.T2N[0:16, o:o + 128], T.RB[0:16, :])], ["RB", "T2N%d" % d], [an])
        mm(p, [(T.T2N[0:40, o:o + 128], T.RG[0:40, :])], ["T2N%d" % d, "RG"], [pn], stop=False)
        on = "pP"[d != E] in CUT
        for c, h, n in cut(on):
            tt(sl(T.AI, d)[:, c], sl(T.HI, d)[:, c], a[:, c], ALU.mult, ["HI%d" % d, an], ["AI%d" % d + h],
               [] if t else [arrival("ha%d" % d, -1 - d, [1, 2])], n)
            t1(sl(T.PL, d)[:, c], sl(T.AI, d)[:, c], 1023.5 + EPS, ALU.add, ["AI%d" % d + h], ["PL%d" % d + h], n=n)
        lift = OVER / 2.0 if t else 0.0
        if t and "dD"[d != E] in ONS:
            ts(sl(T.SD, d), sl(T.AI, d), float(RING), 2.0, ALU.is_ge, ALU.mult, ["AI%d" % d], ["SD%d" % d])
            lift = 0.0
        elif t:
            act(sl(T.SD, d), sl(T.AI, d), ACT.Sign, ["AI%d" % d], ["SD%d" % d], bias=EPS - RING)
        mm(p, [(T.IH[:], sl(T.PL, d))], ["IH", "PL%d" % d], [pn], start=False, stop=t == 0)
        if t:
            mm(p, [(T.IDO[:], sl(T.SD, d))], ["IDO", "SD%d" % d], [pn], start=False)
        for c, h, n in cut(on):
            t1(sl(T.OFF, d)[:, c], p[:, c], lift - 1024.0, ALU.add, [pn], ["OFF%d" % d + h], n=n)

    def tmat(d):
        ts(sl(T.BT, d), T.BB[:], fmsg(d, 0, 256, 257), -1.0, ALU.mult, ALU.mult, ["BB", "TP%d" % d], ["BT%d" % d], fext(d, 0), 64)

    def fallback(d, t):
        b, o, xn = 4 + d, 392 * d, "X%d" % d
        (a, an), (c, cn), (e, en) = slot(b, 1), slot(b, 2), slot(b, 3)
        x, m, ext = xs(d), fmsg(d, t, 128, 256), [arrival("dv0", -1, [1])]
        if t == 0:
            cp(fmsg(d, 0, 256, 257), T.DVL[:, o + 7:o + 8], [], ["TP%d" % d], ext, 1)
            tmat(d)
        o += 8 + 128 * t
        mm(a, [(T.BB[:], x)], ["BB", xn, "HI%d" % d], [an], xext(d))
        if "f" in ONS:
            ts(sl(T.TQ, d), a, 1.0 / 64, MAGIC, ALU.mult, ALU.add, [an], ["TQ%d" % d])
        else:
            act(sl(T.TQ, d), a, ACT.Identity, [an], ["TQ%d" % d], bias=MAGIC, scale=1.0 / 64)
        mm(e, [(T.BB[:], x), (T.IDN64[:], sl(T.TQ, d))], ["BB", xn, "IDN64", "TQ%d" % d], [en])
        mm(c, [(ID[:], x), (T.IDN[:], T.DVL[:, o:o + 128])], ["ID", "IDN", xn, "HI%d" % d], [cn], xext(d) + ext)
        if "f" in ONS:
            t1(m, e, 129.0 * 64, ALU.add, [en], ["SM%d%d" % (d, t)])
        else:
            act(m, e, ACT.Identity, [en], ["SM%d%d" % (d, t)], bias=129.0 * 64)
        act(sl(T.ZZ, d), c, ACT.Abs, [cn], ["ZZ%d" % d])
        act(sl(T.AZ, d), sl(T.ZZ, d), ACT.Abs, ["ZZ%d" % d], ["AZ%d" % d], bias=tgc[d], scale=-1.0)
        mm(a, [(ID[:], sl(T.ZZ, d)), (T.IDN[:], x)], ["ID", "IDN", "ZZ%d" % d, xn], [an])
        mm(c, [(T.BN[:], sl(T.AX, d)), (sl(T.BT, d), m), (T.BB[:], sl(T.AZ, d))],
           ["BB", "BN", "AX%d" % d, "AZ%d" % d, "BT%d" % d, "SM%d%d" % (d, t)], [cn])
        t1(sl(T.OKZ, d), c, 0.0, ALU.is_le, [cn], ["OKZ%d" % d])
        tt(fmsg(d, t, 0, 128), a, sl(T.OKZ, d), ALU.mult, [an, "OKZ%d" % d], ["MZ%d%d" % (d, t)])

    def tell(d, t):
        n = 256 if t else 257
        send([(1 - 2 * d, fmsg(d, t, 0, n), fmsg(1 - d, t, 0, n), "fa%d_%d" % (1 - d, t))], 2 * n,
             ["MZ%d%d" % (d, t), "SM%d%d" % (d, t), "TP%d" % d])
        ops[-1]["out"] = [(s, lat + MARGIN, rows) for s, lat, rows in ops[-1]["out"]]

    def job(d, t):
        second = 0 if d == E else 1
        b = 2 + second
        win = T.H1[:, :] if t else T.H1[:, 0:16 * RING]
        o, ys, ms = 0, ["BOFF%d" % d], ["BOFF%d" % d]
        for k, n in enumerate(BLOCKS[second]):
            src = win.indirect(T.OFF[:, 128 * d + o // 16:128 * d + (o + n) // 16])
            r, w, ex = ["OFF%d" % d + "<" * (o + n <= 1024) + ">" * (o >= 1024), "H"], ["Y%d_%d" % (d, k)], [("h1a", 16), ("h1b", 16)]
            if (second, k) in (ONV[role] if t else ONV[role][FIRST:]):
                cp(YY[d][:, o:o + n], src, r, w, ex, 50 + n * GAT)
            else:
                act(YY[d][:, o:o + n], src, ACT.Copy, r, w, ex, n=65 + n * GAT)
                ops[-1]["line"] = "Y"
            ops[-1]["pen"] = PEN
            ys += w
            for u in range(o, o + n, XR):
                m, c = "M%d_%d" % (d, u // 128), min(XR, o + n - u)
                ms.append(m)
                tt(MM[d][:, u:u + c], YY[d][:, u:u + c], PB[d][:, 0:c], ALU.max, w + [ps(d, s) for s in range(XR // 128)], [m], n=c)
                ops[-1]["pen"] = PEN
                mms([(PB[b][:, 15 - pos:128:16], [(sl(YY[d], pos), T.BS[:, 16:24]), (sl(MM[d], pos), T.BS[:, 8:16])])
                     for pos in range(u // 128, (u + c) // 128)], w + [m, "BSP", "BSN"], [ps(b, 0)], c)
            o += n
        off, o, z = sl(T.BOFF, d, 8), 128 * d, 144 * d
        key, mark = sl(KK[d], 3 * t + d), len(ops)
        (cm, cn), (df, dfn), (kd, kn) = slot(4 + d, 2), slot(d, 3), slot(6 + second, 3)
        x, mz, r = xs(d), fmsg(d, t, 0, 128), ["ID", "IDN", "IDH", "IDHN", "X%d" % d, "MZ%d%d" % (d, t)]
        sign = int(TEST[second] == "s")
        one, neg = (T.IDH[:], T.IDHN[:]) if sign else (ID[:], T.IDN[:])
        def bound():
            mm(cm, [(T.BN[:], sl(T.AX, d)), (sl(T.BT, d), fmsg(d, t, 128, 256))],
               ["BN", "AX%d" % d, "BT%d" % d, "SM%d%d" % (d, t)], [cn], fext(d, t), stop=False)

        if BEST[second] != "p":
            bound()
        mm(kd, [(T.BB[:], T.C16[:])][d:] + [(one, x), (one, mz)], r + ["BB", "C16"], [kn], fext(d, t), stop=False)
        scan(sl(T.S1, d), T.D0[:], PB[b][:, 0:128], 0.0, ALU.add, ALU.max, ["D0", ps(b, 0)], ["S1%d" % d])
        scan(sl(T.S2, d), T.D1[:], PB[b][:, 0:128], 0.0, ALU.add, ALU.max, ["D1", ps(b, 0)], ["S2%d" % d])
        ix = T.ZW[:, z + 15:z + 143:16]
        tt(ix, T.S1[:, o + 15:o + 128:16], T.S2[:, o + 15:o + 128:16], ALU.subtract, ["S1%d" % d, "S2%d" % d], ["IX%d" % d], n=16)
        if TURN[second] == "z":
            terms = [(T.ONE[:], T.CB[:])] + [(T.ZW[:, z + 15 - a:z + 143 - a], T.ID2[:, a:128:16]) for a in range(16)]
            step = 17 if second else 5
            for a in range(0, 17, step):
                mm(PB[b][:, 0:8], terms[a:a + step], ["ONE", "CB", "ID2", "IX%d" % d], [ps(b, 0)], n=64 * len(terms[a:a + step]),
                   start=a == 0, stop=a + step >= 17)
        else:
            mms([(PB[d][0:8, a:128:16], [(T.ID2[:, a:128:16], ix)]) for a in range(16)], ["ID2", "IX%d" % d], [ps(d, 0)], 128)
            t1(T.TT[0:8, o:o + 128], PB[d][0:8, 0:128], COL[0:8, 7:8], ALU.add, [ps(d, 0), "c7"], ["TT%d" % d])
            mm(PB[b][:, 0:8], [(T.TT[0:8, o:o + 128], ID[0:8, 0:8])], ["TT%d" % d, "ID"], [ps(b, 0)], n=64)
        t1(off, PB[b][:, 0:8], col(2), ALU.add, [ps(b, 0), "c2"], ["BOFF%d" % d], n=8)
        if second or not LEAN:
            act(sl(T.AY, d), YY[d][:, :].indirect(off), ACT.Abs, ys, ["AY%d" % d], xext(d), tgc[d], -1.0, 65 + 128 * GAT)
        if PICK[second] == "s":
            act(sl(T.YB, d), YY[d][:, :].indirect(off), ACT.Copy, ys, ["YB%d" % d], n=65 + 128 * GAT)
        else:
            cp(sl(T.YB, d), YY[d][:, :].indirect(off), ys, ["YB%d" % d], n=50 + 128 * GAT)
        if LEAN and not second:
            act(sl(T.AY, d), sl(T.YB, d), ACT.Abs, ["YB%d" % d], ["AY%d" % d], xext(d), tgc[d], -1.0)
        if BEST[second] == "p":
            (far, fn) = slot(4 + d, 0)
            mm(far[0:8, :], [(T.S2[:, o + 15:o + 128:16], T.IDF[:])], ["S2%d" % d, "IDF"], [fn], n=512)
            act(T.FAR[0:8, o:o + 128], far[0:8, :], ACT.Copy, [fn], ["MB%d" % d])
            bound()
        elif BEST[second] == "s":
            act(sl(T.MB, d), MM[d][:, :].indirect(off), ACT.Copy, ms, ["MB%d" % d], n=65 + 128 * GAT)
        else:
            cp(sl(T.MB, d), MM[d][:, :].indirect(off), ms, ["MB%d" % d], n=50 + 128 * GAT)
        mm(cm, [(T.BB[:], sl(T.AY, d))], ["BB", "AY%d" % d], [cn], start=False)
        mm(df, [(neg, x), (neg, mz), (one, sl(T.YB, d))], r + ["YB%d" % d], [dfn], fext(d, t))
        if BEST[second] == "p":
            mm(kd, [(one, sl(T.YB, d))][sign ^ 1:] + [(T.REP[0:8, :], T.FAR[0:8, o:o + 128])],
               ["IDH", "REP", "MB%d" % d] + ["YB%d" % d] * sign, [kn], n=512 + 128 * sign, start=False)
        else:
            mm(kd, [(one, sl(T.YB, d))][sign ^ 1:] + [(T.BN512[:], sl(T.YB, d)), (T.B1024[:], sl(T.MB, d))],
               ["IDH", "BN512", "B1024", "YB%d" % d, "MB%d" % d], [kn], start=False)
        for c, h, n in cut("kK"[second ^ 1] in CUT):
            ok, my = sl(T.OKY, d)[:, c], sl(T.MY, d)[:, c]
            if sign:
                act(ok, cm[:, c], ACT.Sign, [cn], ["OKY%d" % d + h], bias=0.5, scale=-1.0, n=n)
            else:
                t1(ok, cm[:, c], 0.0, ALU.is_le, [cn], ["OKY%d" % d + h], n=n)
            tt(my, df[:, c], ok, ALU.mult, [dfn, "OKY%d" % d + h], ["MY%d" % d + h], n=n)
            tt(key[:, c], kd[:, c], my, ALU.add, [kn, "MY%d" % d + h], ["key%d_%d" % (d, t) + h], n=n)
        for a in ops[mark:]:
            a["pen"] = -BOOST[second]
        land = {(0, 1): (1, "ka1"), (0, -1): (2, "ka2"), (1, -1): (0, "kb0"), (1, -2): (2, "kb2")}
        items = [(k, key, sl(KK[d], 3 * t + land[d, k][0]), "%s_%d" % (land[d, k][1], t)) for k in key_offs(d, t)]
        if both_off(rank, d, t):
            es = plan(rank, [items[0][0]])[0]
            tr = RemoteDMATransfer(dst_ids=[DstId(rid=topo.addr(peer(it[0]))[0], pnc=topo.addr(peer(it[0]))[1]) for it in items],
                                   dma_engine_mask=sum(1 << e for e in es), remote_sem=T.sem["ke_%d" % t], srcs=[key],
                                   dsts=[it[2] for it in items])
            sent[0] += len(es)
            rows = 256 / len(es) * (ROW + 512 / RATE)
            op("g", lambda q: q.remote_dma_fused([tr], local_sem=T.sem.sent), ["key%d_%d" % (d, t)], (), (), CALL, False,
               [("ke_%d" % t, HOP + rows, rows)])
        else:
            send(items, 512, ["key%d_%d" % (d, t)])

    def before(t):
        return T.RN[:, 144 * t - 17:144 * t - 16]

    def append(t):
        (pos, pn), (a, an) = slot(7, 1), slot(6, 1)
        scan(T.RN[:, 144 * t:144 * t + 136], T.EQ[:, 256:392], T.CAP[:, 0:136], before(t), ALU.add, ALU.min,
             ["CAP", "EQ2", "EQX", "RN%d" % (t - 1)], ["RN%d" % t], 136)
        scan(pos, T.ONE[:], sl(T.EQ, 2), before(t), ALU.mult, ALU.add, ["ONE", "EQ2", "RN%d" % (t - 1)], [pn])
        tt(T.VV[:], sl(T.EQ, 2), pos, ALU.mult, ["EQ2", pn], ["VV"])
        ts(T.DO[:], T.VV[:], RING - 255.0, float(OVER), ALU.is_ge, ALU.mult, ["VV"], ["DO"], n=64)
        ops[-1]["pen"] = ops[-2]["pen"] = ops[-3]["pen"] = -HASTE
        mm(a, [(T.IDBIG[:], T.MA[:]), (T.BK[:], sl(T.EQ, 2)), (T.BB[:], T.VV[:])], ["IDBIG", "MA", "BK", "EQ2", "BB", "VV"], [an],
           stop=False)
        mm(a, [(T.BB[:], T.DO[:])], ["BB", "DO"], [an], start=False)
        scan(T.SC2[:], T.RS[:], a, 0.0, ALU.mult, ALU.max, ["RS", an], ["SC2"])
        t1(T.SOFF[:], T.SC2[:, 15:128:16], 255.0 - 16384.0, ALU.add, ["SC2"], ["SOFF"], n=8)
        cp(T.H1[:, :].indirect(T.SOFF[:, 0:8]), xs(2), ["SOFF", "X2"], ["H"], (), 50 + 128 * SCA)

    first_hashes()
    send([(1, T.DVS[:, 7:392], T.DVL[:, 7:392], "dv0")], 770, ["DVS"], [("ldv", 16)])
    for t in range(STEPS):
        for d in (E, Z):
            mark = len(ops)
            if t:
                finish(d, t - 1)
            ring(d, t)
            if t:
                hashes(d, t)
            xrep(d)
            for a in ops[mark:]:
                a["pen"] = -AHEAD[role] * (d == Z)
            if d == 0:
                fallback(d, t)
            elif t == 0:
                tmat(d)
        if t:
            finish(2, t - 1)
            ring(2)
            append(t)
        for d in (E, Z):
            mark = len(ops)
            places(d, t)
            for a in ops[mark:]:
                a["pen"] = -AHEAD[role] * (d == Z)
        tell(0, t)
        for d in (E, Z):
            job(d, t)
        if t == 0:
            for o in later:
                o["r"].append(GATE % Z)
            ops.extend(later)

    finish(2, STEPS - 1)
    ring(2)
    dma("y", T.yx[:], xs(2), "out0", r=["X2"], tail=2.5)
    scan(T.YN[:, 0:138], T.EQ[:, 256:394], T.CAP[:, 0:138], before(STEPS), ALU.add, ALU.min,
         ["CAP", "EQ2", "EQX", "RN%d" % (STEPS - 1)], ["YN"], 138)
    dma("y", T.yn[:], T.YN[:, 137:138], "out1", r=["YN"], tail=2.3)
    return ops, sent[0]


def rank_program(g, core, T, topo):
    rank = T.rank_of(core)
    if rank is None:
        return
    role = role_of(T, topo, rank)
    mine, sent = program(T, topo, rank)
    other = [r for r in range(NR) if role_of(T, topo, r) != role][0]
    progs = [mine, program(T, topo, other)[0]]
    emit(g, T, schedule(progs if role == 0 else progs[::-1])[role])
    g.sync.wait_ge(T.sem.out0, 16)
    g.sync.wait_ge(T.sem.out1, 16)
    g.wait_ge(T.sem.sent, sent)
